import numpy as np
import ml_dtypes


def mxq(x, axis, fmt="e4m3"):
    dtype, down = {"e4m3": (ml_dtypes.float8_e4m3fn, 7), "e5m2": (ml_dtypes.float8_e5m2, 14)}[fmt]
    v = np.moveaxis(np.asarray(x, np.float32).astype(ml_dtypes.bfloat16).astype(np.float64), axis, -1)
    blocks = v.reshape(v.shape[:-1] + (-1, 32))
    amax = np.abs(blocks).max(-1, keepdims=True)
    byte = np.maximum(np.where(amax > 0, np.frexp(amax)[1] - 1 + 127, 0) - down, 1)
    scale = np.exp2(byte - 127.0)
    codes = (blocks / scale).astype(np.float32).astype(dtype).astype(np.float64)
    return np.moveaxis((codes * scale).reshape(v.shape), -1, axis)


WIDE = False


def mx_kscale(k):
    if not WIDE:
        return np.ones(k)
    levels = np.array([10, -10, 5, -5, 0])
    if k % 512:
        return np.exp2(np.random.permutation(np.resize(levels, k // 32))).repeat(32)
    a = np.empty((k // 512, 16))
    for p in range(k // 512):
        a[p, :8] = np.random.permutation(np.resize(levels, 8))
        for g in range(8):
            far = levels[np.abs(levels - a[p, g]) >= 10]
            a[p, g + 8] = far[np.random.randint(len(far))]
    return np.exp2(a.ravel()).repeat(32)


def f64(x):
    return np.asarray(x).astype(np.float64)


def striped(idx):
    return np.tile(idx.reshape(-1, 16).T, (8, 1)).astype(np.uint16)


def unstriped(offs):
    return offs[:16].T.reshape(-1).astype(np.int64)


E2M1 = np.array([0.0, 0.5, 1.0, 1.5, 2.0, 3.0, 4.0, 6.0, -0.0, -0.5, -1.0, -1.5, -2.0, -3.0, -4.0, -6.0])


def pack_weight(w, fmt):
    k, n = w.shape
    w = f64(np.asarray(w, np.float32).astype(ml_dtypes.bfloat16)).reshape(k // 32, 32, n)
    amax = np.abs(w).max(1)
    if fmt == "e4m3":
        byte = np.frexp(amax)[1] - 1 + 127 - 7
    else:
        mant, ex = np.frexp(amax / 6.0)
        byte = np.where(mant > 0.5, ex, ex - 1) + 127
    byte = np.clip(np.where(amax > 0, byte, 1), 1, 254)
    scaled = (w * np.exp2(127.0 - byte)[:, None, :]).reshape(k, n).astype(np.float32)
    by_word = np.ascontiguousarray(scaled.reshape(k // 512, 128, 4, n).transpose(0, 1, 3, 2))
    if fmt == "e4m3":
        words = by_word.astype(ml_dtypes.float8_e4m3fn).view(np.uint8)
    else:
        c = by_word.astype(ml_dtypes.float4_e2m1fn).view(np.uint8) & 0xF
        words = (c[..., 0::2] | (c[..., 1::2] << 4)).reshape(k // 512, 128, 2 * n)
    return np.ascontiguousarray(words), np.ascontiguousarray(byte.astype(np.uint8).reshape(k // 512, 16, n))


def unpack_weight(words, scales, fmt):
    g, _, n = scales.shape
    words = np.ascontiguousarray(words).reshape(g, 128, n, -1)
    if fmt == "e4m3":
        vals = words.view(ml_dtypes.float8_e4m3fn).astype(np.float64)
    else:
        nib = np.empty((g, 128, n, 4), np.uint8)
        nib[..., 0::2] = words & 0xF
        nib[..., 1::2] = words >> 4
        vals = E2M1[nib]
    vals = vals * np.repeat(np.exp2(scales.astype(np.float64) - 127.0), 8, axis=1)[..., None]
    return vals.transpose(0, 1, 3, 2).reshape(g * 512, n)


def gelu(v):
    return 0.5 * v * (1.0 + np.tanh(np.sqrt(2.0 / np.pi) * (v + 0.044715 * v**3)))


K, T, S, T2, S2, N = 1024, 2048, 1024, 4096, 1024, 512

def setup_inputs():
    n = np.random.standard_normal
    s = mx_kscale(K)[:, None]
    u = mx_kscale(S)[:, None]
    tab_words, tab_scales = pack_weight(n((K, T)) * s, "e4m3")
    tab2_words, tab2_scales = pack_weight(n((K, T2)) / s / np.sqrt(K), "e4m3")
    w4_words, w4_scales = pack_weight(n((S, N)) / u / np.sqrt(S), "e2m1")
    return {
        "tab_words": tab_words, "tab_scales": tab_scales,
        "tab2_words": tab2_words, "tab2_scales": tab2_scales,
        "offs": striped(np.random.permutation(T)[:S]),
        "offs2": striped(np.random.permutation(T2)[:S2]),
        "ga": (np.exp(0.3 * n(S)) * u[:, 0]).astype(np.float32),
        "gb": (np.exp(0.3 * n(S)) * u[:, 0]).astype(np.float32),
        "w1": (n((S, N)) / u / np.sqrt(S)).astype(np.float32),
        "w4_words": w4_words, "w4_scales": w4_scales,
        "bias": (0.5 * n(N)).astype(np.float32),
    }

def reference(tab_words, tab_scales, tab2_words, tab2_scales, offs, offs2, ga, gb, w1, w4_words, w4_scales, bias):
    v = unpack_weight(tab_words, tab_scales, "e4m3")[:, unstriped(offs)]
    v2 = unpack_weight(tab2_words, tab2_scales, "e4m3")[:, unstriped(offs2)]
    A = v.T @ v2
    h1 = mxq(A * f64(ga)[:, None], 0, "e4m3")
    h2 = mxq(np.tanh(A) * f64(gb)[:, None], 0, "e4m3")
    wq = mxq(f64(w1), 0, "e4m3")
    w4 = unpack_weight(w4_words, w4_scales, "e2m1")
    y = wq.T @ h1 + w4.T @ h2
    return y + f64(bias)[:, None]

@@ -1,0 +1,243 @@
+from contextlib import ExitStack
+
+import concourse.mybir as mybir
+
+K, T, S, T2, S2, N = 1024, 2048, 1024, 4096, 1024, 512
+FLOPS = 2 * K * S * S2 + 2 * 2 * S * N * S2
+
+F32 = mybir.dt.float32
+BF16 = mybir.dt.bfloat16
+I32 = mybir.dt.int32
+U32 = mybir.dt.uint32
+U16 = mybir.dt.uint16
+U8 = mybir.dt.uint8
+FP8X4 = mybir.dt.float8_e4m3fn_x4
+FP4X4 = mybir.dt.float4_e2m1fn_x4
+ACT = mybir.ActivationFunctionType
+MULT = mybir.AluOpType.mult
+ADD = mybir.AluOpType.add
+
+P = 128
+PACK = 4
+PASS = P * PACK
+KP = K // PASS
+SP = S // PASS
+JT = 128
+NJ = S2 // JT
+NT = N // P
+HALF = 512
+EARLY = 3
+
+
+def tile_list_creative_user_readout_kernel(
+    tc, tab_words, tab_scales, tab2_words, tab2_scales, offs, offs2, ga, gb, w1, w4_words, w4_scales, bias, out
+):
+    nc = tc.nc
+    with ExitStack() as ctx:
+        keep = ctx.enter_context(tc.tile_pool(name="keep", bufs=1))
+        ring = ctx.enter_context(tc.tile_pool(name="ring", bufs=3))
+        psum = ctx.enter_context(tc.psum_pool(name="psum", bufs=1))
+
+        idx = keep.tile([P, S // 16], U16, name="idx")
+        idx2 = keep.tile([P, S2 // 16], U16, name="idx2")
+        tw = [keep.tile([P, T], I32, name="tw%d" % a, align_bytes=64) for a in range(KP)]
+        t2w = [keep.tile([P, T2], I32, name="t2w%d" % a, align_bytes=64) for a in range(KP)]
+        tsc = keep.tile([P, T // 4], I32, name="tsc", align_bytes=64)
+        t2sc = keep.tile([P, T2 // 4], I32, name="t2sc", align_bytes=64)
+        w4s = keep.tile([P, SP, N // 4], I32, name="w4s", align_bytes=64)
+        w4w = keep.tile([P, SP, N // 2], I32, name="w4w", align_bytes=64)
+        ga_t = keep.tile([P, SP, PACK], F32, name="ga_t")
+        gb_t = keep.tile([P, SP, PACK], F32, name="gb_t")
+        bias_t = keep.tile([P, NT], F32, name="bias_t")
+        w1_raw = [keep.tile([P, PACK, N], F32, name="w1_raw%d" % b, align_bytes=64) for b in range(SP)]
+
+        nc.vector.memset(tsc[:], 0)
+        nc.vector.memset(t2sc[:], 0)
+        nc.vector.memset(w4s[:], 0)
+
+        def load_words(tile, words):
+            nc.sync.dma_start(out=tile[:], in_=words.rearrange("p n t -> p (n t)").bitcast(I32))
+
+        def load_planes(tile, scales):
+            for q in range(4):
+                nc.sync.dma_start(out=tile[32 * q : 32 * q + 4 * KP, :], in_=scales[:, 4 * q : 4 * q + 4, :].bitcast(I32))
+
+        nc.sync.dma_start(idx[:], offs)
+        load_words(tw[0], tab_words[0])
+        load_planes(tsc, tab_scales)
+        load_words(tw[1], tab_words[1])
+        nc.sync.dma_start(idx2[:], offs2)
+        load_planes(t2sc, tab2_scales)
+        load_words(t2w[0], tab2_words[0])
+        load_words(t2w[1], tab2_words[1])
+        nc.sync.dma_start(out=ga_t[:], in_=ga.rearrange("(b p t) -> p b t", p=P, t=PACK))
+        nc.sync.dma_start(out=gb_t[:], in_=gb.rearrange("(b p t) -> p b t", p=P, t=PACK))
+        nc.sync.dma_start(out=w1_raw[0][:], in_=w1[0:PASS, :].rearrange("(p t) n -> p t n", t=PACK))
+        nc.sync.dma_start(out=w4w[:], in_=w4_words.rearrange("b p c -> p b c").bitcast(I32))
+        for q in range(4):
+            nc.sync.dma_start(
+                out=w4s[32 * q : 32 * q + 4, :, :],
+                in_=w4_scales[:, 4 * q : 4 * q + 4, :].rearrange("b r c -> r b c").bitcast(I32),
+            )
+        nc.sync.dma_start(out=w1_raw[1][:], in_=w1[PASS : 2 * PASS, :].rearrange("(p t) n -> p t n", t=PACK))
+        with nc.allow_non_contiguous_dma(reason="one bias value for each partition and output tile"):
+            nc.sync.dma_start(out=bias_t[:], in_=bias.rearrange("(c p) -> p c", p=P))
+
+        cols = HALF // 16
+        vw = [[keep.tile([P, PASS], U32, name="vw%d_%d" % (a, b), align_bytes=64) for b in range(SP)] for a in range(KP)]
+        uw = [[keep.tile([P, HALF], U32, name="uw%d_%d" % (a, h), align_bytes=64) for h in range(2)] for a in range(KP)]
+        vs_listed = keep.tile([P, S], U8, name="vs_listed", align_bytes=64)
+        vs = keep.tile([P, S], U8, name="vs", align_bytes=64)
+        us = keep.tile([P, S2], U8, name="us", align_bytes=64)
+
+        def gather_v(a):
+            for b in range(SP):
+                nc.vector.tensor_copy(
+                    vw[a][b][:].rearrange("p (t m) -> p m t", t=PACK),
+                    tw[a][:].bitcast(U32).indirect(idx[:, b * cols : (b + 1) * cols]),
+                )
+
+        def gather_u(a):
+            for h in range(2):
+                nc.vector.tensor_copy(uw[a][h][:], t2w[a][:].bitcast(U32).indirect(idx2[:, h * cols : (h + 1) * cols]))
+
+        gather_v(0)
+        nc.vector.tensor_copy(vs_listed[:], tsc[:].bitcast(U8).indirect(idx[:]))
+        gather_v(1)
+        nc.vector.tensor_copy(
+            vs[:].rearrange("p (b t m) -> p b t m", b=SP, t=PACK),
+            vs_listed[:].rearrange("p (b m t) -> p b t m", b=SP, t=PACK),
+        )
+        nc.vector.tensor_copy(us[:], t2sc[:].bitcast(U8).indirect(idx2[:]))
+        gather_u(0)
+        gather_u(1)
+
+        w1_bf = [keep.tile([P, N, PACK], BF16, name="w1_bf%d" % b, align_bytes=64) for b in range(SP)]
+        w1_codes = [keep.tile([P, N], U32, name="w1_codes%d" % b, align_bytes=64) for b in range(SP)]
+        w1_scales = [keep.tile([P, N], U8, name="w1_scales%d" % b, align_bytes=64) for b in range(SP)]
+
+        def round_w1(b, c):
+            nc.scalar.copy(
+                out=w1_bf[b][:, c * P : (c + 1) * P, :].rearrange("p (g i) t -> p g t i", i=4),
+                in_=w1_raw[b][:, :, c * P : (c + 1) * P].rearrange("p t (g i) -> p g t i", i=4),
+            )
+
+        def quantize_w1(b):
+            nc.vector.quantize_mx(
+                out=w1_codes[b][:].bitcast(FP8X4), scales=w1_scales[b][:], in_=w1_bf[b][:].rearrange("p n t -> p (n t)")
+            )
+
+        hq, th, h_codes, h_scales = {}, {}, {}, {}
+
+        def scores(j):
+            half, j0 = divmod(j * JT, HALF)
+            hq[j] = ring.tile([P, 2 * SP, JT, PACK], BF16, name="hq", align_bytes=64)
+            th[j] = ring.tile([P, SP, JT, PACK], F32, name="th", align_bytes=64)
+            h_codes[j] = keep.tile([P, 2 * SP * JT], U32, name="h_codes%d" % j, align_bytes=64)
+            h_scales[j] = keep.tile([P, 2 * SP * JT], U8, name="h_scales%d" % j, align_bytes=64)
+            for b in range(SP):
+                acc = psum.tile([P, PACK, JT], F32, name="acc", bufs=5)
+                for a in range(KP):
+                    for t in range(PACK):
+                        nc.tensor.matmul_mx(
+                            out=acc[:, t, :],
+                            lhsT=vw[a][b][:, t * P : (t + 1) * P].bitcast(FP8X4),
+                            lhsT_scale=vs[4 * a :, b * PASS + t * P : b * PASS + (t + 1) * P],
+                            rhs=uw[a][half][:, j0 : j0 + JT].bitcast(FP8X4),
+                            rhs_scale=us[4 * a :, j * JT : (j + 1) * JT],
+                            start=(a == 0 and t == 0),
+                            stop=(a == KP - 1 and t == PACK - 1),
+                        )
+                woven = acc[:].rearrange("p t n -> p n t")
+
+                def linear():
+                    nc.vector.tensor_tensor(
+                        hq[j][:, b, :, :], woven, ga_t[:, b : b + 1, :].to_broadcast([P, JT, PACK]), MULT
+                    )
+
+                def saturate():
+                    nc.scalar.activation(out=th[j][:, b, :, :], in_=woven, func=ACT.Tanh)
+
+                for step in (linear, saturate) if b == 0 else (saturate, linear):
+                    step()
+
+        def weigh(j, lo, hi):
+            nc.vector.tensor_tensor(
+                hq[j][:, SP + lo : SP + hi, :, :],
+                th[j][:, lo:hi, :, :],
+                gb_t[:, lo:hi, :].unsqueeze(2).to_broadcast([P, hi - lo, JT, PACK]),
+                MULT,
+            )
+
+        def quantize(j, lo, hi):
+            nc.vector.quantize_mx(
+                out=h_codes[j][:, lo * JT : hi * JT].bitcast(FP8X4),
+                scales=h_scales[j][:, lo * JT : hi * JT],
+                in_=hq[j][:, lo:hi, :, :].rearrange("p g n t -> p (g n t)"),
+            )
+
+        def passes(j, y, tiles, order):
+            for g in order:
+                b = g % SP
+                for c in tiles:
+                    if g < SP:
+                        w = w1_codes[b][:, c * P : (c + 1) * P].bitcast(FP8X4)
+                        ws = w1_scales[b][:, c * P : (c + 1) * P]
+                    else:
+                        w = w4w[:, b, :].bitcast(U8)[:, 2 * c * P : 2 * (c + 1) * P].bitcast(FP4X4)
+                        ws = w4s[:, b, :].bitcast(U8)[:, c * P : (c + 1) * P]
+                    nc.tensor.matmul_mx(
+                        out=y[:, c - tiles[0], :],
+                        lhsT=w,
+                        lhsT_scale=ws,
+                        rhs=h_codes[j][:, g * JT : (g + 1) * JT].bitcast(FP8X4),
+                        rhs_scale=h_scales[j][:, g * JT : (g + 1) * JT],
+                        start=(g == order[0] and c == tiles[0]),
+                        stop=(g == order[-1] and c == tiles[-1]),
+                    )
+
+        out_tiles = out.rearrange("(c p) j -> p c j", p=P)
+
+        def read_out(j):
+            y = psum.tile([P, NT, JT], F32, name="y", bufs=3)
+            res = ring.tile([P, NT, JT], F32, name="res")
+            passes(j, y, [0, 1, 2, 3], [2, 3, 0, 1] if j < EARLY else [0, 1, 2, 3])
+            for c in range(NT):
+                nc.scalar.activation(out=res[:, c, :], in_=y[:, c, :], func=ACT.Identity, bias=bias_t[:, c : c + 1])
+            nc.sync.dma_start(out=out_tiles[:, :, j * JT : (j + 1) * JT], in_=res[:])
+
+        def read_out_last(j):
+            ys = [psum.tile([P, 2, JT], F32, name="y", bufs=3) for u in range(2)]
+            for u in range(2):
+                passes(j, ys[u], [2 * u, 2 * u + 1], [0, 1, 2, 3])
+            res0 = ring.tile([P, 2, JT], F32, name="res")
+            for c in range(2):
+                nc.scalar.activation(out=res0[:, c, :], in_=ys[0][:, c, :], func=ACT.Identity, bias=bias_t[:, c : c + 1])
+            nc.sync.dma_start(out=out_tiles[:, 0:2, j * JT : (j + 1) * JT], in_=res0[:])
+            res1 = ring.tile([P, 2, JT], F32, name="res")
+            nc.vector.tensor_tensor(res1[:], ys[1][:], bias_t[:, 2:4].unsqueeze(2).to_broadcast([P, 2, JT]), ADD)
+            nc.sync.dma_start(out=out_tiles[:, 2:4, j * JT : (j + 1) * JT], in_=res1[:])
+
+        for s in range(NJ):
+            scores(s)
+            if s < 2 * SP:
+                round_w1(s // 2, 2 * (s % 2))
+                round_w1(s // 2, 2 * (s % 2) + 1)
+            if s >= 1:
+                weigh(s - 1, 0, SP)
+            quantize(s, 0, SP)
+            if s >= 1:
+                quantize(s - 1, SP, 2 * SP)
+            if s in (1, 3):
+                quantize_w1(s // 2)
+            if s == EARLY:
+                for j in range(EARLY):
+                    read_out(j)
+            if s > EARLY:
+                read_out(s - 1)
+        last = NJ - 1
+        for b in range(SP):
+            weigh(last, b, b + 1)
+        for b in range(SP):
+            quantize(last, SP + b, SP + b + 1)
+        read_out_last(last)

@@ -27,6 +27,7 @@ NJ = S2 // JT
 NT = N // P
 HALF = 512
 EARLY = 3
+U_ROW = 8
 
 
 def tile_list_creative_user_readout_kernel(
@@ -51,23 +52,25 @@ def tile_list_creative_user_readout_kernel(
         bias_t = keep.tile([P, NT], F32, name="bias_t")
         w1_raw = [keep.tile([P, PACK, N], F32, name="w1_raw%d" % b, align_bytes=64) for b in range(SP)]
 
-        nc.vector.memset(tsc[:], 0)
         nc.vector.memset(t2sc[:], 0)
+        nc.vector.memset(tsc[:], 0)
         nc.vector.memset(w4s[:], 0)
 
         def load_words(tile, words):
             nc.sync.dma_start(out=tile[:], in_=words.rearrange("p n t -> p (n t)").bitcast(I32))
 
-        def load_planes(tile, scales):
+        def load_planes(queue, tile, row0, scales):
             for q in range(4):
-                nc.sync.dma_start(out=tile[32 * q : 32 * q + 4 * KP, :], in_=scales[:, 4 * q : 4 * q + 4, :].bitcast(I32))
+                queue.dma_start(
+                    out=tile[32 * q + row0 : 32 * q + row0 + 4 * KP, :], in_=scales[:, 4 * q : 4 * q + 4, :].bitcast(I32)
+                )
 
         nc.sync.dma_start(idx[:], offs)
         load_words(tw[0], tab_words[0])
-        load_planes(tsc, tab_scales)
+        load_planes(nc.sync, tsc, 0, tab_scales)
         load_words(tw[1], tab_words[1])
         nc.sync.dma_start(idx2[:], offs2)
-        load_planes(t2sc, tab2_scales)
+        load_planes(nc.gpsimd, t2sc, U_ROW, tab2_scales)
         load_words(t2w[0], tab2_words[0])
         load_words(t2w[1], tab2_words[1])
         nc.sync.dma_start(out=ga_t[:], in_=ga.rearrange("(b p t) -> p b t", p=P, t=PACK))
@@ -144,7 +147,7 @@ def tile_list_creative_user_readout_kernel(
                             lhsT=vw[a][b][:, t * P : (t + 1) * P].bitcast(FP8X4),
                             lhsT_scale=vs[4 * a :, b * PASS + t * P : b * PASS + (t + 1) * P],
                             rhs=uw[a][half][:, j0 : j0 + JT].bitcast(FP8X4),
-                            rhs_scale=us[4 * a :, j * JT : (j + 1) * JT],
+                            rhs_scale=us[U_ROW + 4 * a :, j * JT : (j + 1) * JT],
                             start=(a == 0 and t == 0),
                             stop=(a == KP - 1 and t == PACK - 1),
                         )

@@ -1,6 +1,7 @@
 from contextlib import ExitStack
 
 import concourse.mybir as mybir
+from concourse.masks import make_identity
 
 K, T, S, T2, S2, N = 1024, 2048, 1024, 4096, 1024, 512
 FLOPS = 2 * K * S * S2 + 2 * 2 * S * N * S2
@@ -52,9 +53,11 @@ def tile_list_creative_user_readout_kernel(
         bias_t = keep.tile([P, NT], F32, name="bias_t")
         w1_raw = [keep.tile([P, PACK, N], F32, name="w1_raw%d" % b, align_bytes=64) for b in range(SP)]
 
-        nc.vector.memset(t2sc[:], 0)
         nc.vector.memset(tsc[:], 0)
+        nc.vector.memset(t2sc[:], 0)
         nc.vector.memset(w4s[:], 0)
+        gb_rows = keep.tile([P, PASS], F32, name="gb_rows")
+        nc.vector.memset(gb_rows[:], 0.0)
 
         def load_words(tile, words):
             nc.sync.dma_start(out=tile[:], in_=words.rearrange("p n t -> p (n t)").bitcast(I32))
@@ -70,9 +73,10 @@ def tile_list_creative_user_readout_kernel(
         load_planes(nc.sync, tsc, 0, tab_scales)
         load_words(tw[1], tab_words[1])
         nc.sync.dma_start(idx2[:], offs2)
-        load_planes(nc.gpsimd, t2sc, U_ROW, tab2_scales)
+        load_planes(nc.sync, t2sc, U_ROW, tab2_scales)
         load_words(t2w[0], tab2_words[0])
         load_words(t2w[1], tab2_words[1])
+        nc.sync.dma_start(out=gb_rows[0:SP, :], in_=gb.rearrange("(b i) -> b i", b=SP))
         nc.sync.dma_start(out=ga_t[:], in_=ga.rearrange("(b p t) -> p b t", p=P, t=PACK))
         nc.sync.dma_start(out=gb_t[:], in_=gb.rearrange("(b p t) -> p b t", p=P, t=PACK))
         nc.sync.dma_start(out=w1_raw[0][:], in_=w1[0:PASS, :].rearrange("(p t) n -> p t n", t=PACK))
@@ -85,6 +89,12 @@ def tile_list_creative_user_readout_kernel(
         nc.sync.dma_start(out=w1_raw[1][:], in_=w1[PASS : 2 * PASS, :].rearrange("(p t) n -> p t n", t=PACK))
         with nc.allow_non_contiguous_dma(reason="one bias value for each partition and output tile"):
             nc.sync.dma_start(out=bias_t[:], in_=bias.rearrange("(c p) -> p c", p=P))
+
+        ident = keep.tile([P, P], F32, name="ident")
+        make_identity(nc, ident[:])
+        gb_bank = psum.tile([P, PACK, P], F32, name="gb_bank")
+        for t in range(PACK):
+            nc.tensor.transpose(gb_bank[:, t, :], gb_rows[:, t::PACK], ident[:])
 
         cols = HALF // 16
         vw = [[keep.tile([P, PASS], U32, name="vw%d_%d" % (a, b), align_bytes=64) for b in range(SP)] for a in range(KP)]
@@ -130,16 +140,16 @@ def tile_list_creative_user_readout_kernel(
                 out=w1_codes[b][:].bitcast(FP8X4), scales=w1_scales[b][:], in_=w1_bf[b][:].rearrange("p n t -> p (n t)")
             )
 
-        hq, th, h_codes, h_scales = {}, {}, {}, {}
+        hq, hq2, th, h_codes, h_scales = {}, {}, {}, {}, {}
 
         def scores(j):
             half, j0 = divmod(j * JT, HALF)
-            hq[j] = ring.tile([P, 2 * SP, JT, PACK], BF16, name="hq", align_bytes=64)
+            hq[j] = ring.tile([P, SP, JT, PACK], BF16, name="hq", align_bytes=64)
             th[j] = ring.tile([P, SP, JT, PACK], F32, name="th", align_bytes=64)
             h_codes[j] = keep.tile([P, 2 * SP * JT], U32, name="h_codes%d" % j, align_bytes=64)
             h_scales[j] = keep.tile([P, 2 * SP * JT], U8, name="h_scales%d" % j, align_bytes=64)
             for b in range(SP):
-                acc = psum.tile([P, PACK, JT], F32, name="acc", bufs=5)
+                acc = psum.tile([P, PACK, JT], F32, name="acc", bufs=4)
                 for a in range(KP):
                     for t in range(PACK):
                         nc.tensor.matmul_mx(
@@ -164,19 +174,21 @@ def tile_list_creative_user_readout_kernel(
                 for step in (linear, saturate) if b == 0 else (saturate, linear):
                     step()
 
-        def weigh(j, lo, hi):
+        def weigh_vector(j, b):
             nc.vector.tensor_tensor(
-                hq[j][:, SP + lo : SP + hi, :, :],
-                th[j][:, lo:hi, :, :],
-                gb_t[:, lo:hi, :].unsqueeze(2).to_broadcast([P, hi - lo, JT, PACK]),
-                MULT,
+                hq2[j][:, b, :, :], th[j][:, b, :, :], gb_bank[:, :, b].unsqueeze(1).to_broadcast([P, JT, PACK]), MULT
             )
 
-        def quantize(j, lo, hi):
+        def weigh_gpsimd(j, b):
+            nc.gpsimd.tensor_tensor(
+                hq2[j][:, b, :, :], th[j][:, b, :, :], gb_t[:, b : b + 1, :].to_broadcast([P, JT, PACK]), MULT
+            )
+
+        def quantize(j, src, g0, lo, hi):
             nc.vector.quantize_mx(
-                out=h_codes[j][:, lo * JT : hi * JT].bitcast(FP8X4),
-                scales=h_scales[j][:, lo * JT : hi * JT],
-                in_=hq[j][:, lo:hi, :, :].rearrange("p g n t -> p (g n t)"),
+                out=h_codes[j][:, (g0 + lo) * JT : (g0 + hi) * JT].bitcast(FP8X4),
+                scales=h_scales[j][:, (g0 + lo) * JT : (g0 + hi) * JT],
+                in_=src[j][:, lo:hi, :, :].rearrange("p g n t -> p (g n t)"),
             )
 
         def passes(j, y, tiles, order):
@@ -212,7 +224,7 @@ def tile_list_creative_user_readout_kernel(
         def read_out_last(j):
             ys = [psum.tile([P, 2, JT], F32, name="y", bufs=3) for u in range(2)]
             for u in range(2):
-                passes(j, ys[u], [2 * u, 2 * u + 1], [0, 1, 2, 3])
+                passes(j, ys[u], [2 * u, 2 * u + 1], [0, 1, 3, 2])
             res0 = ring.tile([P, 2, JT], F32, name="res")
             for c in range(2):
                 nc.scalar.activation(out=res0[:, c, :], in_=ys[0][:, c, :], func=ACT.Identity, bias=bias_t[:, c : c + 1])
@@ -227,10 +239,12 @@ def tile_list_creative_user_readout_kernel(
                 round_w1(s // 2, 2 * (s % 2))
                 round_w1(s // 2, 2 * (s % 2) + 1)
             if s >= 1:
-                weigh(s - 1, 0, SP)
-            quantize(s, 0, SP)
+                hq2[s - 1] = ring.tile([P, SP, JT, PACK], BF16, name="hq2", bufs=1, align_bytes=64)
+                weigh_gpsimd(s - 1, 1)
+                weigh_vector(s - 1, 0)
+            quantize(s, hq, 0, 0, SP)
             if s >= 1:
-                quantize(s - 1, SP, 2 * SP)
+                quantize(s - 1, hq2, SP, 0, SP)
             if s in (1, 3):
                 quantize_w1(s // 2)
             if s == EARLY:
@@ -239,8 +253,9 @@ def tile_list_creative_user_readout_kernel(
             if s > EARLY:
                 read_out(s - 1)
         last = NJ - 1
-        for b in range(SP):
-            weigh(last, b, b + 1)
-        for b in range(SP):
-            quantize(last, SP + b, SP + b + 1)
+        hq2[last] = ring.tile([P, SP, JT, PACK], BF16, name="hq2_last", bufs=1, align_bytes=64)
+        for b in (1, 0):
+            weigh_vector(last, b)
+        for b in (1, 0):
+            quantize(last, hq2, SP, b, b + 1)
         read_out_last(last)

@@ -28,7 +28,7 @@ NJ = S2 // JT
 NT = N // P
 HALF = 512
 EARLY = 3
-U_ROW = 8
+G_COLS = 40
 
 
 def tile_list_creative_user_readout_kernel(
@@ -62,21 +62,24 @@ def tile_list_creative_user_readout_kernel(
         def load_words(tile, words):
             nc.sync.dma_start(out=tile[:], in_=words.rearrange("p n t -> p (n t)").bitcast(I32))
 
-        def load_planes(queue, tile, row0, scales):
-            for q in range(4):
-                queue.dma_start(
-                    out=tile[32 * q + row0 : 32 * q + row0 + 4 * KP, :], in_=scales[:, 4 * q : 4 * q + 4, :].bitcast(I32)
-                )
+        def load_planes(tile, scales, q):
+            nc.sync.dma_start(out=tile[32 * q : 32 * q + 4 * KP, :], in_=scales[:, 4 * q : 4 * q + 4, :].bitcast(I32))
 
         nc.sync.dma_start(idx[:], offs)
         load_words(tw[0], tab_words[0])
-        load_planes(nc.sync, tsc, 0, tab_scales)
+        for q in (2, 3):
+            load_planes(tsc, tab_scales, q)
+        for q in (2, 3):
+            load_planes(t2sc, tab2_scales, q)
+        for q in (0, 1):
+            load_planes(tsc, tab_scales, q)
+        load_planes(t2sc, tab2_scales, 0)
         load_words(tw[1], tab_words[1])
+        load_planes(t2sc, tab2_scales, 1)
         nc.sync.dma_start(idx2[:], offs2)
-        load_planes(nc.sync, t2sc, U_ROW, tab2_scales)
+        nc.sync.dma_start(out=gb_rows[0:SP, :], in_=gb.rearrange("(b i) -> b i", b=SP))
         load_words(t2w[0], tab2_words[0])
         load_words(t2w[1], tab2_words[1])
-        nc.sync.dma_start(out=gb_rows[0:SP, :], in_=gb.rearrange("(b i) -> b i", b=SP))
         nc.sync.dma_start(out=ga_t[:], in_=ga.rearrange("(b p t) -> p b t", p=P, t=PACK))
         nc.sync.dma_start(out=gb_t[:], in_=gb.rearrange("(b p t) -> p b t", p=P, t=PACK))
         nc.sync.dma_start(out=w1_raw[0][:], in_=w1[0:PASS, :].rearrange("(p t) n -> p t n", t=PACK))
@@ -131,8 +134,8 @@ def tile_list_creative_user_readout_kernel(
 
         def round_w1(b, c):
             nc.scalar.copy(
-                out=w1_bf[b][:, c * P : (c + 1) * P, :].rearrange("p (g i) t -> p g t i", i=4),
-                in_=w1_raw[b][:, :, c * P : (c + 1) * P].rearrange("p t (g i) -> p g t i", i=4),
+                out=w1_bf[b][:, c * P : (c + 1) * P, :].rearrange("p (g i) t -> p g t i", i=2),
+                in_=w1_raw[b][:, :, c * P : (c + 1) * P].rearrange("p t (g i) -> p g t i", i=2),
             )
 
         def quantize_w1(b):
@@ -157,7 +160,7 @@ def tile_list_creative_user_readout_kernel(
                             lhsT=vw[a][b][:, t * P : (t + 1) * P].bitcast(FP8X4),
                             lhsT_scale=vs[4 * a :, b * PASS + t * P : b * PASS + (t + 1) * P],
                             rhs=uw[a][half][:, j0 : j0 + JT].bitcast(FP8X4),
-                            rhs_scale=us[U_ROW + 4 * a :, j * JT : (j + 1) * JT],
+                            rhs_scale=us[4 * a :, j * JT : (j + 1) * JT],
                             start=(a == 0 and t == 0),
                             stop=(a == KP - 1 and t == PACK - 1),
                         )
@@ -174,14 +177,22 @@ def tile_list_creative_user_readout_kernel(
                 for step in (linear, saturate) if b == 0 else (saturate, linear):
                     step()
 
-        def weigh_vector(j, b):
+        gb_psum = gb_bank[:, :, 0:SP].rearrange("p t b -> p b t")
+
+        def weigh_vector(j, b0, b1, n):
             nc.vector.tensor_tensor(
-                hq2[j][:, b, :, :], th[j][:, b, :, :], gb_bank[:, :, b].unsqueeze(1).to_broadcast([P, JT, PACK]), MULT
+                hq2[j][:, b0:b1, 0:n, :],
+                th[j][:, b0:b1, 0:n, :],
+                gb_psum[:, b0:b1, :].unsqueeze(2).to_broadcast([P, b1 - b0, n, PACK]),
+                MULT,
             )
 
-        def weigh_gpsimd(j, b):
+        def weigh_gpsimd(j, n):
             nc.gpsimd.tensor_tensor(
-                hq2[j][:, b, :, :], th[j][:, b, :, :], gb_t[:, b : b + 1, :].to_broadcast([P, JT, PACK]), MULT
+                hq2[j][:, :, n:JT, :],
+                th[j][:, :, n:JT, :],
+                gb_t[:].unsqueeze(2).to_broadcast([P, SP, JT - n, PACK]),
+                MULT,
             )
 
         def quantize(j, src, g0, lo, hi):
@@ -240,8 +251,8 @@ def tile_list_creative_user_readout_kernel(
                 round_w1(s // 2, 2 * (s % 2) + 1)
             if s >= 1:
                 hq2[s - 1] = ring.tile([P, SP, JT, PACK], BF16, name="hq2", bufs=1, align_bytes=64)
-                weigh_gpsimd(s - 1, 1)
-                weigh_vector(s - 1, 0)
+                weigh_gpsimd(s - 1, JT - G_COLS)
+                weigh_vector(s - 1, 0, SP, JT - G_COLS)
             quantize(s, hq, 0, 0, SP)
             if s >= 1:
                 quantize(s - 1, hq2, SP, 0, SP)
@@ -255,7 +266,7 @@ def tile_list_creative_user_readout_kernel(
         last = NJ - 1
         hq2[last] = ring.tile([P, SP, JT, PACK], BF16, name="hq2_last", bufs=1, align_bytes=64)
         for b in (1, 0):
-            weigh_vector(last, b)
+            weigh_vector(last, b, b + 1, JT)
         for b in (1, 0):
             quantize(last, hq2, SP, b, b + 1)
         read_out_last(last)

@@ -21,14 +21,17 @@ ADD = mybir.AluOpType.add
 P = 128
 PACK = 4
 PASS = P * PACK
-KP = K // PASS
-SP = S // PASS
-JT = 128
-NJ = S2 // JT
-NT = N // P
-HALF = 512
-EARLY = 3
-G_COLS = 40
+K_PASSES = K // PASS
+I_PASSES = S // PASS
+QUADRANT = 32
+USERS = 128
+USER_TILES = S2 // USERS
+N_TILES = N // P
+LIST_ROWS = 16
+USER_SLICE = 512
+GPSIMD_USERS = 40
+SCORE_BANKS = 5
+OUT_BANKS = 2
 
 
 def tile_list_creative_user_readout_kernel(
@@ -40,56 +43,56 @@ def tile_list_creative_user_readout_kernel(
         ring = ctx.enter_context(tc.tile_pool(name="ring", bufs=3))
         psum = ctx.enter_context(tc.psum_pool(name="psum", bufs=1))
 
-        idx = keep.tile([P, S // 16], U16, name="idx")
-        idx2 = keep.tile([P, S2 // 16], U16, name="idx2")
-        tw = [keep.tile([P, T], I32, name="tw%d" % a, align_bytes=64) for a in range(KP)]
-        t2w = [keep.tile([P, T2], I32, name="t2w%d" % a, align_bytes=64) for a in range(KP)]
-        tsc = keep.tile([P, T // 4], I32, name="tsc", align_bytes=64)
-        t2sc = keep.tile([P, T2 // 4], I32, name="t2sc", align_bytes=64)
-        w4s = keep.tile([P, SP, N // 4], I32, name="w4s", align_bytes=64)
-        w4w = keep.tile([P, SP, N // 2], I32, name="w4w", align_bytes=64)
-        ga_t = keep.tile([P, SP, PACK], F32, name="ga_t")
-        gb_t = keep.tile([P, SP, PACK], F32, name="gb_t")
-        bias_t = keep.tile([P, NT], F32, name="bias_t")
-        w1_raw = [keep.tile([P, PACK, N], F32, name="w1_raw%d" % b, align_bytes=64) for b in range(SP)]
+        idx = keep.tile([P, S // LIST_ROWS], U16, name="idx")
+        idx2 = keep.tile([P, S2 // LIST_ROWS], U16, name="idx2")
+        v_words = [keep.tile([P, T], I32, name="v_words%d" % a, align_bytes=64) for a in range(K_PASSES)]
+        v2_words = [keep.tile([P, T2], I32, name="v2_words%d" % a, align_bytes=64) for a in range(K_PASSES)]
+        v_planes = keep.tile([P, T // 4], I32, name="v_planes", align_bytes=64)
+        v2_planes = keep.tile([P, T2 // 4], I32, name="v2_planes", align_bytes=64)
+        w4_planes = keep.tile([P, I_PASSES, N // 4], I32, name="w4_planes", align_bytes=64)
+        w4_codes = keep.tile([P, I_PASSES, N // 2], I32, name="w4_codes", align_bytes=64)
+        ga_t = keep.tile([P, I_PASSES, PACK], F32, name="ga_t")
+        gb_t = keep.tile([P, I_PASSES, PACK], F32, name="gb_t")
+        bias_t = keep.tile([P, N_TILES], F32, name="bias_t")
+        w1_raw = [keep.tile([P, PACK, N], F32, name="w1_raw%d" % b, align_bytes=64) for b in range(I_PASSES)]
 
-        nc.vector.memset(tsc[:], 0)
-        nc.vector.memset(t2sc[:], 0)
-        nc.vector.memset(w4s[:], 0)
+        nc.vector.memset(v_planes[:], 0)
+        nc.vector.memset(v2_planes[:], 0)
+        nc.vector.memset(w4_planes[:], 0)
         gb_rows = keep.tile([P, PASS], F32, name="gb_rows")
         nc.vector.memset(gb_rows[:], 0.0)
 
         def load_words(tile, words):
             nc.sync.dma_start(out=tile[:], in_=words.rearrange("p n t -> p (n t)").bitcast(I32))
 
-        def load_planes(tile, scales, q):
-            nc.sync.dma_start(out=tile[32 * q : 32 * q + 4 * KP, :], in_=scales[:, 4 * q : 4 * q + 4, :].bitcast(I32))
+        def load_planes(tile, scales, quadrants):
+            for q in quadrants:
+                nc.sync.dma_start(
+                    out=tile[QUADRANT * q : QUADRANT * q + 4 * K_PASSES, :],
+                    in_=scales[:, 4 * q : 4 * q + 4, :].bitcast(I32),
+                )
 
+        load_words(v_words[0], tab_words[0])
         nc.sync.dma_start(idx[:], offs)
-        load_words(tw[0], tab_words[0])
-        for q in (2, 3):
-            load_planes(tsc, tab_scales, q)
-        for q in (2, 3):
-            load_planes(t2sc, tab2_scales, q)
-        for q in (0, 1):
-            load_planes(tsc, tab_scales, q)
-        load_planes(t2sc, tab2_scales, 0)
-        load_words(tw[1], tab_words[1])
-        load_planes(t2sc, tab2_scales, 1)
+        load_planes(v_planes, tab_scales, (2, 3))
+        load_planes(v2_planes, tab2_scales, (2, 3))
+        load_planes(v_planes, tab_scales, (0, 1))
+        load_words(v_words[1], tab_words[1])
+        load_planes(v2_planes, tab2_scales, (0, 1))
         nc.sync.dma_start(idx2[:], offs2)
-        nc.sync.dma_start(out=gb_rows[0:SP, :], in_=gb.rearrange("(b i) -> b i", b=SP))
-        load_words(t2w[0], tab2_words[0])
-        load_words(t2w[1], tab2_words[1])
+        nc.sync.dma_start(out=gb_rows[0:I_PASSES, :], in_=gb.rearrange("(b i) -> b i", b=I_PASSES))
+        load_words(v2_words[0], tab2_words[0])
+        load_words(v2_words[1], tab2_words[1])
         nc.sync.dma_start(out=ga_t[:], in_=ga.rearrange("(b p t) -> p b t", p=P, t=PACK))
         nc.sync.dma_start(out=gb_t[:], in_=gb.rearrange("(b p t) -> p b t", p=P, t=PACK))
-        nc.sync.dma_start(out=w1_raw[0][:], in_=w1[0:PASS, :].rearrange("(p t) n -> p t n", t=PACK))
-        nc.sync.dma_start(out=w4w[:], in_=w4_words.rearrange("b p c -> p b c").bitcast(I32))
-        for q in range(4):
+        for b in range(I_PASSES):
+            nc.sync.dma_start(out=w1_raw[b][:], in_=w1[b * PASS : (b + 1) * PASS, :].rearrange("(p t) n -> p t n", t=PACK))
+        nc.sync.dma_start(out=w4_codes[:], in_=w4_words.rearrange("b p c -> p b c").bitcast(I32))
+        for q in range(P // QUADRANT):
             nc.sync.dma_start(
-                out=w4s[32 * q : 32 * q + 4, :, :],
+                out=w4_planes[QUADRANT * q : QUADRANT * q + 4, :, :],
                 in_=w4_scales[:, 4 * q : 4 * q + 4, :].rearrange("b r c -> r b c").bitcast(I32),
             )
-        nc.sync.dma_start(out=w1_raw[1][:], in_=w1[PASS : 2 * PASS, :].rearrange("(p t) n -> p t n", t=PACK))
         with nc.allow_non_contiguous_dma(reason="one bias value for each partition and output tile"):
             nc.sync.dma_start(out=bias_t[:], in_=bias.rearrange("(c p) -> p c", p=P))
 
@@ -98,175 +101,178 @@ def tile_list_creative_user_readout_kernel(
         gb_bank = psum.tile([P, PACK, P], F32, name="gb_bank")
         for t in range(PACK):
             nc.tensor.transpose(gb_bank[:, t, :], gb_rows[:, t::PACK], ident[:])
+        gb_psum = gb_bank[:, :, 0:I_PASSES].rearrange("p t b -> p b t")
 
-        cols = HALF // 16
-        vw = [[keep.tile([P, PASS], U32, name="vw%d_%d" % (a, b), align_bytes=64) for b in range(SP)] for a in range(KP)]
-        uw = [[keep.tile([P, HALF], U32, name="uw%d_%d" % (a, h), align_bytes=64) for h in range(2)] for a in range(KP)]
-        vs_listed = keep.tile([P, S], U8, name="vs_listed", align_bytes=64)
-        vs = keep.tile([P, S], U8, name="vs", align_bytes=64)
-        us = keep.tile([P, S2], U8, name="us", align_bytes=64)
+        creative_words = [keep.tile([P, S], U32, name="creative_words%d" % a, align_bytes=64) for a in range(K_PASSES)]
+        user_words = [keep.tile([P, S2], U32, name="user_words%d" % a, align_bytes=64) for a in range(K_PASSES)]
+        listed_planes = keep.tile([P, S], U8, name="listed_planes", align_bytes=64)
+        creative_planes = keep.tile([P, S], U8, name="creative_planes", align_bytes=64)
+        user_planes = keep.tile([P, S2], U8, name="user_planes", align_bytes=64)
 
-        def gather_v(a):
-            for b in range(SP):
+        def gather_creatives(a):
+            nc.vector.tensor_copy(
+                creative_words[a][:].rearrange("p (b t m) -> p b m t", b=I_PASSES, t=PACK),
+                v_words[a][:].bitcast(U32).indirect(idx[:]),
+            )
+
+        gather_creatives(0)
+        nc.vector.tensor_copy(listed_planes[:], v_planes[:].bitcast(U8).indirect(idx[:]))
+        gather_creatives(1)
+        nc.vector.tensor_copy(
+            creative_planes[:].rearrange("p (b t m) -> p b t m", b=I_PASSES, t=PACK),
+            listed_planes[:].rearrange("p (b m t) -> p b t m", b=I_PASSES, t=PACK),
+        )
+        nc.vector.tensor_copy(user_planes[:], v2_planes[:].bitcast(U8).indirect(idx2[:]))
+        for a in range(K_PASSES):
+            for lo in range(0, S2, USER_SLICE):
                 nc.vector.tensor_copy(
-                    vw[a][b][:].rearrange("p (t m) -> p m t", t=PACK),
-                    tw[a][:].bitcast(U32).indirect(idx[:, b * cols : (b + 1) * cols]),
+                    user_words[a][:, lo : lo + USER_SLICE],
+                    v2_words[a][:].bitcast(U32).indirect(idx2[:, lo // LIST_ROWS : (lo + USER_SLICE) // LIST_ROWS]),
                 )
 
-        def gather_u(a):
-            for h in range(2):
-                nc.vector.tensor_copy(uw[a][h][:], t2w[a][:].bitcast(U32).indirect(idx2[:, h * cols : (h + 1) * cols]))
+        w1_bf = [keep.tile([P, N, PACK], BF16, name="w1_bf%d" % b, align_bytes=64) for b in range(I_PASSES)]
+        w1_codes = [keep.tile([P, N], U32, name="w1_codes%d" % b, align_bytes=64) for b in range(I_PASSES)]
+        w1_plane = [keep.tile([P, N], U8, name="w1_plane%d" % b, align_bytes=64) for b in range(I_PASSES)]
 
-        gather_v(0)
-        nc.vector.tensor_copy(vs_listed[:], tsc[:].bitcast(U8).indirect(idx[:]))
-        gather_v(1)
-        nc.vector.tensor_copy(
-            vs[:].rearrange("p (b t m) -> p b t m", b=SP, t=PACK),
-            vs_listed[:].rearrange("p (b m t) -> p b t m", b=SP, t=PACK),
-        )
-        nc.vector.tensor_copy(us[:], t2sc[:].bitcast(U8).indirect(idx2[:]))
-        gather_u(0)
-        gather_u(1)
-
-        w1_bf = [keep.tile([P, N, PACK], BF16, name="w1_bf%d" % b, align_bytes=64) for b in range(SP)]
-        w1_codes = [keep.tile([P, N], U32, name="w1_codes%d" % b, align_bytes=64) for b in range(SP)]
-        w1_scales = [keep.tile([P, N], U8, name="w1_scales%d" % b, align_bytes=64) for b in range(SP)]
-
-        def round_w1(b, c):
-            nc.scalar.copy(
-                out=w1_bf[b][:, c * P : (c + 1) * P, :].rearrange("p (g i) t -> p g t i", i=2),
-                in_=w1_raw[b][:, :, c * P : (c + 1) * P].rearrange("p t (g i) -> p g t i", i=2),
-            )
+        def round_w1(b):
+            for c in range(N_TILES):
+                nc.scalar.copy(
+                    out=w1_bf[b][:, c * P : (c + 1) * P, :].rearrange("p (g i) t -> p g t i", i=2),
+                    in_=w1_raw[b][:, :, c * P : (c + 1) * P].rearrange("p t (g i) -> p g t i", i=2),
+                )
 
         def quantize_w1(b):
             nc.vector.quantize_mx(
-                out=w1_codes[b][:].bitcast(FP8X4), scales=w1_scales[b][:], in_=w1_bf[b][:].rearrange("p n t -> p (n t)")
+                out=w1_codes[b][:].bitcast(FP8X4), scales=w1_plane[b][:], in_=w1_bf[b][:].rearrange("p n t -> p (n t)")
             )
 
-        hq, hq2, th, h_codes, h_scales = {}, {}, {}, {}, {}
+        h1, h2, tanh_a, h_codes, h_plane = {}, {}, {}, {}, {}
 
         def scores(j):
-            half, j0 = divmod(j * JT, HALF)
-            hq[j] = ring.tile([P, SP, JT, PACK], BF16, name="hq", align_bytes=64)
-            th[j] = ring.tile([P, SP, JT, PACK], F32, name="th", align_bytes=64)
-            h_codes[j] = keep.tile([P, 2 * SP * JT], U32, name="h_codes%d" % j, align_bytes=64)
-            h_scales[j] = keep.tile([P, 2 * SP * JT], U8, name="h_scales%d" % j, align_bytes=64)
-            for b in range(SP):
-                acc = psum.tile([P, PACK, JT], F32, name="acc", bufs=4)
-                for a in range(KP):
+            h1[j] = ring.tile([P, I_PASSES, USERS, PACK], BF16, name="h1", align_bytes=64)
+            tanh_a[j] = ring.tile([P, I_PASSES, USERS, PACK], F32, name="tanh_a", align_bytes=64)
+            h_codes[j] = keep.tile([P, 2 * I_PASSES * USERS], U32, name="h_codes%d" % j, align_bytes=64)
+            h_plane[j] = keep.tile([P, 2 * I_PASSES * USERS], U8, name="h_plane%d" % j, align_bytes=64)
+            users = slice(j * USERS, (j + 1) * USERS)
+            for b in range(I_PASSES):
+                acc = psum.tile([P, PACK, USERS], F32, name="acc", bufs=SCORE_BANKS)
+                for a in range(K_PASSES):
                     for t in range(PACK):
+                        slots = slice(b * PASS + t * P, b * PASS + (t + 1) * P)
                         nc.tensor.matmul_mx(
                             out=acc[:, t, :],
-                            lhsT=vw[a][b][:, t * P : (t + 1) * P].bitcast(FP8X4),
-                            lhsT_scale=vs[4 * a :, b * PASS + t * P : b * PASS + (t + 1) * P],
-                            rhs=uw[a][half][:, j0 : j0 + JT].bitcast(FP8X4),
-                            rhs_scale=us[4 * a :, j * JT : (j + 1) * JT],
+                            lhsT=creative_words[a][:, slots].bitcast(FP8X4),
+                            lhsT_scale=creative_planes[4 * a :, slots],
+                            rhs=user_words[a][:, users].bitcast(FP8X4),
+                            rhs_scale=user_planes[4 * a :, users],
                             start=(a == 0 and t == 0),
-                            stop=(a == KP - 1 and t == PACK - 1),
+                            stop=(a == K_PASSES - 1 and t == PACK - 1),
                         )
                 woven = acc[:].rearrange("p t n -> p n t")
 
                 def linear():
                     nc.vector.tensor_tensor(
-                        hq[j][:, b, :, :], woven, ga_t[:, b : b + 1, :].to_broadcast([P, JT, PACK]), MULT
+                        h1[j][:, b, :, :], woven, ga_t[:, b : b + 1, :].to_broadcast([P, USERS, PACK]), MULT
                     )
 
                 def saturate():
-                    nc.scalar.activation(out=th[j][:, b, :, :], in_=woven, func=ACT.Tanh)
+                    nc.scalar.activation(out=tanh_a[j][:, b, :, :], in_=woven, func=ACT.Tanh)
 
                 for step in (linear, saturate) if b == 0 else (saturate, linear):
                     step()
 
-        gb_psum = gb_bank[:, :, 0:SP].rearrange("p t b -> p b t")
-
         def weigh_vector(j, b0, b1, n):
             nc.vector.tensor_tensor(
-                hq2[j][:, b0:b1, 0:n, :],
-                th[j][:, b0:b1, 0:n, :],
+                h2[j][:, b0:b1, 0:n, :],
+                tanh_a[j][:, b0:b1, 0:n, :],
                 gb_psum[:, b0:b1, :].unsqueeze(2).to_broadcast([P, b1 - b0, n, PACK]),
                 MULT,
             )
 
         def weigh_gpsimd(j, n):
             nc.gpsimd.tensor_tensor(
-                hq2[j][:, :, n:JT, :],
-                th[j][:, :, n:JT, :],
-                gb_t[:].unsqueeze(2).to_broadcast([P, SP, JT - n, PACK]),
+                h2[j][:, :, n:USERS, :],
+                tanh_a[j][:, :, n:USERS, :],
+                gb_t[:].unsqueeze(2).to_broadcast([P, I_PASSES, USERS - n, PACK]),
                 MULT,
             )
 
-        def quantize(j, src, g0, lo, hi):
+        def quantize(j, h, g0, b0, b1):
+            columns = slice((g0 + b0) * USERS, (g0 + b1) * USERS)
             nc.vector.quantize_mx(
-                out=h_codes[j][:, (g0 + lo) * JT : (g0 + hi) * JT].bitcast(FP8X4),
-                scales=h_scales[j][:, (g0 + lo) * JT : (g0 + hi) * JT],
-                in_=src[j][:, lo:hi, :, :].rearrange("p g n t -> p (g n t)"),
+                out=h_codes[j][:, columns].bitcast(FP8X4),
+                scales=h_plane[j][:, columns],
+                in_=h[j][:, b0:b1, :, :].rearrange("p b n t -> p (b n t)"),
             )
 
-        def passes(j, y, tiles, order):
+        def readout_passes(j, y, tiles, order):
             for g in order:
-                b = g % SP
+                b = g % I_PASSES
                 for c in tiles:
-                    if g < SP:
+                    if g < I_PASSES:
                         w = w1_codes[b][:, c * P : (c + 1) * P].bitcast(FP8X4)
-                        ws = w1_scales[b][:, c * P : (c + 1) * P]
+                        w_scale = w1_plane[b][:, c * P : (c + 1) * P]
                     else:
-                        w = w4w[:, b, :].bitcast(U8)[:, 2 * c * P : 2 * (c + 1) * P].bitcast(FP4X4)
-                        ws = w4s[:, b, :].bitcast(U8)[:, c * P : (c + 1) * P]
+                        w = w4_codes[:, b, :].bitcast(U8)[:, 2 * c * P : 2 * (c + 1) * P].bitcast(FP4X4)
+                        w_scale = w4_planes[:, b, :].bitcast(U8)[:, c * P : (c + 1) * P]
                     nc.tensor.matmul_mx(
                         out=y[:, c - tiles[0], :],
                         lhsT=w,
-                        lhsT_scale=ws,
-                        rhs=h_codes[j][:, g * JT : (g + 1) * JT].bitcast(FP8X4),
-                        rhs_scale=h_scales[j][:, g * JT : (g + 1) * JT],
+                        lhsT_scale=w_scale,
+                        rhs=h_codes[j][:, g * USERS : (g + 1) * USERS].bitcast(FP8X4),
+                        rhs_scale=h_plane[j][:, g * USERS : (g + 1) * USERS],
                         start=(g == order[0] and c == tiles[0]),
                         stop=(g == order[-1] and c == tiles[-1]),
                     )
 
         out_tiles = out.rearrange("(c p) j -> p c j", p=P)
 
-        def read_out(j):
-            y = psum.tile([P, NT, JT], F32, name="y", bufs=3)
-            res = ring.tile([P, NT, JT], F32, name="res")
-            passes(j, y, [0, 1, 2, 3], [2, 3, 0, 1] if j < EARLY else [0, 1, 2, 3])
-            for c in range(NT):
+        def add_bias_scalar(res, y, count):
+            for c in range(count):
                 nc.scalar.activation(out=res[:, c, :], in_=y[:, c, :], func=ACT.Identity, bias=bias_t[:, c : c + 1])
-            nc.sync.dma_start(out=out_tiles[:, :, j * JT : (j + 1) * JT], in_=res[:])
 
-        def read_out_last(j):
-            ys = [psum.tile([P, 2, JT], F32, name="y", bufs=3) for u in range(2)]
+        def read_out(j):
+            y = psum.tile([P, N_TILES, USERS], F32, name="y", bufs=OUT_BANKS)
+            res = ring.tile([P, N_TILES, USERS], F32, name="res")
+            readout_passes(j, y, list(range(N_TILES)), list(range(2 * I_PASSES)))
+            add_bias_scalar(res, y, N_TILES)
+            nc.sync.dma_start(out=out_tiles[:, :, j * USERS : (j + 1) * USERS], in_=res[:])
+
+        def read_out_last(j, order):
+            half = N_TILES // 2
+            users = slice(j * USERS, (j + 1) * USERS)
+            ys = [psum.tile([P, half, USERS], F32, name="y", bufs=OUT_BANKS) for u in range(2)]
             for u in range(2):
-                passes(j, ys[u], [2 * u, 2 * u + 1], [0, 1, 3, 2])
-            res0 = ring.tile([P, 2, JT], F32, name="res")
-            for c in range(2):
-                nc.scalar.activation(out=res0[:, c, :], in_=ys[0][:, c, :], func=ACT.Identity, bias=bias_t[:, c : c + 1])
-            nc.sync.dma_start(out=out_tiles[:, 0:2, j * JT : (j + 1) * JT], in_=res0[:])
-            res1 = ring.tile([P, 2, JT], F32, name="res")
-            nc.vector.tensor_tensor(res1[:], ys[1][:], bias_t[:, 2:4].unsqueeze(2).to_broadcast([P, 2, JT]), ADD)
-            nc.sync.dma_start(out=out_tiles[:, 2:4, j * JT : (j + 1) * JT], in_=res1[:])
+                readout_passes(j, ys[u], list(range(half * u, half * (u + 1))), order)
+            res_low = ring.tile([P, half, USERS], F32, name="res")
+            add_bias_scalar(res_low, ys[0], half)
+            nc.scalar.dma_start(out=out_tiles[:, 0:half, users], in_=res_low[:])
+            res_high = ring.tile([P, half, USERS], F32, name="res")
+            nc.vector.tensor_tensor(
+                res_high[:], ys[1][:], bias_t[:, half:N_TILES].unsqueeze(2).to_broadcast([P, half, USERS]), ADD
+            )
+            nc.sync.dma_start(out=out_tiles[:, half:N_TILES, users], in_=res_high[:])
 
-        for s in range(NJ):
+        for s in range(USER_TILES):
             scores(s)
-            if s < 2 * SP:
-                round_w1(s // 2, 2 * (s % 2))
-                round_w1(s // 2, 2 * (s % 2) + 1)
+            if s < I_PASSES:
+                round_w1(s)
             if s >= 1:
-                hq2[s - 1] = ring.tile([P, SP, JT, PACK], BF16, name="hq2", bufs=1, align_bytes=64)
-                weigh_gpsimd(s - 1, JT - G_COLS)
-                weigh_vector(s - 1, 0, SP, JT - G_COLS)
-            quantize(s, hq, 0, 0, SP)
+                h2[s - 1] = ring.tile([P, I_PASSES, USERS, PACK], BF16, name="h2", bufs=1, align_bytes=64)
+                weigh_gpsimd(s - 1, USERS - GPSIMD_USERS)
+                weigh_vector(s - 1, 0, I_PASSES, USERS - GPSIMD_USERS)
+            quantize(s, h1, 0, 0, I_PASSES)
             if s >= 1:
-                quantize(s - 1, hq2, SP, 0, SP)
-            if s in (1, 3):
-                quantize_w1(s // 2)
-            if s == EARLY:
-                for j in range(EARLY):
-                    read_out(j)
-            if s > EARLY:
+                quantize(s - 1, h2, I_PASSES, 0, I_PASSES)
+            if s < I_PASSES:
+                quantize_w1(s)
+            if s >= 1:
                 read_out(s - 1)
-        last = NJ - 1
-        hq2[last] = ring.tile([P, SP, JT, PACK], BF16, name="hq2_last", bufs=1, align_bytes=64)
-        for b in (1, 0):
-            weigh_vector(last, b, b + 1, JT)
-        for b in (1, 0):
-            quantize(last, hq2, SP, b, b + 1)
-        read_out_last(last)
+
+        last = USER_TILES - 1
+        h2[last] = ring.tile([P, I_PASSES, USERS, PACK], BF16, name="h2_last", bufs=1, align_bytes=64)
+        for b in reversed(range(I_PASSES)):
+            weigh_vector(last, b, b + 1, USERS)
+        for b in reversed(range(I_PASSES)):
+            quantize(last, h2, I_PASSES, b, b + 1)
+        read_out_last(last, list(range(I_PASSES)) + [I_PASSES + b for b in reversed(range(I_PASSES))])

@@ -32,6 +32,7 @@ USER_SLICE = 512
 GPSIMD_USERS = 40
 SCORE_BANKS = 5
 OUT_BANKS = 2
+USER_ROWS_AT = 4 * (T + T2)
 
 
 def tile_list_creative_user_readout_kernel(
@@ -40,61 +41,47 @@ def tile_list_creative_user_readout_kernel(
     nc = tc.nc
     with ExitStack() as ctx:
         keep = ctx.enter_context(tc.tile_pool(name="keep", bufs=1))
+        shared = ctx.enter_context(tc.tile_pool(name="shared", bufs=1))
         ring = ctx.enter_context(tc.tile_pool(name="ring", bufs=3))
         psum = ctx.enter_context(tc.psum_pool(name="psum", bufs=1))
 
         idx = keep.tile([P, S // LIST_ROWS], U16, name="idx")
         idx2 = keep.tile([P, S2 // LIST_ROWS], U16, name="idx2")
-        v_words = [keep.tile([P, T], I32, name="v_words%d" % a, align_bytes=64) for a in range(K_PASSES)]
-        v2_words = [keep.tile([P, T2], I32, name="v2_words%d" % a, align_bytes=64) for a in range(K_PASSES)]
-        v_planes = keep.tile([P, T // 4], I32, name="v_planes", align_bytes=64)
-        v2_planes = keep.tile([P, T2 // 4], I32, name="v2_planes", align_bytes=64)
-        w4_planes = keep.tile([P, I_PASSES, N // 4], I32, name="w4_planes", align_bytes=64)
-        w4_codes = keep.tile([P, I_PASSES, N // 2], I32, name="w4_codes", align_bytes=64)
+        v_words = [
+            shared.tile([P, T], I32, name="v_words0", align_bytes=64, offset=0),
+            shared.tile([P, T], I32, name="v_words1", align_bytes=64, offset=USER_ROWS_AT),
+        ]
+        v2_words = [
+            shared.tile([P, T2], I32, name="v2_words0", align_bytes=64, offset=4 * T),
+            keep.tile([P, T2], I32, name="v2_words1", align_bytes=64),
+        ]
+        v_rows = keep.tile([P, T // 4], I32, name="v_rows", align_bytes=64)
+        v2_rows = keep.tile([P, T2 // 4], I32, name="v2_rows", align_bytes=64)
         ga_t = keep.tile([P, I_PASSES, PACK], F32, name="ga_t")
         gb_t = keep.tile([P, I_PASSES, PACK], F32, name="gb_t")
-        bias_t = keep.tile([P, N_TILES], F32, name="bias_t")
-        w1_raw = [keep.tile([P, PACK, N], F32, name="w1_raw%d" % b, align_bytes=64) for b in range(I_PASSES)]
-
-        nc.vector.memset(v_planes[:], 0)
-        nc.vector.memset(v2_planes[:], 0)
-        nc.vector.memset(w4_planes[:], 0)
         gb_rows = keep.tile([P, PASS], F32, name="gb_rows")
+
+        nc.vector.memset(v_rows[:], 0)
+        nc.vector.memset(v2_rows[:], 0)
         nc.vector.memset(gb_rows[:], 0.0)
 
-        def load_words(tile, words):
-            nc.sync.dma_start(out=tile[:], in_=words.rearrange("p n t -> p (n t)").bitcast(I32))
+        def load_words(tile, words, lo, hi):
+            nc.sync.dma_start(out=tile[:, lo:hi], in_=words[:, lo:hi, :].rearrange("p n t -> p (n t)").bitcast(I32))
 
-        def load_planes(tile, scales, quadrants):
-            for q in quadrants:
-                nc.sync.dma_start(
-                    out=tile[QUADRANT * q : QUADRANT * q + 4 * K_PASSES, :],
-                    in_=scales[:, 4 * q : 4 * q + 4, :].bitcast(I32),
-                )
+        def load_rows(tile, scales):
+            nc.sync.dma_start(out=tile[0:P:4, :], in_=scales.rearrange("a q n -> q a n").bitcast(I32))
 
-        load_words(v_words[0], tab_words[0])
+        load_words(v_words[0], tab_words[0], 0, T // 2)
+        load_rows(v_rows, tab_scales)
+        load_rows(v2_rows, tab2_scales)
         nc.sync.dma_start(idx[:], offs)
-        load_planes(v_planes, tab_scales, (2, 3))
-        load_planes(v2_planes, tab2_scales, (2, 3))
-        load_planes(v_planes, tab_scales, (0, 1))
-        load_words(v_words[1], tab_words[1])
-        load_planes(v2_planes, tab2_scales, (0, 1))
         nc.sync.dma_start(idx2[:], offs2)
-        nc.sync.dma_start(out=gb_rows[0:I_PASSES, :], in_=gb.rearrange("(b i) -> b i", b=I_PASSES))
-        load_words(v2_words[0], tab2_words[0])
-        load_words(v2_words[1], tab2_words[1])
+        load_words(v_words[0], tab_words[0], T // 2, T)
+        load_words(v2_words[0], tab2_words[0], 0, T2)
         nc.sync.dma_start(out=ga_t[:], in_=ga.rearrange("(b p t) -> p b t", p=P, t=PACK))
+        nc.sync.dma_start(out=gb_rows[0:I_PASSES, :], in_=gb.rearrange("(b i) -> b i", b=I_PASSES))
         nc.sync.dma_start(out=gb_t[:], in_=gb.rearrange("(b p t) -> p b t", p=P, t=PACK))
-        for b in range(I_PASSES):
-            nc.sync.dma_start(out=w1_raw[b][:], in_=w1[b * PASS : (b + 1) * PASS, :].rearrange("(p t) n -> p t n", t=PACK))
-        nc.sync.dma_start(out=w4_codes[:], in_=w4_words.rearrange("b p c -> p b c").bitcast(I32))
-        for q in range(P // QUADRANT):
-            nc.sync.dma_start(
-                out=w4_planes[QUADRANT * q : QUADRANT * q + 4, :, :],
-                in_=w4_scales[:, 4 * q : 4 * q + 4, :].rearrange("b r c -> r b c").bitcast(I32),
-            )
-        with nc.allow_non_contiguous_dma(reason="one bias value for each partition and output tile"):
-            nc.sync.dma_start(out=bias_t[:], in_=bias.rearrange("(c p) -> p c", p=P))
+        load_words(v2_words[1], tab2_words[1], 0, T2)
 
         ident = keep.tile([P, P], F32, name="ident")
         make_identity(nc, ident[:])
@@ -105,30 +92,64 @@ def tile_list_creative_user_readout_kernel(
 
         creative_words = [keep.tile([P, S], U32, name="creative_words%d" % a, align_bytes=64) for a in range(K_PASSES)]
         user_words = [keep.tile([P, S2], U32, name="user_words%d" % a, align_bytes=64) for a in range(K_PASSES)]
-        listed_planes = keep.tile([P, S], U8, name="listed_planes", align_bytes=64)
-        creative_planes = keep.tile([P, S], U8, name="creative_planes", align_bytes=64)
-        user_planes = keep.tile([P, S2], U8, name="user_planes", align_bytes=64)
+        creative_rows = keep.tile([P, S], U8, name="creative_rows", align_bytes=64)
+        user_rows = shared.tile([P, S2], U8, name="user_rows", align_bytes=64, offset=USER_ROWS_AT)
+        planes = keep.tile([P, S + S2], U8, name="planes", align_bytes=64)
+        creative_planes = planes[:, 0:S]
+        user_planes = planes[:, S : S + S2]
 
-        def gather_creatives(a):
+        nc.vector.tensor_copy(creative_rows[:], v_rows[:].bitcast(U8).indirect(idx[:]))
+        nc.vector.tensor_copy(user_rows[:], v2_rows[:].bitcast(U8).indirect(idx2[:]))
+        nc.vector.tensor_copy(
+            creative_planes.rearrange("p (b t m) -> p b t m", b=I_PASSES, t=PACK),
+            creative_rows[:].rearrange("p (b m t) -> p b t m", b=I_PASSES, t=PACK),
+        )
+        nc.vector.tensor_copy(user_planes.bitcast(I32), user_rows[:].bitcast(I32))
+        for r in range(1, 4):
+            for a in range(K_PASSES):
+                nc.sync.dma_start(
+                    out=planes[4 * a + r : P : QUADRANT, :].bitcast(I32),
+                    in_=planes[4 * a + 8 * r : P : QUADRANT, :].bitcast(I32),
+                )
+        load_words(v_words[1], tab_words[1], 0, T)
+
+        def gather_creatives(a, lo, hi):
             nc.vector.tensor_copy(
-                creative_words[a][:].rearrange("p (b t m) -> p b m t", b=I_PASSES, t=PACK),
-                v_words[a][:].bitcast(U32).indirect(idx[:]),
+                creative_words[a][:, lo:hi].rearrange("p (b t m) -> p b m t", m=P, t=PACK),
+                v_words[a][:].bitcast(U32).indirect(idx[:, lo // LIST_ROWS : hi // LIST_ROWS]),
             )
 
-        gather_creatives(0)
-        nc.vector.tensor_copy(listed_planes[:], v_planes[:].bitcast(U8).indirect(idx[:]))
-        gather_creatives(1)
-        nc.vector.tensor_copy(
-            creative_planes[:].rearrange("p (b t m) -> p b t m", b=I_PASSES, t=PACK),
-            listed_planes[:].rearrange("p (b m t) -> p b t m", b=I_PASSES, t=PACK),
-        )
-        nc.vector.tensor_copy(user_planes[:], v2_planes[:].bitcast(U8).indirect(idx2[:]))
+        gather_creatives(0, 0, S)
         for a in range(K_PASSES):
             for lo in range(0, S2, USER_SLICE):
                 nc.vector.tensor_copy(
                     user_words[a][:, lo : lo + USER_SLICE],
                     v2_words[a][:].bitcast(U32).indirect(idx2[:, lo // LIST_ROWS : (lo + USER_SLICE) // LIST_ROWS]),
                 )
+        for b in range(I_PASSES):
+            gather_creatives(1, b * PASS, (b + 1) * PASS)
+
+        w1_raw = [
+            shared.tile([P, PACK, N], F32, name="w1_raw%d" % b, align_bytes=64, offset=4 * T * b) for b in range(I_PASSES)
+        ]
+        w4_codes = shared.tile([P, I_PASSES, N // 2], I32, name="w4_codes", align_bytes=64, offset=8 * T)
+        w4_planes = shared.tile([P, I_PASSES, N // 4], I32, name="w4_planes", align_bytes=64, offset=9 * T)
+        bias_t = shared.tile([P, N_TILES], F32, name="bias_t", align_bytes=64, offset=10 * T)
+        nc.gpsimd.memset(w4_planes[:], 0)
+
+        def load_w1(b):
+            nc.sync.dma_start(out=w1_raw[b][:], in_=w1[b * PASS : (b + 1) * PASS, :].rearrange("(p t) n -> p t n", t=PACK))
+
+        load_w1(0)
+        load_w1(1)
+        nc.sync.dma_start(out=w4_codes[:], in_=w4_words.rearrange("b p c -> p b c").bitcast(I32))
+        for q in range(P // QUADRANT):
+            nc.sync.dma_start(
+                out=w4_planes[QUADRANT * q : QUADRANT * q + 4, :, :],
+                in_=w4_scales[:, 4 * q : 4 * q + 4, :].rearrange("b r c -> r b c").bitcast(I32),
+            )
+        with nc.allow_non_contiguous_dma(reason="one bias value for each partition and output tile"):
+            nc.sync.dma_start(out=bias_t[:], in_=bias.rearrange("(c p) -> p c", p=P))
 
         w1_bf = [keep.tile([P, N, PACK], BF16, name="w1_bf%d" % b, align_bytes=64) for b in range(I_PASSES)]
         w1_codes = [keep.tile([P, N], U32, name="w1_codes%d" % b, align_bytes=64) for b in range(I_PASSES)]
@@ -162,9 +183,9 @@ def tile_list_creative_user_readout_kernel(
                         nc.tensor.matmul_mx(
                             out=acc[:, t, :],
                             lhsT=creative_words[a][:, slots].bitcast(FP8X4),
-                            lhsT_scale=creative_planes[4 * a :, slots],
+                            lhsT_scale=planes[4 * a :, slots],
                             rhs=user_words[a][:, users].bitcast(FP8X4),
-                            rhs_scale=user_planes[4 * a :, users],
+                            rhs_scale=planes[4 * a :, S + j * USERS : S + (j + 1) * USERS],
                             start=(a == 0 and t == 0),
                             stop=(a == K_PASSES - 1 and t == PACK - 1),
                         )

@@ -29,9 +29,10 @@ USER_TILES = S2 // USERS
 N_TILES = N // P
 LIST_ROWS = 16
 USER_SLICE = 512
-GPSIMD_USERS = 40
-SCORE_BANKS = 5
-OUT_BANKS = 2
+PAIR = 2 * USERS
+WIDE = 4 * USERS
+GPSIMD_USERS = 128
+SCORE_RING = 3
 USER_ROWS_AT = 4 * (T + T2)
 
 
@@ -57,13 +58,11 @@ def tile_list_creative_user_readout_kernel(
         ]
         v_rows = keep.tile([P, T // 4], I32, name="v_rows", align_bytes=64)
         v2_rows = keep.tile([P, T2 // 4], I32, name="v2_rows", align_bytes=64)
-        ga_t = keep.tile([P, I_PASSES, PACK], F32, name="ga_t")
-        gb_t = keep.tile([P, I_PASSES, PACK], F32, name="gb_t")
-        gb_rows = keep.tile([P, PASS], F32, name="gb_rows")
+        g_rows = keep.tile([P, PASS], F32, name="g_rows")
 
         nc.vector.memset(v_rows[:], 0)
         nc.vector.memset(v2_rows[:], 0)
-        nc.vector.memset(gb_rows[:], 0.0)
+        nc.vector.memset(g_rows[:], 0.0)
 
         def load_words(tile, words, lo, hi):
             nc.sync.dma_start(out=tile[:, lo:hi], in_=words[:, lo:hi, :].rearrange("p n t -> p (n t)").bitcast(I32))
@@ -71,24 +70,27 @@ def tile_list_creative_user_readout_kernel(
         def load_rows(tile, scales):
             nc.sync.dma_start(out=tile[0:P:4, :], in_=scales.rearrange("a q n -> q a n").bitcast(I32))
 
-        load_words(v_words[0], tab_words[0], 0, T // 2)
+        load_words(v_words[0], tab_words[0], 0, T // 4)
         load_rows(v_rows, tab_scales)
-        load_rows(v2_rows, tab2_scales)
         nc.sync.dma_start(idx[:], offs)
+        load_words(v_words[0], tab_words[0], T // 4, T)
+        load_rows(v2_rows, tab2_scales)
         nc.sync.dma_start(idx2[:], offs2)
-        load_words(v_words[0], tab_words[0], T // 2, T)
         load_words(v2_words[0], tab2_words[0], 0, T2)
-        nc.sync.dma_start(out=ga_t[:], in_=ga.rearrange("(b p t) -> p b t", p=P, t=PACK))
-        nc.sync.dma_start(out=gb_rows[0:I_PASSES, :], in_=gb.rearrange("(b i) -> b i", b=I_PASSES))
-        nc.sync.dma_start(out=gb_t[:], in_=gb.rearrange("(b p t) -> p b t", p=P, t=PACK))
+        for row, g in ((0, ga), (I_PASSES, gb)):
+            nc.sync.dma_start(out=g_rows[row : row + I_PASSES, :], in_=g.rearrange("(b i) -> b i", b=I_PASSES))
         load_words(v2_words[1], tab2_words[1], 0, T2)
 
         ident = keep.tile([P, P], F32, name="ident")
         make_identity(nc, ident[:])
         gb_bank = psum.tile([P, PACK, P], F32, name="gb_bank")
         for t in range(PACK):
-            nc.tensor.transpose(gb_bank[:, t, :], gb_rows[:, t::PACK], ident[:])
-        gb_psum = gb_bank[:, :, 0:I_PASSES].rearrange("p t b -> p b t")
+            nc.tensor.transpose(gb_bank[:, t, :], g_rows[:, t::PACK], ident[:])
+        gb_psum = gb_bank[:, :, I_PASSES : 2 * I_PASSES].rearrange("p t b -> p b t")
+        g_t = keep.tile([P, 2 * I_PASSES, PACK], F32, name="g_t")
+        nc.scalar.copy(out=g_t[:], in_=gb_bank[:, :, 0 : 2 * I_PASSES].rearrange("p t b -> p b t"))
+        ga_t = g_t[:, 0:I_PASSES, :]
+        gb_t = g_t[:, I_PASSES : 2 * I_PASSES, :]
 
         creative_words = [keep.tile([P, S], U32, name="creative_words%d" % a, align_bytes=64) for a in range(K_PASSES)]
         user_words = [keep.tile([P, S2], U32, name="user_words%d" % a, align_bytes=64) for a in range(K_PASSES)]
@@ -135,7 +137,7 @@ def tile_list_creative_user_readout_kernel(
         w4_codes = shared.tile([P, I_PASSES, N // 2], I32, name="w4_codes", align_bytes=64, offset=8 * T)
         w4_planes = shared.tile([P, I_PASSES, N // 4], I32, name="w4_planes", align_bytes=64, offset=9 * T)
         bias_t = shared.tile([P, N_TILES], F32, name="bias_t", align_bytes=64, offset=10 * T)
-        nc.gpsimd.memset(w4_planes[:], 0)
+        nc.vector.memset(w4_planes[:], 0)
 
         def load_w1(b):
             nc.sync.dma_start(out=w1_raw[b][:], in_=w1[b * PASS : (b + 1) * PASS, :].rearrange("(p t) n -> p t n", t=PACK))
@@ -155,8 +157,8 @@ def tile_list_creative_user_readout_kernel(
         w1_codes = [keep.tile([P, N], U32, name="w1_codes%d" % b, align_bytes=64) for b in range(I_PASSES)]
         w1_plane = [keep.tile([P, N], U8, name="w1_plane%d" % b, align_bytes=64) for b in range(I_PASSES)]
 
-        def round_w1(b):
-            for c in range(N_TILES):
+        def round_w1(b, tiles):
+            for c in tiles:
                 nc.scalar.copy(
                     out=w1_bf[b][:, c * P : (c + 1) * P, :].rearrange("p (g i) t -> p g t i", i=2),
                     in_=w1_raw[b][:, :, c * P : (c + 1) * P].rearrange("p t (g i) -> p g t i", i=2),
@@ -167,133 +169,203 @@ def tile_list_creative_user_readout_kernel(
                 out=w1_codes[b][:].bitcast(FP8X4), scales=w1_plane[b][:], in_=w1_bf[b][:].rearrange("p n t -> p (n t)")
             )
 
-        h1, h2, tanh_a, h_codes, h_plane = {}, {}, {}, {}, {}
+        steps = [(0, 0), (0, 1), (1, 0), (1, 1), (0, 2), (1, 2), (0, 3), (1, 3)]
+        h_codes = [keep.tile([P, S2], U32, name="h_codes%d" % g, align_bytes=64) for g in range(2 * I_PASSES)]
+        h_plane = [keep.tile([P, S2], U8, name="h_plane%d" % g, align_bytes=64) for g in range(2 * I_PASSES)]
+        h1 = [keep.tile([P, S2 * PACK], BF16, name="h1_%d" % b, align_bytes=64) for b in range(I_PASSES)]
 
-        def scores(j):
-            h1[j] = ring.tile([P, I_PASSES, USERS, PACK], BF16, name="h1", align_bytes=64)
-            tanh_a[j] = ring.tile([P, I_PASSES, USERS, PACK], F32, name="tanh_a", align_bytes=64)
-            h_codes[j] = keep.tile([P, 2 * I_PASSES * USERS], U32, name="h_codes%d" % j, align_bytes=64)
-            h_plane[j] = keep.tile([P, 2 * I_PASSES * USERS], U8, name="h_plane%d" % j, align_bytes=64)
-            users = slice(j * USERS, (j + 1) * USERS)
-            for b in range(I_PASSES):
-                acc = psum.tile([P, PACK, USERS], F32, name="acc", bufs=SCORE_BANKS)
+        def quantised(g, lo, hi):
+            return h_codes[g][:, lo:hi].bitcast(FP8X4), h_plane[g][:, lo:hi]
+
+        def bank(number):
+            return psum.tile([P, PASS], F32, name="bank%d" % number)
+
+        h2, tanh_a = {}, {}
+
+        def scores(s):
+            b, pair = steps[s]
+            tanh_a[s] = ring.tile([P, PAIR, PACK], F32, name="tanh_a", align_bytes=64)
+            for e in range(2):
+                n = 2 * s + e
+                acc = bank(SCORE_RING + n if n < N_TILES else (n - N_TILES) % SCORE_RING)
+                lo = pair * PAIR + e * USERS
                 for a in range(K_PASSES):
                     for t in range(PACK):
                         slots = slice(b * PASS + t * P, b * PASS + (t + 1) * P)
                         nc.tensor.matmul_mx(
-                            out=acc[:, t, :],
+                            out=acc[:, t * USERS : (t + 1) * USERS],
                             lhsT=creative_words[a][:, slots].bitcast(FP8X4),
                             lhsT_scale=planes[4 * a :, slots],
-                            rhs=user_words[a][:, users].bitcast(FP8X4),
-                            rhs_scale=planes[4 * a :, S + j * USERS : S + (j + 1) * USERS],
+                            rhs=user_words[a][:, lo : lo + USERS].bitcast(FP8X4),
+                            rhs_scale=planes[4 * a :, S + lo : S + lo + USERS],
                             start=(a == 0 and t == 0),
                             stop=(a == K_PASSES - 1 and t == PACK - 1),
                         )
-                woven = acc[:].rearrange("p t n -> p n t")
+                woven = acc[:].rearrange("p (t n) -> p n t", t=PACK)
+                tile_users = slice(e * USERS, (e + 1) * USERS)
 
                 def linear():
                     nc.vector.tensor_tensor(
-                        h1[j][:, b, :, :], woven, ga_t[:, b : b + 1, :].to_broadcast([P, USERS, PACK]), MULT
+                        h1[b][:, PACK * lo : PACK * (lo + USERS)].rearrange("p (n t) -> p n t", t=PACK),
+                        woven,
+                        ga_t[:, b : b + 1, :].to_broadcast([P, USERS, PACK]),
+                        MULT,
                     )
 
                 def saturate():
-                    nc.scalar.activation(out=tanh_a[j][:, b, :, :], in_=woven, func=ACT.Tanh)
+                    nc.scalar.activation(out=tanh_a[s][:, tile_users, :], in_=woven, func=ACT.Tanh)
 
-                for step in (linear, saturate) if b == 0 else (saturate, linear):
-                    step()
+                for reader in (linear, saturate) if s >= 2 else (saturate, linear):
+                    reader()
 
-        def weigh_vector(j, b0, b1, n):
+        def weigh_vector(s, lo, hi):
+            b = steps[s][0]
             nc.vector.tensor_tensor(
-                h2[j][:, b0:b1, 0:n, :],
-                tanh_a[j][:, b0:b1, 0:n, :],
-                gb_psum[:, b0:b1, :].unsqueeze(2).to_broadcast([P, b1 - b0, n, PACK]),
-                MULT,
+                h2[s][:, lo:hi, :], tanh_a[s][:, lo:hi, :], gb_psum[:, b : b + 1, :].to_broadcast([P, hi - lo, PACK]), MULT
             )
 
-        def weigh_gpsimd(j, n):
+        def weigh_gpsimd(s, lo, hi):
+            b = steps[s][0]
             nc.gpsimd.tensor_tensor(
-                h2[j][:, :, n:USERS, :],
-                tanh_a[j][:, :, n:USERS, :],
-                gb_t[:].unsqueeze(2).to_broadcast([P, I_PASSES, USERS - n, PACK]),
-                MULT,
+                h2[s][:, lo:hi, :], tanh_a[s][:, lo:hi, :], gb_t[:, b : b + 1, :].to_broadcast([P, hi - lo, PACK]), MULT
             )
 
-        def quantize(j, h, g0, b0, b1):
-            columns = slice((g0 + b0) * USERS, (g0 + b1) * USERS)
-            nc.vector.quantize_mx(
-                out=h_codes[j][:, columns].bitcast(FP8X4),
-                scales=h_plane[j][:, columns],
-                in_=h[j][:, b0:b1, :, :].rearrange("p b n t -> p (b n t)"),
-            )
+        def quantize_h1(b, lo, hi):
+            codes, plane = quantised(b, lo, hi)
+            nc.vector.quantize_mx(out=codes, scales=plane, in_=h1[b][:, PACK * lo : PACK * hi])
 
-        def readout_passes(j, y, tiles, order):
-            for g in order:
-                b = g % I_PASSES
-                for c in tiles:
-                    if g < I_PASSES:
-                        w = w1_codes[b][:, c * P : (c + 1) * P].bitcast(FP8X4)
-                        w_scale = w1_plane[b][:, c * P : (c + 1) * P]
-                    else:
-                        w = w4_codes[:, b, :].bitcast(U8)[:, 2 * c * P : 2 * (c + 1) * P].bitcast(FP4X4)
-                        w_scale = w4_planes[:, b, :].bitcast(U8)[:, c * P : (c + 1) * P]
-                    nc.tensor.matmul_mx(
-                        out=y[:, c - tiles[0], :],
-                        lhsT=w,
-                        lhsT_scale=w_scale,
-                        rhs=h_codes[j][:, g * USERS : (g + 1) * USERS].bitcast(FP8X4),
-                        rhs_scale=h_plane[j][:, g * USERS : (g + 1) * USERS],
-                        start=(g == order[0] and c == tiles[0]),
-                        stop=(g == order[-1] and c == tiles[-1]),
-                    )
+        def quantize_h2(s, lo, hi):
+            b, pair = steps[s]
+            codes, plane = quantised(I_PASSES + b, pair * PAIR + lo, pair * PAIR + hi)
+            nc.vector.quantize_mx(out=codes, scales=plane, in_=h2[s][:, lo:hi, :].rearrange("p n t -> p (n t)"))
+
+        def readout_pair(g, y, tiles, lo, start, stop):
+            if g < I_PASSES:
+                readout(g, y, tiles, lo, lo + PAIR, PAIR, 0, start, stop)
+            else:
+                readout(g, y, tiles, lo, lo + USERS, PAIR, 0, start, False)
+                readout(g, y, tiles, lo + USERS, lo + PAIR, PAIR, USERS, False, stop)
+
+        def readout(g, y, tiles, lo, hi, pitch, at, start, stop):
+            b = g % I_PASSES
+            codes, plane = quantised(g, lo, hi)
+            width = hi - lo
+            for c in tiles:
+                if g < I_PASSES:
+                    w = w1_codes[b][:, c * P : (c + 1) * P].bitcast(FP8X4)
+                    w_scale = w1_plane[b][:, c * P : (c + 1) * P]
+                else:
+                    w = w4_codes[:, b, :].bitcast(U8)[:, 2 * c * P : 2 * (c + 1) * P].bitcast(FP4X4)
+                    w_scale = w4_planes[:, b, :].bitcast(U8)[:, c * P : (c + 1) * P]
+                place = c - tiles[0]
+                nc.tensor.matmul_mx(
+                    out=y[:, place * pitch + at : place * pitch + at + width],
+                    lhsT=w,
+                    lhsT_scale=w_scale,
+                    rhs=codes,
+                    rhs_scale=plane,
+                    start=(start and c == tiles[0]),
+                    stop=(stop and c == tiles[-1]),
+                )
 
         out_tiles = out.rearrange("(c p) j -> p c j", p=P)
 
-        def add_bias_scalar(res, y, count):
-            for c in range(count):
-                nc.scalar.activation(out=res[:, c, :], in_=y[:, c, :], func=ACT.Identity, bias=bias_t[:, c : c + 1])
+        def store_scalar(y, tiles, lo, hi, queue):
+            width = hi - lo
+            res = ring.tile([P, len(tiles), width], F32, name="res", bufs=4)
+            for place, c in enumerate(tiles):
+                nc.scalar.activation(
+                    out=res[:, place, :],
+                    in_=y[:, place * width : (place + 1) * width],
+                    func=ACT.Identity,
+                    bias=bias_t[:, c : c + 1],
+                )
+            queue.dma_start(out=out_tiles[:, tiles[0] : tiles[-1] + 1, lo:hi], in_=res[:])
 
-        def read_out(j):
-            y = psum.tile([P, N_TILES, USERS], F32, name="y", bufs=OUT_BANKS)
-            res = ring.tile([P, N_TILES, USERS], F32, name="res")
-            readout_passes(j, y, list(range(N_TILES)), list(range(2 * I_PASSES)))
-            add_bias_scalar(res, y, N_TILES)
-            nc.sync.dma_start(out=out_tiles[:, :, j * USERS : (j + 1) * USERS], in_=res[:])
-
-        def read_out_last(j, order):
-            half = N_TILES // 2
-            users = slice(j * USERS, (j + 1) * USERS)
-            ys = [psum.tile([P, half, USERS], F32, name="y", bufs=OUT_BANKS) for u in range(2)]
-            for u in range(2):
-                readout_passes(j, ys[u], list(range(half * u, half * (u + 1))), order)
-            res_low = ring.tile([P, half, USERS], F32, name="res")
-            add_bias_scalar(res_low, ys[0], half)
-            nc.scalar.dma_start(out=out_tiles[:, 0:half, users], in_=res_low[:])
-            res_high = ring.tile([P, half, USERS], F32, name="res")
+        def store_vector(y, tiles, lo, hi):
+            width = hi - lo
+            res = ring.tile([P, len(tiles), width], F32, name="res", bufs=4)
             nc.vector.tensor_tensor(
-                res_high[:], ys[1][:], bias_t[:, half:N_TILES].unsqueeze(2).to_broadcast([P, half, USERS]), ADD
+                res[:],
+                y[:, 0 : len(tiles) * width].rearrange("p (c n) -> p c n", n=width),
+                bias_t[:, tiles[0] : tiles[-1] + 1].unsqueeze(2).to_broadcast([P, len(tiles), width]),
+                ADD,
             )
-            nc.sync.dma_start(out=out_tiles[:, half:N_TILES, users], in_=res_high[:])
+            nc.sync.dma_start(out=out_tiles[:, tiles[0] : tiles[-1] + 1, lo:hi], in_=res[:])
 
-        for s in range(USER_TILES):
+        every = list(range(N_TILES))
+        low, high = every[:2], every[2:]
+        wide_y = []
+
+        def wide_pass(g, start, stop):
+            for c in every:
+                if start:
+                    wide_y.append(bank(SCORE_RING + c))
+                readout(g, wide_y[c], [c], 0, WIDE, WIDE, 0, start, stop)
+
+        def step(s):
             scores(s)
-            if s < I_PASSES:
-                round_w1(s)
+            if s == 1:
+                round_w1(0, every)
+            elif s in (2, 3):
+                round_w1(1, low if s == 2 else high)
             if s >= 1:
-                h2[s - 1] = ring.tile([P, I_PASSES, USERS, PACK], BF16, name="h2", bufs=1, align_bytes=64)
-                weigh_gpsimd(s - 1, USERS - GPSIMD_USERS)
-                weigh_vector(s - 1, 0, I_PASSES, USERS - GPSIMD_USERS)
-            quantize(s, h1, 0, 0, I_PASSES)
+                h2[s - 1] = ring.tile([P, PAIR, PACK], BF16, name="h2", bufs=1, align_bytes=64)
+                weigh_gpsimd(s - 1, 0, GPSIMD_USERS)
+                weigh_vector(s - 1, GPSIMD_USERS, PAIR)
+            b, pair = steps[s]
+            if s == 1:
+                quantize_h1(b, 0, WIDE)
+            elif s > 1:
+                quantize_h1(b, pair * PAIR, (pair + 1) * PAIR)
             if s >= 1:
-                quantize(s - 1, h2, I_PASSES, 0, I_PASSES)
-            if s < I_PASSES:
-                quantize_w1(s)
-            if s >= 1:
-                read_out(s - 1)
+                quantize_h2(s - 1, 0, PAIR)
 
-        last = USER_TILES - 1
-        h2[last] = ring.tile([P, I_PASSES, USERS, PACK], BF16, name="h2_last", bufs=1, align_bytes=64)
-        for b in reversed(range(I_PASSES)):
-            weigh_vector(last, b, b + 1, USERS)
-        for b in reversed(range(I_PASSES)):
-            quantize(last, h2, I_PASSES, b, b + 1)
-        read_out_last(last, list(range(I_PASSES)) + [I_PASSES + b for b in reversed(range(I_PASSES))])
+        step(0)
+        step(1)
+        quantize_w1(0)
+        wide_pass(0, True, False)
+        step(2)
+        wide_pass(2, False, False)
+        step(3)
+        quantize_w1(1)
+        wide_pass(1, False, False)
+        step(4)
+        wide_pass(3, False, True)
+        for c in low:
+            store_scalar(wide_y[c], [c], 0, WIDE, nc.sync)
+        step(5)
+        third = [(bank(SCORE_RING), low), (bank(SCORE_RING + 1), high)]
+        for y, tiles in third:
+            for g in range(3):
+                readout_pair(g, y, tiles, WIDE, g == 0, False)
+        for c in high:
+            store_scalar(wide_y[c], [c], 0, WIDE, nc.sync)
+        step(6)
+        for y, tiles in third:
+            readout_pair(3, y, tiles, WIDE, False, True)
+            store_scalar(y, tiles, WIDE, WIDE + PAIR, nc.sync)
+        step(7)
+        second, first = WIDE + PAIR, WIDE + PAIR + USERS
+        ends = [
+            (bank(SCORE_RING + 2), low, second),
+            (bank(SCORE_RING + 3), high, second),
+            (bank(0), low, first),
+            (bank(1), high, first),
+        ]
+        for g in (0, 1, 2):
+            for y, tiles, lo in ends:
+                readout(g, y, tiles, lo, lo + USERS, USERS, 0, g == 0, False)
+
+        last = len(steps) - 1
+        h2[last] = ring.tile([P, PAIR, PACK], BF16, name="h2_last", bufs=1, align_bytes=64)
+        for lo in (0, USERS):
+            weigh_vector(last, lo, lo + USERS)
+        for lo in (0, USERS):
+            quantize_h2(last, lo, lo + USERS)
+        for y, tiles, lo in ends:
+            readout(3, y, tiles, lo, lo + USERS, USERS, 0, False, True)
+        store_scalar(ends[0][0], low, second, second + USERS, nc.sync)
+        store_vector(ends[1][0], high, second, second + USERS)
+        store_scalar(ends[2][0], low, first, first + USERS, nc.scalar)
+        store_vector(ends[3][0], high, first, first + USERS)

@@ -31,9 +31,11 @@ LIST_ROWS = 16
 USER_SLICE = 512
 PAIR = 2 * USERS
 WIDE = 4 * USERS
-GPSIMD_USERS = 128
+GPSIMD_USERS = {PAIR: 128, WIDE: 288}
 SCORE_RING = 3
 USER_ROWS_AT = 4 * (T + T2)
+TANH_AT = USER_ROWS_AT + 4 * T
+TANH_ROOM = 6144
 
 
 def tile_list_creative_user_readout_kernel(
@@ -154,7 +156,7 @@ def tile_list_creative_user_readout_kernel(
             nc.sync.dma_start(out=bias_t[:], in_=bias.rearrange("(c p) -> p c", p=P))
 
         w1_bf = [keep.tile([P, N, PACK], BF16, name="w1_bf%d" % b, align_bytes=64) for b in range(I_PASSES)]
-        w1_codes = [keep.tile([P, N], U32, name="w1_codes%d" % b, align_bytes=64) for b in range(I_PASSES)]
+        w1_codes = {}
         w1_plane = [keep.tile([P, N], U8, name="w1_plane%d" % b, align_bytes=64) for b in range(I_PASSES)]
 
         def round_w1(b, tiles):
@@ -164,31 +166,35 @@ def tile_list_creative_user_readout_kernel(
                     in_=w1_raw[b][:, :, c * P : (c + 1) * P].rearrange("p t (g i) -> p g t i", i=2),
                 )
 
-        def quantize_w1(b):
+        def quantize_w1(b, at):
+            w1_codes[b] = shared.tile([P, N], U32, name="w1_codes%d" % b, align_bytes=64, offset=at)
             nc.vector.quantize_mx(
                 out=w1_codes[b][:].bitcast(FP8X4), scales=w1_plane[b][:], in_=w1_bf[b][:].rearrange("p n t -> p (n t)")
             )
 
-        steps = [(0, 0), (0, 1), (1, 0), (1, 1), (0, 2), (1, 2), (0, 3), (1, 3)]
-        h_codes = [keep.tile([P, S2], U32, name="h_codes%d" % g, align_bytes=64) for g in range(2 * I_PASSES)]
+        third, fourth = WIDE, WIDE + PAIR
+        steps = [(b, lo, hi) for lo, hi in ((0, WIDE), (third, fourth), (fourth, S2)) for b in range(I_PASSES)]
+        score_banks = [3, 4, 5, 6, 0, 1, 2, 6] + [n % SCORE_RING for n in range(8)]
+        h_codes = {}
         h_plane = [keep.tile([P, S2], U8, name="h_plane%d" % g, align_bytes=64) for g in range(2 * I_PASSES)]
         h1 = [keep.tile([P, S2 * PACK], BF16, name="h1_%d" % b, align_bytes=64) for b in range(I_PASSES)]
 
         def quantised(g, lo, hi):
-            return h_codes[g][:, lo:hi].bitcast(FP8X4), h_plane[g][:, lo:hi]
+            base = max(first for path, first in h_codes if path == g and first <= lo)
+            return h_codes[g, base][:, lo - base : hi - base].bitcast(FP8X4), h_plane[g][:, lo:hi]
 
         def bank(number):
             return psum.tile([P, PASS], F32, name="bank%d" % number)
 
-        h2, tanh_a = {}, {}
+        h2, tanh_g, tanh_v = {}, {}, {}
 
         def scores(s):
-            b, pair = steps[s]
-            tanh_a[s] = ring.tile([P, PAIR, PACK], F32, name="tanh_a", align_bytes=64)
-            for e in range(2):
-                n = 2 * s + e
-                acc = bank(SCORE_RING + n if n < N_TILES else (n - N_TILES) % SCORE_RING)
-                lo = pair * PAIR + e * USERS
+            b, base, end = steps[s]
+            share = GPSIMD_USERS[end - base]
+            tanh_g[s] = shared.tile([P, share, PACK], F32, name="tanh_g%d" % s, align_bytes=64, offset=TANH_AT + TANH_ROOM * s)
+            tanh_v[s] = ring.tile([P, end - base - share, PACK], F32, name="tanh_v", align_bytes=64)
+            for lo in range(base, end, USERS):
+                acc = bank(score_banks.pop(0))
                 for a in range(K_PASSES):
                     for t in range(PACK):
                         slots = slice(b * PASS + t * P, b * PASS + (t + 1) * P)
@@ -202,7 +208,8 @@ def tile_list_creative_user_readout_kernel(
                             stop=(a == K_PASSES - 1 and t == PACK - 1),
                         )
                 woven = acc[:].rearrange("p (t n) -> p n t", t=PACK)
-                tile_users = slice(e * USERS, (e + 1) * USERS)
+                at = lo - base
+                mine = min(max(share - at, 0), USERS)
 
                 def linear():
                     nc.vector.tensor_tensor(
@@ -213,30 +220,38 @@ def tile_list_creative_user_readout_kernel(
                     )
 
                 def saturate():
-                    nc.scalar.activation(out=tanh_a[s][:, tile_users, :], in_=woven, func=ACT.Tanh)
+                    if mine > 0:
+                        nc.scalar.activation(out=tanh_g[s][:, at : at + mine, :], in_=woven[:, 0:mine, :], func=ACT.Tanh)
+                    if mine < USERS:
+                        nc.scalar.activation(
+                            out=tanh_v[s][:, at + mine - share : at + USERS - share, :], in_=woven[:, mine:USERS, :], func=ACT.Tanh
+                        )
 
-                for reader in (linear, saturate) if s >= 2 else (saturate, linear):
+                for reader in (linear, saturate) if s >= 1 else (saturate, linear):
                     reader()
 
-        def weigh_vector(s, lo, hi):
+        def weigh_vector(s, lo, hi, tanh):
             b = steps[s][0]
             nc.vector.tensor_tensor(
-                h2[s][:, lo:hi, :], tanh_a[s][:, lo:hi, :], gb_psum[:, b : b + 1, :].to_broadcast([P, hi - lo, PACK]), MULT
+                h2[s][:, lo:hi, :], tanh, gb_psum[:, b : b + 1, :].to_broadcast([P, hi - lo, PACK]), MULT
             )
 
         def weigh_gpsimd(s, lo, hi):
             b = steps[s][0]
             nc.gpsimd.tensor_tensor(
-                h2[s][:, lo:hi, :], tanh_a[s][:, lo:hi, :], gb_t[:, b : b + 1, :].to_broadcast([P, hi - lo, PACK]), MULT
+                h2[s][:, lo:hi, :], tanh_g[s][:, lo:hi, :], gb_t[:, b : b + 1, :].to_broadcast([P, hi - lo, PACK]), MULT
             )
 
-        def quantize_h1(b, lo, hi):
+        def quantize_h1(s, at):
+            b, lo, hi = steps[s]
+            h_codes[b, lo] = shared.tile([P, hi - lo], U32, name="h1_codes%d" % s, align_bytes=64, offset=at)
             codes, plane = quantised(b, lo, hi)
             nc.vector.quantize_mx(out=codes, scales=plane, in_=h1[b][:, PACK * lo : PACK * hi])
 
         def quantize_h2(s, lo, hi):
-            b, pair = steps[s]
-            codes, plane = quantised(I_PASSES + b, pair * PAIR + lo, pair * PAIR + hi)
+            b, base, end = steps[s]
+            h_codes[I_PASSES + b, base + lo] = keep.tile([P, hi - lo], U32, name="h2_codes%d_%d" % (s, lo), align_bytes=64)
+            codes, plane = quantised(I_PASSES + b, base + lo, base + hi)
             nc.vector.quantize_mx(out=codes, scales=plane, in_=h2[s][:, lo:hi, :].rearrange("p n t -> p (n t)"))
 
         def readout_pair(g, y, tiles, lo, start, stop):
@@ -272,7 +287,7 @@ def tile_list_creative_user_readout_kernel(
 
         def store_scalar(y, tiles, lo, hi, queue):
             width = hi - lo
-            res = ring.tile([P, len(tiles), width], F32, name="res", bufs=4)
+            res = ring.tile([P, len(tiles), width], F32, name="res", bufs=10)
             for place, c in enumerate(tiles):
                 nc.scalar.activation(
                     out=res[:, place, :],
@@ -284,7 +299,7 @@ def tile_list_creative_user_readout_kernel(
 
         def store_vector(y, tiles, lo, hi):
             width = hi - lo
-            res = ring.tile([P, len(tiles), width], F32, name="res", bufs=4)
+            res = ring.tile([P, len(tiles), width], F32, name="res", bufs=10)
             nc.vector.tensor_tensor(
                 res[:],
                 y[:, 0 : len(tiles) * width].rearrange("p (c n) -> p c n", n=width),
@@ -303,55 +318,61 @@ def tile_list_creative_user_readout_kernel(
                     wide_y.append(bank(SCORE_RING + c))
                 readout(g, wide_y[c], [c], 0, WIDE, WIDE, 0, start, stop)
 
-        def step(s):
-            scores(s)
-            if s == 1:
-                round_w1(0, every)
-            elif s in (2, 3):
-                round_w1(1, low if s == 2 else high)
-            if s >= 1:
-                h2[s - 1] = ring.tile([P, PAIR, PACK], BF16, name="h2", bufs=1, align_bytes=64)
-                weigh_gpsimd(s - 1, 0, GPSIMD_USERS)
-                weigh_vector(s - 1, GPSIMD_USERS, PAIR)
-            b, pair = steps[s]
-            if s == 1:
-                quantize_h1(b, 0, WIDE)
-            elif s > 1:
-                quantize_h1(b, pair * PAIR, (pair + 1) * PAIR)
-            if s >= 1:
-                quantize_h2(s - 1, 0, PAIR)
+        def weigh(s):
+            width = steps[s][2] - steps[s][1]
+            share = GPSIMD_USERS[width]
+            h2[s] = ring.tile([P, width, PACK], BF16, name="h2", bufs=1, align_bytes=64)
+            if width == WIDE:
+                weigh_gpsimd(s, 0, USERS)
+                weigh_gpsimd(s, USERS, share)
+            else:
+                weigh_gpsimd(s, 0, share)
+            weigh_vector(s, share, width, tanh_v[s][:])
 
-        step(0)
-        step(1)
-        quantize_w1(0)
-        wide_pass(0, True, False)
-        step(2)
-        wide_pass(2, False, False)
-        step(3)
-        quantize_w1(1)
+        scores(0)
+        round_w1(0, every)
+        weigh(0)
+        quantize_h1(0, TANH_AT)
+        quantize_h2(0, 0, WIDE)
+        quantize_w1(0, TANH_AT + 4 * WIDE)
+        scores(1)
+        round_w1(1, every)
+        scores(2)
+        wide_pass(2, True, False)
+        wide_pass(0, False, False)
+        weigh(1)
+        quantize_h1(1, TANH_AT + TANH_ROOM)
+        quantize_h1(2, TANH_AT + TANH_ROOM + 4 * WIDE)
+        quantize_w1(1, TANH_AT + TANH_ROOM + 4 * WIDE + 4 * PAIR)
+        quantize_h2(1, 0, WIDE)
+
+        def finish(s):
+            weigh(s - 1)
+            quantize_h1(s, TANH_AT + TANH_ROOM * (s - 1))
+            quantize_h2(s - 1, 0, PAIR)
+
+        scores(3)
+        finish(3)
+        scores(4)
         wide_pass(1, False, False)
-        step(4)
         wide_pass(3, False, True)
-        for c in low:
+        for c in every:
             store_scalar(wide_y[c], [c], 0, WIDE, nc.sync)
-        step(5)
-        third = [(bank(SCORE_RING), low), (bank(SCORE_RING + 1), high)]
-        for y, tiles in third:
-            for g in range(3):
-                readout_pair(g, y, tiles, WIDE, g == 0, False)
-        for c in high:
-            store_scalar(wide_y[c], [c], 0, WIDE, nc.sync)
-        step(6)
-        for y, tiles in third:
-            readout_pair(3, y, tiles, WIDE, False, True)
-            store_scalar(y, tiles, WIDE, WIDE + PAIR, nc.sync)
-        step(7)
+        finish(4)
+        scores(5)
+        halves = [(bank(SCORE_RING), low), (bank(SCORE_RING + 1), high)]
+        for g in range(4):
+            for y, tiles in halves:
+                readout_pair(g, y, tiles, third, g == 0, g == 3)
+        for y, tiles in halves:
+            store_scalar(y, tiles, third, fourth, nc.sync)
+        finish(5)
         second, first = WIDE + PAIR, WIDE + PAIR + USERS
         ends = [
             (bank(SCORE_RING + 2), low, second),
             (bank(SCORE_RING + 3), high, second),
-            (bank(0), low, first),
-            (bank(1), high, first),
+            (bank(2), low, first),
+            (bank(0), high, first),
         ]
         for g in (0, 1, 2):
             for y, tiles, lo in ends:
@@ -359,8 +380,8 @@ def tile_list_creative_user_readout_kernel(
 
         last = len(steps) - 1
         h2[last] = ring.tile([P, PAIR, PACK], BF16, name="h2_last", bufs=1, align_bytes=64)
-        for lo in (0, USERS):
-            weigh_vector(last, lo, lo + USERS)
+        weigh_vector(last, 0, USERS, tanh_g[last][:])
+        weigh_vector(last, USERS, PAIR, tanh_v[last][:])
         for lo in (0, USERS):
             quantize_h2(last, lo, lo + USERS)
         for y, tiles, lo in ends:

@@ -172,28 +172,30 @@ def tile_list_creative_user_readout_kernel(
                 out=w1_codes[b][:].bitcast(FP8X4), scales=w1_plane[b][:], in_=w1_bf[b][:].rearrange("p n t -> p (n t)")
             )
 
-        third, fourth = WIDE, WIDE + PAIR
-        steps = [(b, lo, hi) for lo, hi in ((0, WIDE), (third, fourth), (fourth, S2)) for b in range(I_PASSES)]
+        third, fourth, last = WIDE, WIDE + PAIR, S2 - USERS
+        steps = [[(0, lo) for lo in range(0, WIDE, USERS)]]
+        steps.extend([(b, first), (b, first + USERS)] for b, first in ((1, 0), (1, PAIR), (0, third), (1, third)))
+        steps.extend([(b, lo) for b in range(I_PASSES)] for lo in (fourth, last))
         score_banks = [3, 4, 5, 6, 0, 1, 2, 6] + [n % SCORE_RING for n in range(8)]
-        h_codes = {}
-        h_plane = [keep.tile([P, S2], U8, name="h_plane%d" % g, align_bytes=64) for g in range(2 * I_PASSES)]
-        h1 = [keep.tile([P, S2 * PACK], BF16, name="h1_%d" % b, align_bytes=64) for b in range(I_PASSES)]
-
-        def quantised(g, lo, hi):
-            base = max(first for path, first in h_codes if path == g and first <= lo)
-            return h_codes[g, base][:, lo - base : hi - base].bitcast(FP8X4), h_plane[g][:, lo:hi]
 
         def bank(number):
             return psum.tile([P, PASS], F32, name="bank%d" % number)
 
-        h2, tanh_g, tanh_v = {}, {}, {}
+        h1, h2, tanh_g, tanh_v, quantised = {}, {}, {}, {}, {}
+        h1_wide = []
 
         def scores(s):
-            b, base, end = steps[s]
-            share = GPSIMD_USERS[end - base]
+            width = USERS * len(steps[s])
+            share = GPSIMD_USERS[width]
+            if s == 1:
+                h1_wide.append(keep.tile([P, WIDE, PACK], BF16, name="h1_wide", align_bytes=64))
+            if s in (1, 2):
+                h1[s] = h1_wide[0][:, (s - 1) * PAIR : s * PAIR, :]
+            else:
+                h1[s] = keep.tile([P, width, PACK], BF16, name="h1_%d" % s, align_bytes=64)[:]
             tanh_g[s] = shared.tile([P, share, PACK], F32, name="tanh_g%d" % s, align_bytes=64, offset=TANH_AT + TANH_ROOM * s)
-            tanh_v[s] = ring.tile([P, end - base - share, PACK], F32, name="tanh_v", align_bytes=64)
-            for lo in range(base, end, USERS):
+            tanh_v[s] = ring.tile([P, width - share, PACK], F32, name="tanh_v", align_bytes=64)
+            for e, (b, lo) in enumerate(steps[s]):
                 acc = bank(score_banks.pop(0))
                 for a in range(K_PASSES):
                     for t in range(PACK):
@@ -208,15 +210,12 @@ def tile_list_creative_user_readout_kernel(
                             stop=(a == K_PASSES - 1 and t == PACK - 1),
                         )
                 woven = acc[:].rearrange("p (t n) -> p n t", t=PACK)
-                at = lo - base
+                at = e * USERS
                 mine = min(max(share - at, 0), USERS)
 
                 def linear():
                     nc.vector.tensor_tensor(
-                        h1[b][:, PACK * lo : PACK * (lo + USERS)].rearrange("p (n t) -> p n t", t=PACK),
-                        woven,
-                        ga_t[:, b : b + 1, :].to_broadcast([P, USERS, PACK]),
-                        MULT,
+                        h1[s][:, at : at + USERS, :], woven, ga_t[:, b : b + 1, :].to_broadcast([P, USERS, PACK]), MULT
                     )
 
                 def saturate():
@@ -231,40 +230,44 @@ def tile_list_creative_user_readout_kernel(
                     reader()
 
         def weigh_vector(s, lo, hi, tanh):
-            b = steps[s][0]
+            b = steps[s][lo // USERS][0]
             nc.vector.tensor_tensor(
                 h2[s][:, lo:hi, :], tanh, gb_psum[:, b : b + 1, :].to_broadcast([P, hi - lo, PACK]), MULT
             )
 
         def weigh_gpsimd(s, lo, hi):
-            b = steps[s][0]
+            b = steps[s][lo // USERS][0]
             nc.gpsimd.tensor_tensor(
                 h2[s][:, lo:hi, :], tanh_g[s][:, lo:hi, :], gb_t[:, b : b + 1, :].to_broadcast([P, hi - lo, PACK]), MULT
             )
 
-        def quantize_h1(s, at):
-            b, lo, hi = steps[s]
-            h_codes[b, lo] = shared.tile([P, hi - lo], U32, name="h1_codes%d" % s, align_bytes=64, offset=at)
-            codes, plane = quantised(b, lo, hi)
-            nc.vector.quantize_mx(out=codes, scales=plane, in_=h1[b][:, PACK * lo : PACK * hi])
+        def quantize(h, codes, plane, column, g0, banks):
+            width = USERS * len(banks)
+            nc.vector.quantize_mx(
+                out=codes[:, column : column + width].bitcast(FP8X4),
+                scales=plane[:, column : column + width],
+                in_=h.rearrange("p n t -> p (n t)"),
+            )
+            for e, (b, first) in enumerate(banks):
+                quantised[g0 + b, first] = (codes, plane, column + e * USERS)
+
+        def quantize_h1(h, banks, at):
+            width = USERS * len(banks)
+            name = "%d_%d" % banks[0]
+            codes = shared.tile([P, width], U32, name="h1_codes" + name, align_bytes=64, offset=at)
+            plane = keep.tile([P, width], U8, name="h1_plane" + name, align_bytes=64)
+            quantize(h, codes, plane, 0, 0, banks)
+
+        h2_codes = keep.tile([P, I_PASSES * S2], U32, name="h2_codes", align_bytes=64)
+        h2_plane = keep.tile([P, I_PASSES * S2], U8, name="h2_plane", align_bytes=64)
 
         def quantize_h2(s, lo, hi):
-            b, base, end = steps[s]
-            h_codes[I_PASSES + b, base + lo] = keep.tile([P, hi - lo], U32, name="h2_codes%d_%d" % (s, lo), align_bytes=64)
-            codes, plane = quantised(I_PASSES + b, base + lo, base + hi)
-            nc.vector.quantize_mx(out=codes, scales=plane, in_=h2[s][:, lo:hi, :].rearrange("p n t -> p (n t)"))
+            column = USERS * sum(len(banks) for banks in steps[:s]) + lo
+            quantize(h2[s][:, lo:hi, :], h2_codes, h2_plane, column, I_PASSES, steps[s][lo // USERS : hi // USERS])
 
-        def readout_pair(g, y, tiles, lo, start, stop):
-            if g < I_PASSES:
-                readout(g, y, tiles, lo, lo + PAIR, PAIR, 0, start, stop)
-            else:
-                readout(g, y, tiles, lo, lo + USERS, PAIR, 0, start, False)
-                readout(g, y, tiles, lo + USERS, lo + PAIR, PAIR, USERS, False, stop)
-
-        def readout(g, y, tiles, lo, hi, pitch, at, start, stop):
+        def readout(g, y, tiles, lo, width, pitch, at, start, stop):
             b = g % I_PASSES
-            codes, plane = quantised(g, lo, hi)
-            width = hi - lo
+            codes, plane, column = quantised[g, lo]
             for c in tiles:
                 if g < I_PASSES:
                     w = w1_codes[b][:, c * P : (c + 1) * P].bitcast(FP8X4)
@@ -272,16 +275,23 @@ def tile_list_creative_user_readout_kernel(
                 else:
                     w = w4_codes[:, b, :].bitcast(U8)[:, 2 * c * P : 2 * (c + 1) * P].bitcast(FP4X4)
                     w_scale = w4_planes[:, b, :].bitcast(U8)[:, c * P : (c + 1) * P]
-                place = c - tiles[0]
+                place = (c - tiles[0]) * pitch + at
                 nc.tensor.matmul_mx(
-                    out=y[:, place * pitch + at : place * pitch + at + width],
+                    out=y[:, place : place + width],
                     lhsT=w,
                     lhsT_scale=w_scale,
-                    rhs=codes,
-                    rhs_scale=plane,
+                    rhs=codes[:, column : column + width].bitcast(FP8X4),
+                    rhs_scale=plane[:, column : column + width],
                     start=(start and c == tiles[0]),
                     stop=(stop and c == tiles[-1]),
                 )
+
+        def readout_pair(g, y, tiles, lo, start, stop):
+            if g < I_PASSES:
+                readout(g, y, tiles, lo, PAIR, PAIR, 0, start, stop)
+            else:
+                readout(g, y, tiles, lo, USERS, PAIR, 0, start, False)
+                readout(g, y, tiles, lo + USERS, USERS, PAIR, USERS, False, stop)
 
         out_tiles = out.rearrange("(c p) j -> p c j", p=P)
 
@@ -319,74 +329,72 @@ def tile_list_creative_user_readout_kernel(
                 readout(g, wide_y[c], [c], 0, WIDE, WIDE, 0, start, stop)
 
         def weigh(s):
-            width = steps[s][2] - steps[s][1]
+            width = USERS * len(steps[s])
             share = GPSIMD_USERS[width]
             h2[s] = ring.tile([P, width, PACK], BF16, name="h2", bufs=1, align_bytes=64)
-            if width == WIDE:
-                weigh_gpsimd(s, 0, USERS)
+            weigh_gpsimd(s, 0, USERS)
+            if share > USERS:
                 weigh_gpsimd(s, USERS, share)
-            else:
-                weigh_gpsimd(s, 0, share)
             weigh_vector(s, share, width, tanh_v[s][:])
+
+        def room(s):
+            return TANH_AT + TANH_ROOM * s
+
+        def finish(s):
+            weigh(s - 1)
+            quantize_h1(h1[s], steps[s], room(s - 1))
+            quantize_h2(s - 1, 0, PAIR)
 
         scores(0)
         round_w1(0, every)
         weigh(0)
-        quantize_h1(0, TANH_AT)
+        quantize_h1(h1[0], steps[0], room(0))
         quantize_h2(0, 0, WIDE)
-        quantize_w1(0, TANH_AT + 4 * WIDE)
+        quantize_w1(0, room(0) + 4 * WIDE)
         scores(1)
-        round_w1(1, every)
         scores(2)
+        round_w1(1, every)
+        weigh(1)
+        quantize_h1(h1_wide[0][:], steps[1] + steps[2], room(1) - 2 * WIDE)
+        quantize_w1(1, room(1) + 2 * WIDE)
+        quantize_h2(1, 0, PAIR)
+        scores(3)
         wide_pass(2, True, False)
         wide_pass(0, False, False)
-        weigh(1)
-        quantize_h1(1, TANH_AT + TANH_ROOM)
-        quantize_h1(2, TANH_AT + TANH_ROOM + 4 * WIDE)
-        quantize_w1(1, TANH_AT + TANH_ROOM + 4 * WIDE + 4 * PAIR)
-        quantize_h2(1, 0, WIDE)
-
-        def finish(s):
-            weigh(s - 1)
-            quantize_h1(s, TANH_AT + TANH_ROOM * (s - 1))
-            quantize_h2(s - 1, 0, PAIR)
-
-        scores(3)
         finish(3)
         scores(4)
         wide_pass(1, False, False)
+        finish(4)
+        scores(5)
         wide_pass(3, False, True)
         for c in every:
             store_scalar(wide_y[c], [c], 0, WIDE, nc.sync)
-        finish(4)
-        scores(5)
+        finish(5)
+        scores(6)
         halves = [(bank(SCORE_RING), low), (bank(SCORE_RING + 1), high)]
         for g in range(4):
             for y, tiles in halves:
                 readout_pair(g, y, tiles, third, g == 0, g == 3)
         for y, tiles in halves:
             store_scalar(y, tiles, third, fourth, nc.sync)
-        finish(5)
-        second, first = WIDE + PAIR, WIDE + PAIR + USERS
-        ends = [
-            (bank(SCORE_RING + 2), low, second),
-            (bank(SCORE_RING + 3), high, second),
-            (bank(2), low, first),
-            (bank(0), high, first),
-        ]
-        for g in (0, 1, 2):
-            for y, tiles, lo in ends:
-                readout(g, y, tiles, lo, lo + USERS, USERS, 0, g == 0, False)
+        finish(6)
+        y = bank(SCORE_RING + 2)
+        for g in range(4):
+            readout(g, y, every, fourth, USERS, USERS, 0, g == 0, g == 3)
+        store_scalar(y, every, fourth, last, nc.sync)
+        ends = [(bank(SCORE_RING + 3), low), (bank(2), high)]
+        for g in range(I_PASSES):
+            for y, tiles in ends:
+                readout(g, y, tiles, last, USERS, USERS, 0, g == 0, False)
 
-        last = len(steps) - 1
-        h2[last] = ring.tile([P, PAIR, PACK], BF16, name="h2_last", bufs=1, align_bytes=64)
-        weigh_vector(last, 0, USERS, tanh_g[last][:])
-        weigh_vector(last, USERS, PAIR, tanh_v[last][:])
-        for lo in (0, USERS):
-            quantize_h2(last, lo, lo + USERS)
-        for y, tiles, lo in ends:
-            readout(3, y, tiles, lo, lo + USERS, USERS, 0, False, True)
-        store_scalar(ends[0][0], low, second, second + USERS, nc.sync)
-        store_vector(ends[1][0], high, second, second + USERS)
-        store_scalar(ends[2][0], low, first, first + USERS, nc.scalar)
-        store_vector(ends[3][0], high, first, first + USERS)
+        s = len(steps) - 1
+        h2[s] = ring.tile([P, PAIR, PACK], BF16, name="h2_last", bufs=1, align_bytes=64)
+        weigh_vector(s, 0, USERS, tanh_g[s][:])
+        weigh_vector(s, USERS, PAIR, tanh_v[s][:])
+        for b in range(I_PASSES):
+            quantize_h2(s, b * USERS, (b + 1) * USERS)
+        for b in range(I_PASSES):
+            for y, tiles in ends:
+                readout(I_PASSES + b, y, tiles, last, USERS, USERS, 0, False, b == I_PASSES - 1)
+        store_scalar(ends[0][0], low, last, S2, nc.scalar)
+        store_vector(ends[1][0], high, last, S2)

@@ -31,7 +31,7 @@ LIST_ROWS = 16
 USER_SLICE = 512
 PAIR = 2 * USERS
 WIDE = 4 * USERS
-GPSIMD_USERS = {PAIR: 128, WIDE: 288}
+GPSIMD_USERS = [288, 128, 128, 128, 128, 128, 48]
 SCORE_RING = 3
 USER_ROWS_AT = 4 * (T + T2)
 TANH_AT = USER_ROWS_AT + 4 * T
@@ -184,50 +184,63 @@ def tile_list_creative_user_readout_kernel(
         h1, h2, tanh_g, tanh_v, quantised = {}, {}, {}, {}, {}
         h1_wide = []
 
-        def scores(s):
+        def open_step(s):
             width = USERS * len(steps[s])
-            share = GPSIMD_USERS[width]
+            share = GPSIMD_USERS[s]
             if s == 1:
-                h1_wide.append(keep.tile([P, WIDE, PACK], BF16, name="h1_wide", align_bytes=64))
+                h1_wide.append(keep.tile([P, WIDE, PACK], BF16, name="h_2", align_bytes=64))
             if s in (1, 2):
                 h1[s] = h1_wide[0][:, (s - 1) * PAIR : s * PAIR, :]
             else:
-                h1[s] = keep.tile([P, width, PACK], BF16, name="h1_%d" % s, align_bytes=64)[:]
+                h1[s] = keep.tile([P, width, PACK], BF16, name="h_%d" % s, align_bytes=64)[:]
             tanh_g[s] = shared.tile([P, share, PACK], F32, name="tanh_g%d" % s, align_bytes=64, offset=TANH_AT + TANH_ROOM * s)
-            tanh_v[s] = ring.tile([P, width - share, PACK], F32, name="tanh_v", align_bytes=64)
-            for e, (b, lo) in enumerate(steps[s]):
-                acc = bank(score_banks.pop(0))
-                for a in range(K_PASSES):
-                    for t in range(PACK):
-                        slots = slice(b * PASS + t * P, b * PASS + (t + 1) * P)
-                        nc.tensor.matmul_mx(
-                            out=acc[:, t * USERS : (t + 1) * USERS],
-                            lhsT=creative_words[a][:, slots].bitcast(FP8X4),
-                            lhsT_scale=planes[4 * a :, slots],
-                            rhs=user_words[a][:, lo : lo + USERS].bitcast(FP8X4),
-                            rhs_scale=planes[4 * a :, S + lo : S + lo + USERS],
-                            start=(a == 0 and t == 0),
-                            stop=(a == K_PASSES - 1 and t == PACK - 1),
-                        )
-                woven = acc[:].rearrange("p (t n) -> p n t", t=PACK)
-                at = e * USERS
-                mine = min(max(share - at, 0), USERS)
+            tanh_v[s] = keep.tile([P, width - share, PACK], F32, name="tanh_v%d" % s, align_bytes=64)
 
-                def linear():
-                    nc.vector.tensor_tensor(
-                        h1[s][:, at : at + USERS, :], woven, ga_t[:, b : b + 1, :].to_broadcast([P, USERS, PACK]), MULT
+        places = [(s, e) for s, banks in enumerate(steps) for e in range(len(banks))]
+        accs = {}
+
+        def multiply(n):
+            s, e = places[n]
+            if e == 0:
+                open_step(s)
+            b, lo = steps[s][e]
+            acc = bank(score_banks[n])
+            accs[n] = acc
+            for a in range(K_PASSES):
+                for t in range(PACK):
+                    slots = slice(b * PASS + t * P, b * PASS + (t + 1) * P)
+                    nc.tensor.matmul_mx(
+                        out=acc[:, t * USERS : (t + 1) * USERS],
+                        lhsT=creative_words[a][:, slots].bitcast(FP8X4),
+                        lhsT_scale=planes[4 * a :, slots],
+                        rhs=user_words[a][:, lo : lo + USERS].bitcast(FP8X4),
+                        rhs_scale=planes[4 * a :, S + lo : S + lo + USERS],
+                        start=(a == 0 and t == 0),
+                        stop=(a == K_PASSES - 1 and t == PACK - 1),
                     )
 
-                def saturate():
-                    if mine > 0:
-                        nc.scalar.activation(out=tanh_g[s][:, at : at + mine, :], in_=woven[:, 0:mine, :], func=ACT.Tanh)
-                    if mine < USERS:
-                        nc.scalar.activation(
-                            out=tanh_v[s][:, at + mine - share : at + USERS - share, :], in_=woven[:, mine:USERS, :], func=ACT.Tanh
-                        )
+        def linear(n):
+            s, e = places[n]
+            b = steps[s][e][0]
+            nc.vector.tensor_tensor(
+                h1[s][:, e * USERS : (e + 1) * USERS, :],
+                accs[n][:].rearrange("p (t n) -> p n t", t=PACK),
+                ga_t[:, b : b + 1, :].to_broadcast([P, USERS, PACK]),
+                MULT,
+            )
 
-                for reader in (linear, saturate) if s >= 1 else (saturate, linear):
-                    reader()
+        def saturate(n):
+            s, e = places[n]
+            share = GPSIMD_USERS[s]
+            woven = accs[n][:].rearrange("p (t n) -> p n t", t=PACK)
+            at = e * USERS
+            mine = min(max(share - at, 0), USERS)
+            if mine > 0:
+                nc.scalar.activation(out=tanh_g[s][:, at : at + mine, :], in_=woven[:, 0:mine, :], func=ACT.Tanh)
+            if mine < USERS:
+                nc.scalar.activation(
+                    out=tanh_v[s][:, at + mine - share : at + USERS - share, :], in_=woven[:, mine:USERS, :], func=ACT.Tanh
+                )
 
         def weigh_vector(s, lo, hi, tanh):
             b = steps[s][lo // USERS][0]
@@ -258,12 +271,17 @@ def tile_list_creative_user_readout_kernel(
             plane = keep.tile([P, width], U8, name="h1_plane" + name, align_bytes=64)
             quantize(h, codes, plane, 0, 0, banks)
 
-        h2_codes = keep.tile([P, I_PASSES * S2], U32, name="h2_codes", align_bytes=64)
-        h2_plane = keep.tile([P, I_PASSES * S2], U8, name="h2_plane", align_bytes=64)
+        wide_codes = keep.tile([P, WIDE], U32, name="wide_codes", align_bytes=64)
+        wide_plane = keep.tile([P, WIDE], U8, name="wide_plane", align_bytes=64)
 
         def quantize_h2(s, lo, hi):
-            column = USERS * sum(len(banks) for banks in steps[:s]) + lo
-            quantize(h2[s][:, lo:hi, :], h2_codes, h2_plane, column, I_PASSES, steps[s][lo // USERS : hi // USERS])
+            banks = steps[s][lo // USERS : hi // USERS]
+            if s in (1, 2):
+                quantize(h2[s][:, lo:hi, :], wide_codes, wide_plane, (s - 1) * PAIR, I_PASSES, banks)
+            else:
+                codes = keep.tile([P, hi - lo], U32, name="h2_codes%d_%d" % (s, lo), align_bytes=64)
+                plane = keep.tile([P, hi - lo], U8, name="h2_plane%d_%d" % (s, lo), align_bytes=64)
+                quantize(h2[s][:, lo:hi, :], codes, plane, 0, I_PASSES, banks)
 
         def readout(g, y, tiles, lo, width, pitch, at, start, stop):
             b = g % I_PASSES
@@ -297,7 +315,7 @@ def tile_list_creative_user_readout_kernel(
 
         def store_scalar(y, tiles, lo, hi, queue):
             width = hi - lo
-            res = ring.tile([P, len(tiles), width], F32, name="res", bufs=10)
+            res = ring.tile([P, len(tiles), width], F32, name="res", bufs=11)
             for place, c in enumerate(tiles):
                 nc.scalar.activation(
                     out=res[:, place, :],
@@ -309,7 +327,7 @@ def tile_list_creative_user_readout_kernel(
 
         def store_vector(y, tiles, lo, hi):
             width = hi - lo
-            res = ring.tile([P, len(tiles), width], F32, name="res", bufs=10)
+            res = ring.tile([P, len(tiles), width], F32, name="res", bufs=11)
             nc.vector.tensor_tensor(
                 res[:],
                 y[:, 0 : len(tiles) * width].rearrange("p (c n) -> p c n", n=width),
@@ -320,18 +338,23 @@ def tile_list_creative_user_readout_kernel(
 
         every = list(range(N_TILES))
         low, high = every[:2], every[2:]
-        wide_y = []
 
-        def wide_pass(g, start, stop):
-            for c in every:
-                if start:
-                    wide_y.append(bank(SCORE_RING + c))
-                readout(g, wide_y[c], [c], 0, WIDE, WIDE, 0, start, stop)
+        def open_pair(number):
+            return [(bank(number), low), (bank(number + 1), high)]
+
+        def pair_passes(halves, lo, passes, start, stop):
+            for g in passes:
+                for y, tiles in halves:
+                    readout_pair(g, y, tiles, lo, start and g == passes[0], stop and g == passes[-1])
+
+        def store_pair(halves, lo):
+            for y, tiles in halves:
+                store_scalar(y, tiles, lo, lo + PAIR, nc.sync)
 
         def weigh(s):
             width = USERS * len(steps[s])
-            share = GPSIMD_USERS[width]
-            h2[s] = ring.tile([P, width, PACK], BF16, name="h2", bufs=1, align_bytes=64)
+            share = GPSIMD_USERS[s]
+            h2[s] = keep.tile([P, width, PACK], BF16, name=("h_%d" if s >= 2 else "h2_%d") % s, align_bytes=64)
             weigh_gpsimd(s, 0, USERS)
             if share > USERS:
                 weigh_gpsimd(s, USERS, share)
@@ -345,52 +368,99 @@ def tile_list_creative_user_readout_kernel(
             quantize_h1(h1[s], steps[s], room(s - 1))
             quantize_h2(s - 1, 0, PAIR)
 
-        scores(0)
+        for n in range(4):
+            multiply(n)
+        for n in range(4):
+            saturate(n)
+            linear(n)
+        for n in range(4, 8):
+            multiply(n)
         round_w1(0, every)
         weigh(0)
         quantize_h1(h1[0], steps[0], room(0))
         quantize_h2(0, 0, WIDE)
         quantize_w1(0, room(0) + 4 * WIDE)
-        scores(1)
-        scores(2)
-        round_w1(1, every)
-        weigh(1)
-        quantize_h1(h1_wide[0][:], steps[1] + steps[2], room(1) - 2 * WIDE)
-        quantize_w1(1, room(1) + 2 * WIDE)
-        quantize_h2(1, 0, PAIR)
-        scores(3)
-        wide_pass(2, True, False)
-        wide_pass(0, False, False)
-        finish(3)
-        scores(4)
-        wide_pass(1, False, False)
-        finish(4)
-        scores(5)
-        wide_pass(3, False, True)
-        for c in every:
+        wide_y = {}
+
+        def wide_passes(passes, tiles, start, stop):
+            for g in passes:
+                for c in tiles:
+                    if start and g == passes[0]:
+                        wide_y[c] = bank(SCORE_RING + c)
+                    readout(g, wide_y[c], [c], 0, WIDE, WIDE, 0, start and g == passes[0], stop and g == passes[-1])
+
+        def store_wide(c):
             store_scalar(wide_y[c], [c], 0, WIDE, nc.sync)
+
+        wide_passes([2, 0], every[:3], True, False)
+        for n in range(4, 7):
+            linear(n)
+            saturate(n)
+            multiply(n + 4)
+        linear(7)
+        saturate(7)
+        round_w1(1, every)
+        wide_passes([2, 0], every[3:], True, False)
+        weigh(1)
+        quantize_w1(1, room(1) + 2 * WIDE)
+        quantize_h1(h1_wide[0][:], steps[1] + steps[2], room(1) - 2 * WIDE)
+        quantize_h2(1, 0, PAIR)
+        wide_passes([1], every, False, False)
+        saturate(8)
+        saturate(10)
+        linear(8)
+        multiply(11)
+        linear(9)
+        saturate(9)
+        multiply(12)
+        finish(3)
+        wide_passes([3], every, False, True)
+        saturate(12)
+        for c in low:
+            store_wide(c)
+        linear(10)
+        multiply(13)
+        linear(11)
+        saturate(11)
+        third_pair = open_pair(SCORE_RING)
+        pair_passes(third_pair, third, [0], True, False)
+        multiply(14)
+        finish(4)
+        store_wide(2)
+        linear(12)
+        pair_passes(third_pair, third, [1], False, False)
+        multiply(15)
+        linear(13)
+        saturate(13)
+        saturate(14)
+        store_wide(3)
+        pair_passes(third_pair, third, [2], False, False)
         finish(5)
-        scores(6)
-        halves = [(bank(SCORE_RING), low), (bank(SCORE_RING + 1), high)]
-        for g in range(4):
-            for y, tiles in halves:
-                readout_pair(g, y, tiles, third, g == 0, g == 3)
-        for y, tiles in halves:
-            store_scalar(y, tiles, third, fourth, nc.sync)
-        finish(6)
         y = bank(SCORE_RING + 2)
-        for g in range(4):
-            readout(g, y, every, fourth, USERS, USERS, 0, g == 0, g == 3)
-        store_scalar(y, every, fourth, last, nc.sync)
-        ends = [(bank(SCORE_RING + 3), low), (bank(2), high)]
         for g in range(I_PASSES):
-            for y, tiles in ends:
-                readout(g, y, tiles, last, USERS, USERS, 0, g == 0, False)
+            readout(g, y, every, fourth, USERS, USERS, 0, g == 0, False)
+        pair_passes(third_pair, third, [3], False, True)
+        linear(14)
+        linear(15)
+        saturate(15)
+        store_pair(third_pair, third)
+        finish(6)
+        ends = [(bank(SCORE_RING + 3), low), (bank(2), high)]
+        for end, tiles in ends:
+            readout(0, end, tiles, last, USERS, USERS, 0, True, False)
+        for g in range(I_PASSES, 2 * I_PASSES):
+            readout(g, y, every, fourth, USERS, USERS, 0, False, g == 3)
+        for end, tiles in ends:
+            readout(1, end, tiles, last, USERS, USERS, 0, False, False)
+        store_scalar(y, low, fourth, last, nc.sync)
+        store_scalar(y[:, PAIR:PASS], high, fourth, last, nc.sync)
 
         s = len(steps) - 1
-        h2[s] = ring.tile([P, PAIR, PACK], BF16, name="h2_last", bufs=1, align_bytes=64)
-        weigh_vector(s, 0, USERS, tanh_g[s][:])
-        weigh_vector(s, USERS, PAIR, tanh_v[s][:])
+        share = GPSIMD_USERS[s]
+        h2[s] = keep.tile([P, PAIR, PACK], BF16, name="h_%d" % s, align_bytes=64)
+        weigh_gpsimd(s, 0, share)
+        weigh_vector(s, share, USERS, tanh_v[s][:, 0 : USERS - share, :])
+        weigh_vector(s, USERS, PAIR, tanh_v[s][:, USERS - share : PAIR - share, :])
         for b in range(I_PASSES):
             quantize_h2(s, b * USERS, (b + 1) * USERS)
         for b in range(I_PASSES):

@@ -31,7 +31,7 @@ LIST_ROWS = 16
 USER_SLICE = 512
 PAIR = 2 * USERS
 WIDE = 4 * USERS
-GPSIMD_USERS = [288, 128, 128, 128, 128, 128, 48]
+GPSIMD_USERS = [288, 128, 80, 128, 128, 128, 48]
 SCORE_RING = 3
 USER_ROWS_AT = 4 * (T + T2)
 TANH_AT = USER_ROWS_AT + 4 * T
@@ -229,6 +229,19 @@ def tile_list_creative_user_readout_kernel(
                 MULT,
             )
 
+        def linear_scalar(n):
+            s, e = places[n]
+            b = steps[s][e][0]
+            apart = keep.tile([P, PACK, USERS], BF16, name="apart", align_bytes=64)
+            for t in range(PACK):
+                nc.scalar.activation(
+                    out=apart[:, t, :], in_=accs[n][:, t * USERS : (t + 1) * USERS], func=ACT.Copy, scale=ga_t[:, b, t : t + 1]
+                )
+            nc.scalar.copy(
+                out=h1[s][:, e * USERS : (e + 1) * USERS, :].rearrange("p (g i) t -> p g t i", i=2),
+                in_=apart[:].rearrange("p t (g i) -> p g t i", i=2),
+            )
+
         def saturate(n):
             s, e = places[n]
             share = GPSIMD_USERS[s]
@@ -355,7 +368,7 @@ def tile_list_creative_user_readout_kernel(
             width = USERS * len(steps[s])
             share = GPSIMD_USERS[s]
             h2[s] = keep.tile([P, width, PACK], BF16, name=("h_%d" if s >= 2 else "h2_%d") % s, align_bytes=64)
-            weigh_gpsimd(s, 0, USERS)
+            weigh_gpsimd(s, 0, min(share, USERS))
             if share > USERS:
                 weigh_gpsimd(s, USERS, share)
             weigh_vector(s, share, width, tanh_v[s][:])
@@ -407,9 +420,9 @@ def tile_list_creative_user_readout_kernel(
         quantize_h2(1, 0, PAIR)
         wide_passes([1], every, False, False)
         saturate(8)
-        saturate(10)
-        linear(8)
+        linear_scalar(8)
         multiply(11)
+        saturate(10)
         linear(9)
         saturate(9)
         multiply(12)

@@ -31,11 +31,9 @@ LIST_ROWS = 16
 USER_SLICE = 512
 PAIR = 2 * USERS
 WIDE = 4 * USERS
-GPSIMD_USERS = [288, 128, 80, 128, 128, 128, 48]
-SCORE_RING = 3
-USER_ROWS_AT = 4 * (T + T2)
-TANH_AT = USER_ROWS_AT + 4 * T
-TANH_ROOM = 6144
+FIRST_LOAD, SECOND_LOAD = 768, 1152
+GPSIMD_USERS = [472, 256, 240, 96]
+KB = 1024
 
 
 def tile_list_creative_user_readout_kernel(
@@ -45,26 +43,22 @@ def tile_list_creative_user_readout_kernel(
     with ExitStack() as ctx:
         keep = ctx.enter_context(tc.tile_pool(name="keep", bufs=1))
         shared = ctx.enter_context(tc.tile_pool(name="shared", bufs=1))
-        ring = ctx.enter_context(tc.tile_pool(name="ring", bufs=3))
         psum = ctx.enter_context(tc.psum_pool(name="psum", bufs=1))
 
         idx = keep.tile([P, S // LIST_ROWS], U16, name="idx")
         idx2 = keep.tile([P, S2 // LIST_ROWS], U16, name="idx2")
-        v_words = [
-            shared.tile([P, T], I32, name="v_words0", align_bytes=64, offset=0),
-            shared.tile([P, T], I32, name="v_words1", align_bytes=64, offset=USER_ROWS_AT),
-        ]
-        v2_words = [
-            shared.tile([P, T2], I32, name="v2_words0", align_bytes=64, offset=4 * T),
-            keep.tile([P, T2], I32, name="v2_words1", align_bytes=64),
-        ]
+        v_words = [keep.tile([P, T], I32, name="v_words%d" % a, align_bytes=64) for a in range(K_PASSES)]
+        v2_words = [keep.tile([P, T2], I32, name="v2_words%d" % a, align_bytes=64) for a in range(K_PASSES)]
         v_rows = keep.tile([P, T // 4], I32, name="v_rows", align_bytes=64)
         v2_rows = keep.tile([P, T2 // 4], I32, name="v2_rows", align_bytes=64)
         g_rows = keep.tile([P, PASS], F32, name="g_rows")
+        late_planes = keep.tile([P, (S + S2) // 4], I32, name="late_planes", align_bytes=64)
+        w4_planes = keep.tile([P, I_PASSES, N // 4], I32, name="w4_planes", align_bytes=64)
 
         nc.vector.memset(v_rows[:], 0)
         nc.vector.memset(v2_rows[:], 0)
         nc.vector.memset(g_rows[:], 0.0)
+        nc.vector.memset(w4_planes[:], 0)
 
         def load_words(tile, words, lo, hi):
             nc.sync.dma_start(out=tile[:, lo:hi], in_=words[:, lo:hi, :].rearrange("p n t -> p (n t)").bitcast(I32))
@@ -72,50 +66,53 @@ def tile_list_creative_user_readout_kernel(
         def load_rows(tile, scales):
             nc.sync.dma_start(out=tile[0:P:4, :], in_=scales.rearrange("a q n -> q a n").bitcast(I32))
 
-        load_words(v_words[0], tab_words[0], 0, T // 4)
-        load_rows(v_rows, tab_scales)
         nc.sync.dma_start(idx[:], offs)
-        load_words(v_words[0], tab_words[0], T // 4, T)
-        load_rows(v2_rows, tab2_scales)
+        load_words(v2_words[0], tab2_words[0], 0, FIRST_LOAD)
+        load_rows(v_rows, tab_scales)
         nc.sync.dma_start(idx2[:], offs2)
-        load_words(v2_words[0], tab2_words[0], 0, T2)
-        for row, g in ((0, ga), (I_PASSES, gb)):
-            nc.sync.dma_start(out=g_rows[row : row + I_PASSES, :], in_=g.rearrange("(b i) -> b i", b=I_PASSES))
-        load_words(v2_words[1], tab2_words[1], 0, T2)
+        load_words(v2_words[0], tab2_words[0], FIRST_LOAD, SECOND_LOAD)
+        load_rows(v2_rows, tab2_scales)
+        load_words(v2_words[0], tab2_words[0], SECOND_LOAD, T2)
+        load_words(v_words[0], tab_words[0], 0, T)
+        for first, g in ((0, ga), (8, gb)):
+            nc.sync.dma_start(out=g_rows[first : first + 8 : 4, :], in_=g.rearrange("(b i) -> b i", b=I_PASSES))
+        load_words(v_words[1], tab_words[1], 0, T)
 
         ident = keep.tile([P, P], F32, name="ident")
         make_identity(nc, ident[:])
         gb_bank = psum.tile([P, PACK, P], F32, name="gb_bank")
         for t in range(PACK):
             nc.tensor.transpose(gb_bank[:, t, :], g_rows[:, t::PACK], ident[:])
-        gb_psum = gb_bank[:, :, I_PASSES : 2 * I_PASSES].rearrange("p t b -> p b t")
+        gb_psum = gb_bank[:, :, 8:16:4].rearrange("p t b -> p b t")
         g_t = keep.tile([P, 2 * I_PASSES, PACK], F32, name="g_t")
-        nc.scalar.copy(out=g_t[:], in_=gb_bank[:, :, 0 : 2 * I_PASSES].rearrange("p t b -> p b t"))
+        nc.scalar.copy(out=g_t[:], in_=gb_bank[:, :, 0:16:4].rearrange("p t b -> p b t"))
         ga_t = g_t[:, 0:I_PASSES, :]
         gb_t = g_t[:, I_PASSES : 2 * I_PASSES, :]
 
         creative_words = [keep.tile([P, S], U32, name="creative_words%d" % a, align_bytes=64) for a in range(K_PASSES)]
         user_words = [keep.tile([P, S2], U32, name="user_words%d" % a, align_bytes=64) for a in range(K_PASSES)]
         creative_rows = keep.tile([P, S], U8, name="creative_rows", align_bytes=64)
-        user_rows = shared.tile([P, S2], U8, name="user_rows", align_bytes=64, offset=USER_ROWS_AT)
-        planes = keep.tile([P, S + S2], U8, name="planes", align_bytes=64)
-        creative_planes = planes[:, 0:S]
-        user_planes = planes[:, S : S + S2]
+        user_rows = keep.tile([P, S2], U8, name="user_rows", align_bytes=64)
+        early_planes = keep.tile([P, S + S2], U8, name="early_planes", align_bytes=64)
 
         nc.vector.tensor_copy(creative_rows[:], v_rows[:].bitcast(U8).indirect(idx[:]))
         nc.vector.tensor_copy(user_rows[:], v2_rows[:].bitcast(U8).indirect(idx2[:]))
         nc.vector.tensor_copy(
-            creative_planes.rearrange("p (b t m) -> p b t m", b=I_PASSES, t=PACK),
+            early_planes[:, 0:S].rearrange("p (b t m) -> p b t m", b=I_PASSES, t=PACK),
             creative_rows[:].rearrange("p (b m t) -> p b t m", b=I_PASSES, t=PACK),
         )
-        nc.vector.tensor_copy(user_planes.bitcast(I32), user_rows[:].bitcast(I32))
+        nc.vector.tensor_copy(early_planes[:, S : S + S2].bitcast(I32), user_rows[:].bitcast(I32))
+        nc.vector.tensor_copy(late_planes[:], early_planes[:].bitcast(I32))
         for r in range(1, 4):
-            for a in range(K_PASSES):
-                nc.sync.dma_start(
-                    out=planes[4 * a + r : P : QUADRANT, :].bitcast(I32),
-                    in_=planes[4 * a + 8 * r : P : QUADRANT, :].bitcast(I32),
-                )
-        load_words(v_words[1], tab_words[1], 0, T)
+            nc.sync.dma_start(
+                out=early_planes[r:P:QUADRANT, :].bitcast(I32), in_=early_planes[8 * r : P : QUADRANT, :].bitcast(I32)
+            )
+        load_words(v2_words[1], tab2_words[1], 0, T2)
+        for r in range(1, 4):
+            nc.sync.dma_start(
+                out=late_planes[4 + r : P : QUADRANT, :], in_=early_planes[8 * r + 4 : P : QUADRANT, :].bitcast(I32)
+            )
+        planes = [early_planes[:], late_planes[4:, :].bitcast(U8)]
 
         def gather_creatives(a, lo, hi):
             nc.vector.tensor_copy(
@@ -123,87 +120,79 @@ def tile_list_creative_user_readout_kernel(
                 v_words[a][:].bitcast(U32).indirect(idx[:, lo // LIST_ROWS : hi // LIST_ROWS]),
             )
 
-        gather_creatives(0, 0, S)
-        for a in range(K_PASSES):
-            for lo in range(0, S2, USER_SLICE):
-                nc.vector.tensor_copy(
-                    user_words[a][:, lo : lo + USER_SLICE],
-                    v2_words[a][:].bitcast(U32).indirect(idx2[:, lo // LIST_ROWS : (lo + USER_SLICE) // LIST_ROWS]),
-                )
-        for b in range(I_PASSES):
-            gather_creatives(1, b * PASS, (b + 1) * PASS)
+        def gather_users(a, lo):
+            nc.vector.tensor_copy(
+                user_words[a][:, lo : lo + USER_SLICE],
+                v2_words[a][:].bitcast(U32).indirect(idx2[:, lo // LIST_ROWS : (lo + USER_SLICE) // LIST_ROWS]),
+            )
 
-        w1_raw = [
-            shared.tile([P, PACK, N], F32, name="w1_raw%d" % b, align_bytes=64, offset=4 * T * b) for b in range(I_PASSES)
-        ]
-        w4_codes = shared.tile([P, I_PASSES, N // 2], I32, name="w4_codes", align_bytes=64, offset=8 * T)
-        w4_planes = shared.tile([P, I_PASSES, N // 4], I32, name="w4_planes", align_bytes=64, offset=9 * T)
-        bias_t = shared.tile([P, N_TILES], F32, name="bias_t", align_bytes=64, offset=10 * T)
-        nc.vector.memset(w4_planes[:], 0)
+        gather_users(0, 0)
+        gather_users(0, USER_SLICE)
+        gather_creatives(0, 0, S)
+        gather_creatives(1, 0, S)
+        gather_users(1, 0)
+        gather_users(1, USER_SLICE)
+
+        w1_raw = [keep.tile([P, PACK, N], F32, name="w1_raw%d" % b, align_bytes=64) for b in range(I_PASSES)]
+        w4_codes = keep.tile([P, I_PASSES, N // 2], I32, name="w4_codes", align_bytes=64)
+        bias_t = keep.tile([P, N_TILES], F32, name="bias_t", align_bytes=64)
 
         def load_w1(b):
             nc.sync.dma_start(out=w1_raw[b][:], in_=w1[b * PASS : (b + 1) * PASS, :].rearrange("(p t) n -> p t n", t=PACK))
 
         load_w1(0)
-        load_w1(1)
         nc.sync.dma_start(out=w4_codes[:], in_=w4_words.rearrange("b p c -> p b c").bitcast(I32))
         for q in range(P // QUADRANT):
             nc.sync.dma_start(
                 out=w4_planes[QUADRANT * q : QUADRANT * q + 4, :, :],
                 in_=w4_scales[:, 4 * q : 4 * q + 4, :].rearrange("b r c -> r b c").bitcast(I32),
             )
+        load_w1(1)
         with nc.allow_non_contiguous_dma(reason="one bias value for each partition and output tile"):
             nc.sync.dma_start(out=bias_t[:], in_=bias.rearrange("(c p) -> p c", p=P))
 
-        w1_bf = [keep.tile([P, N, PACK], BF16, name="w1_bf%d" % b, align_bytes=64) for b in range(I_PASSES)]
-        w1_codes = {}
-        w1_plane = [keep.tile([P, N], U8, name="w1_plane%d" % b, align_bytes=64) for b in range(I_PASSES)]
-
-        def round_w1(b, tiles):
-            for c in tiles:
-                nc.scalar.copy(
-                    out=w1_bf[b][:, c * P : (c + 1) * P, :].rearrange("p (g i) t -> p g t i", i=2),
-                    in_=w1_raw[b][:, :, c * P : (c + 1) * P].rearrange("p t (g i) -> p g t i", i=2),
-                )
-
-        def quantize_w1(b, at):
-            w1_codes[b] = shared.tile([P, N], U32, name="w1_codes%d" % b, align_bytes=64, offset=at)
-            nc.vector.quantize_mx(
-                out=w1_codes[b][:].bitcast(FP8X4), scales=w1_plane[b][:], in_=w1_bf[b][:].rearrange("p n t -> p (n t)")
-            )
-
         third, fourth, last = WIDE, WIDE + PAIR, S2 - USERS
-        steps = [[(0, lo) for lo in range(0, WIDE, USERS)]]
-        steps.extend([(b, first), (b, first + USERS)] for b, first in ((1, 0), (1, PAIR), (0, third), (1, third)))
-        steps.extend([(b, lo) for b in range(I_PASSES)] for lo in (fourth, last))
-        score_banks = [3, 4, 5, 6, 0, 1, 2, 6] + [n % SCORE_RING for n in range(8)]
+        places = [(b, lo) for b in range(I_PASSES) for lo in range(0, WIDE, USERS)]
+        places.extend((b, lo) for b in range(I_PASSES) for lo in (third, third + USERS))
+        places.extend((b, lo) for lo in (fourth, last) for b in range(I_PASSES))
+        score_banks = list(range(7)) + [n % 4 for n in range(8)] + [1]
+        phases = [range(0, 4), range(4, 8), range(8, 12), range(12, 15), range(15, 16)]
+        phase_of = {n: s for s, members in enumerate(phases) for n in members}
 
         def bank(number):
             return psum.tile([P, PASS], F32, name="bank%d" % number)
 
-        h1, h2, tanh_g, tanh_v, quantised = {}, {}, {}, {}, {}
-        h1_wide = []
+        def half(name, users, at):
+            return shared.tile([P, users, PACK], BF16, name=name, align_bytes=64, offset=at)
 
-        def open_step(s):
-            width = USERS * len(steps[s])
-            share = GPSIMD_USERS[s]
-            if s == 1:
-                h1_wide.append(keep.tile([P, WIDE, PACK], BF16, name="h_2", align_bytes=64))
-            if s in (1, 2):
-                h1[s] = h1_wide[0][:, (s - 1) * PAIR : s * PAIR, :]
-            else:
-                h1[s] = keep.tile([P, width, PACK], BF16, name="h_%d" % s, align_bytes=64)[:]
-            tanh_g[s] = shared.tile([P, share, PACK], F32, name="tanh_g%d" % s, align_bytes=64, offset=TANH_AT + TANH_ROOM * s)
-            tanh_v[s] = keep.tile([P, width - share, PACK], F32, name="tanh_v%d" % s, align_bytes=64)
+        room_a, room_b, room_c, tanh_at = 0, 4 * KB, 8 * KB, 12 * KB
+        tanh = [
+            shared.tile([P, USERS * len(members), PACK], F32, name="tanh%d" % s, align_bytes=64, offset=tanh_at + 8 * KB * s)
+            for s, members in enumerate(phases)
+        ]
+        w1_bf = {
+            (0, 0): half("w1_bf0", N, room_b),
+            (1, 0): half("w1_bf1", N, room_c),
+        }
+        h1_a = keep.tile([P, WIDE, PACK], BF16, name="h1_a", align_bytes=64)
+        h1_b = keep.tile([P, WIDE, PACK], BF16, name="h1_b", align_bytes=64)
+        h1_c = keep.tile([P, WIDE, PACK], BF16, name="h1_c", align_bytes=64)
+        h2_a = keep.tile([P, WIDE, PACK], BF16, name="h2_a", align_bytes=64)
+        h2_b = half("h2_b", WIDE, room_b)
+        h1_d = half("h1_d", PAIR, room_b)
+        h1_14 = half("h1_14", USERS, room_b + 2 * KB)
+        h2_c = half("h2_c", WIDE, room_c)
+        h2_d = half("h2_d", PAIR, room_b + 2 * KB)
+        h2_14 = half("h2_14", USERS, room_c)
+        h1_15 = keep.tile([P, USERS, PACK], BF16, name="h1_15", align_bytes=64)
+        h2_15 = half("h2_15", USERS, room_b + 2 * KB)
+        h1_of = [h1_a] * 4 + [h1_b] * 4 + [h1_c] * 4 + [h1_d] * 2 + [h1_14, h1_15]
+        column_of = [0, 1, 2, 3] * 3 + [0, 1, 0, 0]
 
-        places = [(s, e) for s, banks in enumerate(steps) for e in range(len(banks))]
-        accs = {}
+        accs, quantised = {}, {}
 
         def multiply(n):
-            s, e = places[n]
-            if e == 0:
-                open_step(s)
-            b, lo = steps[s][e]
+            b, lo = places[n]
             acc = bank(score_banks[n])
             accs[n] = acc
             for a in range(K_PASSES):
@@ -212,97 +201,96 @@ def tile_list_creative_user_readout_kernel(
                     nc.tensor.matmul_mx(
                         out=acc[:, t * USERS : (t + 1) * USERS],
                         lhsT=creative_words[a][:, slots].bitcast(FP8X4),
-                        lhsT_scale=planes[4 * a :, slots],
+                        lhsT_scale=planes[a][:, slots],
                         rhs=user_words[a][:, lo : lo + USERS].bitcast(FP8X4),
-                        rhs_scale=planes[4 * a :, S + lo : S + lo + USERS],
+                        rhs_scale=planes[a][:, S + lo : S + lo + USERS],
                         start=(a == 0 and t == 0),
                         stop=(a == K_PASSES - 1 and t == PACK - 1),
                     )
 
         def linear(n):
-            s, e = places[n]
-            b = steps[s][e][0]
+            b = places[n][0]
+            at = column_of[n] * USERS
             nc.vector.tensor_tensor(
-                h1[s][:, e * USERS : (e + 1) * USERS, :],
+                h1_of[n][:, at : at + USERS, :],
                 accs[n][:].rearrange("p (t n) -> p n t", t=PACK),
                 ga_t[:, b : b + 1, :].to_broadcast([P, USERS, PACK]),
                 MULT,
             )
 
         def linear_scalar(n):
-            s, e = places[n]
-            b = steps[s][e][0]
+            b = places[n][0]
             apart = keep.tile([P, PACK, USERS], BF16, name="apart", align_bytes=64)
             for t in range(PACK):
                 nc.scalar.activation(
                     out=apart[:, t, :], in_=accs[n][:, t * USERS : (t + 1) * USERS], func=ACT.Copy, scale=ga_t[:, b, t : t + 1]
                 )
             nc.scalar.copy(
-                out=h1[s][:, e * USERS : (e + 1) * USERS, :].rearrange("p (g i) t -> p g t i", i=2),
-                in_=apart[:].rearrange("p t (g i) -> p g t i", i=2),
+                out=h1_of[n][:].rearrange("p (g i) t -> p g t i", i=2), in_=apart[:].rearrange("p t (g i) -> p g t i", i=2)
             )
 
         def saturate(n):
-            s, e = places[n]
-            share = GPSIMD_USERS[s]
-            woven = accs[n][:].rearrange("p (t n) -> p n t", t=PACK)
-            at = e * USERS
-            mine = min(max(share - at, 0), USERS)
-            if mine > 0:
-                nc.scalar.activation(out=tanh_g[s][:, at : at + mine, :], in_=woven[:, 0:mine, :], func=ACT.Tanh)
-            if mine < USERS:
-                nc.scalar.activation(
-                    out=tanh_v[s][:, at + mine - share : at + USERS - share, :], in_=woven[:, mine:USERS, :], func=ACT.Tanh
+            s = phase_of[n]
+            at = (n - phases[s][0]) * USERS
+            nc.scalar.activation(
+                out=tanh[s][:, at : at + USERS, :], in_=accs[n][:].rearrange("p (t n) -> p n t", t=PACK), func=ACT.Tanh
+            )
+
+        def weigh_vector(s, lo, hi, h2, shift=0):
+            b = places[phases[s][lo // USERS]][0]
+            nc.vector.tensor_tensor(
+                h2[:, lo - shift : hi - shift, :],
+                tanh[s][:, lo:hi, :],
+                gb_psum[:, b : b + 1, :].to_broadcast([P, hi - lo, PACK]),
+                MULT,
+            )
+
+        def weigh_gpsimd(s, lo, hi, h2):
+            b = places[phases[s][lo // USERS]][0]
+            nc.gpsimd.tensor_tensor(
+                h2[:, lo:hi, :], tanh[s][:, lo:hi, :], gb_t[:, b : b + 1, :].to_broadcast([P, hi - lo, PACK]), MULT
+            )
+
+        def quantize(h, name, at):
+            width = h.shape[1]
+            if at is None:
+                codes = keep.tile([P, width], U32, name="codes_" + name, align_bytes=64)
+            else:
+                codes = shared.tile([P, width], U32, name="codes_" + name, align_bytes=64, offset=at)
+            plane = keep.tile([P, width], U8, name="plane_" + name, align_bytes=64)
+            nc.vector.quantize_mx(out=codes[:].bitcast(FP8X4), scales=plane[:], in_=h.rearrange("p n t -> p (n t)"))
+            return codes, plane
+
+        def quantize_h(h, g0, members, at=None):
+            codes, plane = quantize(h[:], "h%d_%d" % (g0, members[0]), at)
+            for e, n in enumerate(members):
+                b, lo = places[n]
+                quantised[g0 + b, lo] = (codes, plane, e * USERS)
+
+        def room(s, k):
+            return tanh_at + 8 * KB * s + 2 * KB * k
+
+        w1_mx = {}
+
+        def round_w1(b, tiles):
+            for place, c in enumerate(tiles):
+                nc.scalar.copy(
+                    out=w1_bf[b, tiles[0]][:, place * P : (place + 1) * P, :].rearrange("p (g i) t -> p g t i", i=2),
+                    in_=w1_raw[b][:, :, c * P : (c + 1) * P].rearrange("p t (g i) -> p g t i", i=2),
                 )
 
-        def weigh_vector(s, lo, hi, tanh):
-            b = steps[s][lo // USERS][0]
-            nc.vector.tensor_tensor(
-                h2[s][:, lo:hi, :], tanh, gb_psum[:, b : b + 1, :].to_broadcast([P, hi - lo, PACK]), MULT
-            )
-
-        def weigh_gpsimd(s, lo, hi):
-            b = steps[s][lo // USERS][0]
-            nc.gpsimd.tensor_tensor(
-                h2[s][:, lo:hi, :], tanh_g[s][:, lo:hi, :], gb_t[:, b : b + 1, :].to_broadcast([P, hi - lo, PACK]), MULT
-            )
-
-        def quantize(h, codes, plane, column, g0, banks):
-            width = USERS * len(banks)
-            nc.vector.quantize_mx(
-                out=codes[:, column : column + width].bitcast(FP8X4),
-                scales=plane[:, column : column + width],
-                in_=h.rearrange("p n t -> p (n t)"),
-            )
-            for e, (b, first) in enumerate(banks):
-                quantised[g0 + b, first] = (codes, plane, column + e * USERS)
-
-        def quantize_h1(h, banks, at):
-            width = USERS * len(banks)
-            name = "%d_%d" % banks[0]
-            codes = shared.tile([P, width], U32, name="h1_codes" + name, align_bytes=64, offset=at)
-            plane = keep.tile([P, width], U8, name="h1_plane" + name, align_bytes=64)
-            quantize(h, codes, plane, 0, 0, banks)
-
-        wide_codes = keep.tile([P, WIDE], U32, name="wide_codes", align_bytes=64)
-        wide_plane = keep.tile([P, WIDE], U8, name="wide_plane", align_bytes=64)
-
-        def quantize_h2(s, lo, hi):
-            banks = steps[s][lo // USERS : hi // USERS]
-            if s in (1, 2):
-                quantize(h2[s][:, lo:hi, :], wide_codes, wide_plane, (s - 1) * PAIR, I_PASSES, banks)
-            else:
-                codes = keep.tile([P, hi - lo], U32, name="h2_codes%d_%d" % (s, lo), align_bytes=64)
-                plane = keep.tile([P, hi - lo], U8, name="h2_plane%d_%d" % (s, lo), align_bytes=64)
-                quantize(h2[s][:, lo:hi, :], codes, plane, 0, I_PASSES, banks)
+        def quantize_w1(b, tiles, at):
+            codes, plane = quantize(w1_bf[b, tiles[0]][:], "w1_%d_%d" % (b, tiles[0]), at)
+            for place, c in enumerate(tiles):
+                w1_mx[b, c] = (codes[:, place * P : (place + 1) * P], plane[:, place * P : (place + 1) * P])
 
         def readout(g, y, tiles, lo, width, pitch, at, start, stop):
             b = g % I_PASSES
             codes, plane, column = quantised[g, lo]
             for c in tiles:
                 if g < I_PASSES:
-                    w = w1_codes[b][:, c * P : (c + 1) * P].bitcast(FP8X4)
-                    w_scale = w1_plane[b][:, c * P : (c + 1) * P]
+                    w = w1_mx[b, c][0].bitcast(FP8X4)
+                    w_scale = w1_mx[b, c][1]
                 else:
                     w = w4_codes[:, b, :].bitcast(U8)[:, 2 * c * P : 2 * (c + 1) * P].bitcast(FP4X4)
                     w_scale = w4_planes[:, b, :].bitcast(U8)[:, c * P : (c + 1) * P]
@@ -328,7 +316,7 @@ def tile_list_creative_user_readout_kernel(
 
         def store_scalar(y, tiles, lo, hi, queue):
             width = hi - lo
-            res = ring.tile([P, len(tiles), width], F32, name="res", bufs=11)
+            res = keep.tile([P, len(tiles), width], F32, name="res%d_%d" % (tiles[0], lo))
             for place, c in enumerate(tiles):
                 nc.scalar.activation(
                     out=res[:, place, :],
@@ -340,7 +328,7 @@ def tile_list_creative_user_readout_kernel(
 
         def store_vector(y, tiles, lo, hi):
             width = hi - lo
-            res = ring.tile([P, len(tiles), width], F32, name="res", bufs=11)
+            res = keep.tile([P, len(tiles), width], F32, name="res%d_%d" % (tiles[0], lo))
             nc.vector.tensor_tensor(
                 res[:],
                 y[:, 0 : len(tiles) * width].rearrange("p (c n) -> p c n", n=width),
@@ -351,133 +339,129 @@ def tile_list_creative_user_readout_kernel(
 
         every = list(range(N_TILES))
         low, high = every[:2], every[2:]
-
-        def open_pair(number):
-            return [(bank(number), low), (bank(number + 1), high)]
-
-        def pair_passes(halves, lo, passes, start, stop):
-            for g in passes:
-                for y, tiles in halves:
-                    readout_pair(g, y, tiles, lo, start and g == passes[0], stop and g == passes[-1])
-
-        def store_pair(halves, lo):
-            for y, tiles in halves:
-                store_scalar(y, tiles, lo, lo + PAIR, nc.sync)
-
-        def weigh(s):
-            width = USERS * len(steps[s])
-            share = GPSIMD_USERS[s]
-            h2[s] = keep.tile([P, width, PACK], BF16, name=("h_%d" if s >= 2 else "h2_%d") % s, align_bytes=64)
-            weigh_gpsimd(s, 0, min(share, USERS))
-            if share > USERS:
-                weigh_gpsimd(s, USERS, share)
-            weigh_vector(s, share, width, tanh_v[s][:])
-
-        def room(s):
-            return TANH_AT + TANH_ROOM * s
-
-        def finish(s):
-            weigh(s - 1)
-            quantize_h1(h1[s], steps[s], room(s - 1))
-            quantize_h2(s - 1, 0, PAIR)
-
-        for n in range(4):
-            multiply(n)
-        for n in range(4):
-            saturate(n)
-            linear(n)
-        for n in range(4, 8):
-            multiply(n)
-        round_w1(0, every)
-        weigh(0)
-        quantize_h1(h1[0], steps[0], room(0))
-        quantize_h2(0, 0, WIDE)
-        quantize_w1(0, room(0) + 4 * WIDE)
         wide_y = {}
 
-        def wide_passes(passes, tiles, start, stop):
-            for g in passes:
-                for c in tiles:
-                    if start and g == passes[0]:
-                        wide_y[c] = bank(SCORE_RING + c)
-                    readout(g, wide_y[c], [c], 0, WIDE, WIDE, 0, start and g == passes[0], stop and g == passes[-1])
+        def wide(g, tiles, start, stop):
+            for c in tiles:
+                readout(g, wide_y[c], [c], 0, WIDE, WIDE, 0, start, stop)
 
-        def store_wide(c):
-            store_scalar(wide_y[c], [c], 0, WIDE, nc.sync)
-
-        wide_passes([2, 0], every[:3], True, False)
-        for n in range(4, 7):
-            linear(n)
-            saturate(n)
-            multiply(n + 4)
-        linear(7)
+        share = GPSIMD_USERS[0]
+        for n in range(7):
+            multiply(n)
+        saturate(0)
+        linear(1)
+        saturate(2)
+        linear(0)
+        saturate(1)
+        multiply(7)
+        multiply(8)
+        linear(3)
+        saturate(4)
+        linear(2)
+        saturate(3)
+        multiply(9)
+        multiply(10)
+        linear(5)
+        saturate(6)
+        linear(4)
         saturate(7)
-        round_w1(1, every)
-        wide_passes([2, 0], every[3:], True, False)
-        weigh(1)
-        quantize_w1(1, room(1) + 2 * WIDE)
-        quantize_h1(h1_wide[0][:], steps[1] + steps[2], room(1) - 2 * WIDE)
-        quantize_h2(1, 0, PAIR)
-        wide_passes([1], every, False, False)
-        saturate(8)
-        linear_scalar(8)
+        saturate(5)
+        for n in (0, 2, 1):
+            weigh_gpsimd(0, n * USERS, (n + 1) * USERS, h2_a)
+        weigh_gpsimd(0, 3 * USERS, share, h2_a)
+        linear(6)
+        weigh_vector(0, share, WIDE, h2_a)
+        linear(7)
+        linear(8)
         multiply(11)
-        saturate(10)
-        linear(9)
-        saturate(9)
-        multiply(12)
-        finish(3)
-        wide_passes([3], every, False, True)
-        saturate(12)
-        for c in low:
-            store_wide(c)
-        linear(10)
-        multiply(13)
-        linear(11)
-        saturate(11)
-        third_pair = open_pair(SCORE_RING)
-        pair_passes(third_pair, third, [0], True, False)
-        multiply(14)
-        finish(4)
-        store_wide(2)
-        linear(12)
-        pair_passes(third_pair, third, [1], False, False)
-        multiply(15)
-        linear(13)
-        saturate(13)
-        saturate(14)
-        store_wide(3)
-        pair_passes(third_pair, third, [2], False, False)
-        finish(5)
-        y = bank(SCORE_RING + 2)
-        for g in range(I_PASSES):
-            readout(g, y, every, fourth, USERS, USERS, 0, g == 0, False)
-        pair_passes(third_pair, third, [3], False, True)
-        linear(14)
-        linear(15)
-        saturate(15)
-        store_pair(third_pair, third)
-        finish(6)
-        ends = [(bank(SCORE_RING + 3), low), (bank(2), high)]
-        for end, tiles in ends:
-            readout(0, end, tiles, last, USERS, USERS, 0, True, False)
-        for g in range(I_PASSES, 2 * I_PASSES):
-            readout(g, y, every, fourth, USERS, USERS, 0, False, g == 3)
-        for end, tiles in ends:
-            readout(1, end, tiles, last, USERS, USERS, 0, False, False)
-        store_scalar(y, low, fourth, last, nc.sync)
-        store_scalar(y[:, PAIR:PASS], high, fourth, last, nc.sync)
+        round_w1(0, every)
+        quantize_h(h2_a, I_PASSES, phases[0])
+        quantize_h(h1_a, 0, phases[0], room(0, 0))
+        quantize_h(h1_b, 0, phases[1], room(0, 1))
+        quantize_w1(0, every, room(0, 2))
+        for c in every[:3]:
+            wide_y[c] = bank(4 + c)
+        wide(2, every[:3], True, False)
 
-        s = len(steps) - 1
-        share = GPSIMD_USERS[s]
-        h2[s] = keep.tile([P, PAIR, PACK], BF16, name="h_%d" % s, align_bytes=64)
-        weigh_gpsimd(s, 0, share)
-        weigh_vector(s, share, USERS, tanh_v[s][:, 0 : USERS - share, :])
-        weigh_vector(s, USERS, PAIR, tanh_v[s][:, USERS - share : PAIR - share, :])
-        for b in range(I_PASSES):
-            quantize_h2(s, b * USERS, (b + 1) * USERS)
-        for b in range(I_PASSES):
+        share = GPSIMD_USERS[1]
+        saturate(9)
+        saturate(8)
+        multiply(12)
+        wide(0, every[:3], False, False)
+        saturate(10)
+        saturate(11)
+        linear(9)
+        weigh_gpsimd(1, 0, share, h2_b)
+        linear(10)
+        weigh_vector(1, share, WIDE, h2_b)
+        linear(11)
+        multiply(13)
+        multiply(14)
+        wide_y[3] = bank(0)
+        wide(2, [3], True, False)
+        wide(0, [3], False, False)
+        round_w1(1, every)
+        quantize_h(h2_b, I_PASSES, phases[1])
+        quantize_h(h1_c, 0, phases[2], room(1, 0))
+        quantize_w1(1, every, room(1, 1))
+        wide(3, every, False, False)
+        wide(1, every, False, True)
+
+        share = GPSIMD_USERS[2]
+        for n in range(12, 15):
+            saturate(n)
+        linear(12)
+        multiply(15)
+        weigh_gpsimd(2, 0, share, h2_c)
+        linear(13)
+        if share < PAIR:
+            weigh_vector(2, share, PAIR, h2_c)
+        weigh_vector(2, PAIR, WIDE, h2_c)
+        linear(14)
+        for c in low:
+            store_scalar(wide_y[c], [c], 0, WIDE, nc.sync)
+        saturate(15)
+        linear_scalar(15)
+        pair = [(bank(4), low), (bank(5), high)]
+        for c in high:
+            store_scalar(wide_y[c], [c], 0, WIDE, nc.sync)
+        for y, tiles in pair:
+            for g in range(I_PASSES):
+                readout_pair(g, y, tiles, third, g == 0, False)
+        quantize_h(h1_d, 0, [12, 13], room(2, 0))
+        quantize_h(h1_14, 0, [14], room(2, 2))
+        quantize_h(h2_c, I_PASSES, phases[2])
+        sixth = bank(2)
+        for g in range(I_PASSES):
+            readout(g, sixth, every, fourth, USERS, USERS, 0, g == 0, False)
+        for y, tiles in pair:
+            for g in range(I_PASSES, 2 * I_PASSES):
+                readout_pair(g, y, tiles, third, False, g == 3)
+        ends = [(bank(6), low), (bank(3), high)]
+        for y, tiles in pair:
+            store_scalar(y, tiles, third, fourth, nc.sync)
+
+        share = GPSIMD_USERS[3]
+        weigh_gpsimd(3, 0, share, h2_d)
+        weigh_vector(3, USERS, PAIR, h2_d)
+        if share < USERS:
+            weigh_vector(3, share, USERS, h2_d)
+        weigh_vector(3, PAIR, PAIR + USERS, h2_14, PAIR)
+        quantize_h(h2_d, I_PASSES, [12, 13])
+        quantize_h(h1_15, 0, [15])
+        for g in range(I_PASSES, 2 * I_PASSES):
+            readout(g, sixth, every, fourth, USERS, USERS, 0, False, g == 3)
+        for g in range(I_PASSES):
             for y, tiles in ends:
-                readout(I_PASSES + b, y, tiles, last, USERS, USERS, 0, False, b == I_PASSES - 1)
+                readout(g, y, tiles, last, USERS, USERS, 0, g == 0, False)
+        store_scalar(sixth, low, fourth, last, nc.sync)
+        store_scalar(sixth[:, PAIR:PASS], high, fourth, last, nc.sync)
+
+        weigh_vector(4, 0, USERS, h2_15)
+        quantize_h(h2_14, I_PASSES, [14])
+        quantize_h(h2_15, I_PASSES, [15])
+        for g in range(I_PASSES, 2 * I_PASSES):
+            for y, tiles in ends:
+                readout(g, y, tiles, last, USERS, USERS, 0, False, g == 3)
         store_scalar(ends[0][0], low, last, S2, nc.scalar)
         store_vector(ends[1][0], high, last, S2)

@@ -31,8 +31,8 @@ LIST_ROWS = 16
 USER_SLICE = 512
 PAIR = 2 * USERS
 WIDE = 4 * USERS
-FIRST_LOAD, SECOND_LOAD = 768, 1152
-GPSIMD_USERS = [472, 256, 240, 96]
+FIRST_LOAD, SECOND_LOAD = 512, 1152
+GPSIMD_USERS = [472, 240, 240, 96]
 KB = 1024
 
 
@@ -58,6 +58,7 @@ def tile_list_creative_user_readout_kernel(
         nc.vector.memset(v_rows[:], 0)
         nc.vector.memset(v2_rows[:], 0)
         nc.vector.memset(g_rows[:], 0.0)
+        nc.vector.memset(late_planes[:], 0)
         nc.vector.memset(w4_planes[:], 0)
 
         def load_words(tile, words, lo, hi):
@@ -66,9 +67,9 @@ def tile_list_creative_user_readout_kernel(
         def load_rows(tile, scales):
             nc.sync.dma_start(out=tile[0:P:4, :], in_=scales.rearrange("a q n -> q a n").bitcast(I32))
 
-        nc.sync.dma_start(idx[:], offs)
         load_words(v2_words[0], tab2_words[0], 0, FIRST_LOAD)
         load_rows(v_rows, tab_scales)
+        nc.sync.dma_start(idx[:], offs)
         nc.sync.dma_start(idx2[:], offs2)
         load_words(v2_words[0], tab2_words[0], FIRST_LOAD, SECOND_LOAD)
         load_rows(v2_rows, tab2_scales)
@@ -95,20 +96,24 @@ def tile_list_creative_user_readout_kernel(
         user_rows = keep.tile([P, S2], U8, name="user_rows", align_bytes=64)
         early_planes = keep.tile([P, S + S2], U8, name="early_planes", align_bytes=64)
 
-        nc.vector.tensor_copy(creative_rows[:], v_rows[:].bitcast(U8).indirect(idx[:]))
+        for lo in range(0, S, PASS):
+            nc.vector.tensor_copy(
+                creative_rows[:, lo : lo + PASS],
+                v_rows[:].bitcast(U8).indirect(idx[:, lo // LIST_ROWS : (lo + PASS) // LIST_ROWS]),
+            )
         nc.vector.tensor_copy(user_rows[:], v2_rows[:].bitcast(U8).indirect(idx2[:]))
-        nc.vector.tensor_copy(
-            early_planes[:, 0:S].rearrange("p (b t m) -> p b t m", b=I_PASSES, t=PACK),
-            creative_rows[:].rearrange("p (b m t) -> p b t m", b=I_PASSES, t=PACK),
-        )
+        for lo in range(0, S, PASS):
+            nc.vector.tensor_copy(
+                early_planes[:, lo : lo + PASS].rearrange("p (t m) -> p t m", t=PACK),
+                creative_rows[:, lo : lo + PASS].rearrange("p (m t) -> p t m", t=PACK),
+            )
         nc.vector.tensor_copy(early_planes[:, S : S + S2].bitcast(I32), user_rows[:].bitcast(I32))
-        nc.vector.tensor_copy(late_planes[:], early_planes[:].bitcast(I32))
         for r in range(1, 4):
             nc.sync.dma_start(
                 out=early_planes[r:P:QUADRANT, :].bitcast(I32), in_=early_planes[8 * r : P : QUADRANT, :].bitcast(I32)
             )
         load_words(v2_words[1], tab2_words[1], 0, T2)
-        for r in range(1, 4):
+        for r in range(4):
             nc.sync.dma_start(
                 out=late_planes[4 + r : P : QUADRANT, :], in_=early_planes[8 * r + 4 : P : QUADRANT, :].bitcast(I32)
             )
@@ -120,18 +125,16 @@ def tile_list_creative_user_readout_kernel(
                 v_words[a][:].bitcast(U32).indirect(idx[:, lo // LIST_ROWS : hi // LIST_ROWS]),
             )
 
-        def gather_users(a, lo):
+        def gather_users(a, lo, hi):
             nc.vector.tensor_copy(
-                user_words[a][:, lo : lo + USER_SLICE],
-                v2_words[a][:].bitcast(U32).indirect(idx2[:, lo // LIST_ROWS : (lo + USER_SLICE) // LIST_ROWS]),
+                user_words[a][:, lo:hi], v2_words[a][:].bitcast(U32).indirect(idx2[:, lo // LIST_ROWS : hi // LIST_ROWS])
             )
 
-        gather_users(0, 0)
-        gather_users(0, USER_SLICE)
+        gather_users(0, 0, S2)
         gather_creatives(0, 0, S)
         gather_creatives(1, 0, S)
-        gather_users(1, 0)
-        gather_users(1, USER_SLICE)
+        gather_users(1, 0, USER_SLICE)
+        gather_users(1, USER_SLICE, S2)
 
         w1_raw = [keep.tile([P, PACK, N], F32, name="w1_raw%d" % b, align_bytes=64) for b in range(I_PASSES)]
         w4_codes = keep.tile([P, I_PASSES, N // 2], I32, name="w4_codes", align_bytes=64)
@@ -366,8 +369,8 @@ def tile_list_creative_user_readout_kernel(
         linear(4)
         saturate(7)
         saturate(5)
-        for n in (0, 2, 1):
-            weigh_gpsimd(0, n * USERS, (n + 1) * USERS, h2_a)
+        weigh_gpsimd(0, 0, USERS, h2_a)
+        weigh_gpsimd(0, USERS, 3 * USERS, h2_a)
         weigh_gpsimd(0, 3 * USERS, share, h2_a)
         linear(6)
         weigh_vector(0, share, WIDE, h2_a)

@@ -31,8 +31,8 @@ LIST_ROWS = 16
 USER_SLICE = 512
 PAIR = 2 * USERS
 WIDE = 4 * USERS
-FIRST_LOAD, SECOND_LOAD = 512, 1152
-GPSIMD_USERS = [472, 240, 240, 96]
+FIRST_LOAD, SECOND_LOAD = 384, 1024
+GPSIMD_USERS = [456, 280, 200, 80]
 KB = 1024
 
 
@@ -55,9 +55,8 @@ def tile_list_creative_user_readout_kernel(
         late_planes = keep.tile([P, (S + S2) // 4], I32, name="late_planes", align_bytes=64)
         w4_planes = keep.tile([P, I_PASSES, N // 4], I32, name="w4_planes", align_bytes=64)
 
-        nc.vector.memset(v_rows[:], 0)
+        nc.gpsimd.memset(v_rows[:], 0)
         nc.vector.memset(v2_rows[:], 0)
-        nc.vector.memset(g_rows[:], 0.0)
         nc.vector.memset(late_planes[:], 0)
         nc.vector.memset(w4_planes[:], 0)
 
@@ -67,9 +66,13 @@ def tile_list_creative_user_readout_kernel(
         def load_rows(tile, scales):
             nc.sync.dma_start(out=tile[0:P:4, :], in_=scales.rearrange("a q n -> q a n").bitcast(I32))
 
+        ident = keep.tile([P, P], F32, name="ident")
+        make_identity(nc, ident[:])
+        nc.scalar.activation(out=g_rows[:], in_=ident[:, 0:1].to_broadcast([P, PASS]), func=ACT.Copy, scale=0.0)
+
+        nc.sync.dma_start(idx[:], offs)
         load_words(v2_words[0], tab2_words[0], 0, FIRST_LOAD)
         load_rows(v_rows, tab_scales)
-        nc.sync.dma_start(idx[:], offs)
         nc.sync.dma_start(idx2[:], offs2)
         load_words(v2_words[0], tab2_words[0], FIRST_LOAD, SECOND_LOAD)
         load_rows(v2_rows, tab2_scales)
@@ -79,8 +82,6 @@ def tile_list_creative_user_readout_kernel(
             nc.sync.dma_start(out=g_rows[first : first + 8 : 4, :], in_=g.rearrange("(b i) -> b i", b=I_PASSES))
         load_words(v_words[1], tab_words[1], 0, T)
 
-        ident = keep.tile([P, P], F32, name="ident")
-        make_identity(nc, ident[:])
         gb_bank = psum.tile([P, PACK, P], F32, name="gb_bank")
         for t in range(PACK):
             nc.tensor.transpose(gb_bank[:, t, :], g_rows[:, t::PACK], ident[:])
@@ -168,29 +169,26 @@ def tile_list_creative_user_readout_kernel(
         def half(name, users, at):
             return shared.tile([P, users, PACK], BF16, name=name, align_bytes=64, offset=at)
 
-        room_a, room_b, room_c, tanh_at = 0, 4 * KB, 8 * KB, 12 * KB
+        room_b, room_c, room_a, tanh_at = 0, 8 * KB, 12 * KB, 16 * KB
         tanh = [
             shared.tile([P, USERS * len(members), PACK], F32, name="tanh%d" % s, align_bytes=64, offset=tanh_at + 8 * KB * s)
             for s, members in enumerate(phases)
         ]
-        w1_bf = {
-            (0, 0): half("w1_bf0", N, room_b),
-            (1, 0): half("w1_bf1", N, room_c),
-        }
-        h1_a = keep.tile([P, WIDE, PACK], BF16, name="h1_a", align_bytes=64)
+        both_a = half("both_a", 2 * WIDE, room_b)
+        h2_a, h1_a = both_a[:, 0:WIDE, :], both_a[:, WIDE : 2 * WIDE, :]
         h1_b = keep.tile([P, WIDE, PACK], BF16, name="h1_b", align_bytes=64)
-        h1_c = keep.tile([P, WIDE, PACK], BF16, name="h1_c", align_bytes=64)
-        h2_a = keep.tile([P, WIDE, PACK], BF16, name="h2_a", align_bytes=64)
+        h1_8 = keep.tile([P, PAIR, PACK], BF16, name="h1_8", align_bytes=64)
+        w1_bf = [half("w1_bf0", N, room_a), half("w1_bf1", N, room_c)]
+        h1_10 = half("h1_10", PAIR, room_a)
+        h1_12 = half("h1_12", PAIR, room_a + 2 * KB)
         h2_b = half("h2_b", WIDE, room_b)
-        h1_d = half("h1_d", PAIR, room_b)
-        h1_14 = half("h1_14", USERS, room_b + 2 * KB)
+        h1_14 = half("h1_14", PAIR, room_b)
         h2_c = half("h2_c", WIDE, room_c)
-        h2_d = half("h2_d", PAIR, room_b + 2 * KB)
+        h2_d = half("h2_d", PAIR, room_b)
         h2_14 = half("h2_14", USERS, room_c)
-        h1_15 = keep.tile([P, USERS, PACK], BF16, name="h1_15", align_bytes=64)
-        h2_15 = half("h2_15", USERS, room_b + 2 * KB)
-        h1_of = [h1_a] * 4 + [h1_b] * 4 + [h1_c] * 4 + [h1_d] * 2 + [h1_14, h1_15]
-        column_of = [0, 1, 2, 3] * 3 + [0, 1, 0, 0]
+        h2_15 = half("h2_15", USERS, room_b)
+        h1_of = [h1_a] * 4 + [h1_b] * 4 + [h1_8] * 2 + [h1_10] * 2 + [h1_12] * 2 + [h1_14] * 2
+        column_of = [0, 1, 2, 3] * 2 + [0, 1] * 4
 
         accs, quantised = {}, {}
 
@@ -223,13 +221,15 @@ def tile_list_creative_user_readout_kernel(
 
         def linear_scalar(n):
             b = places[n][0]
+            at = column_of[n] * USERS
             apart = keep.tile([P, PACK, USERS], BF16, name="apart", align_bytes=64)
             for t in range(PACK):
                 nc.scalar.activation(
                     out=apart[:, t, :], in_=accs[n][:, t * USERS : (t + 1) * USERS], func=ACT.Copy, scale=ga_t[:, b, t : t + 1]
                 )
             nc.scalar.copy(
-                out=h1_of[n][:].rearrange("p (g i) t -> p g t i", i=2), in_=apart[:].rearrange("p t (g i) -> p g t i", i=2)
+                out=h1_of[n][:, at : at + USERS, :].rearrange("p (g i) t -> p g t i", i=2),
+                in_=apart[:].rearrange("p t (g i) -> p g t i", i=2),
             )
 
         def saturate(n):
@@ -264,28 +264,31 @@ def tile_list_creative_user_readout_kernel(
             nc.vector.quantize_mx(out=codes[:].bitcast(FP8X4), scales=plane[:], in_=h.rearrange("p n t -> p (n t)"))
             return codes, plane
 
-        def quantize_h(h, g0, members, at=None):
-            codes, plane = quantize(h[:], "h%d_%d" % (g0, members[0]), at)
+        def name_h(codes, plane, column, g0, members):
             for e, n in enumerate(members):
                 b, lo = places[n]
-                quantised[g0 + b, lo] = (codes, plane, e * USERS)
+                quantised[g0 + b, lo] = (codes, plane, column + e * USERS)
+
+        def quantize_h(h, g0, members, at=None):
+            codes, plane = quantize(h[:], "h%d_%d" % (g0, members[0]), at)
+            name_h(codes, plane, 0, g0, members)
 
         def room(s, k):
             return tanh_at + 8 * KB * s + 2 * KB * k
 
         w1_mx = {}
 
-        def round_w1(b, tiles):
-            for place, c in enumerate(tiles):
+        def round_w1(b):
+            for c in range(N_TILES):
                 nc.scalar.copy(
-                    out=w1_bf[b, tiles[0]][:, place * P : (place + 1) * P, :].rearrange("p (g i) t -> p g t i", i=2),
+                    out=w1_bf[b][:, c * P : (c + 1) * P, :].rearrange("p (g i) t -> p g t i", i=2),
                     in_=w1_raw[b][:, :, c * P : (c + 1) * P].rearrange("p t (g i) -> p g t i", i=2),
                 )
 
-        def quantize_w1(b, tiles, at):
-            codes, plane = quantize(w1_bf[b, tiles[0]][:], "w1_%d_%d" % (b, tiles[0]), at)
-            for place, c in enumerate(tiles):
-                w1_mx[b, c] = (codes[:, place * P : (place + 1) * P], plane[:, place * P : (place + 1) * P])
+        def quantize_w1(b, at):
+            codes, plane = quantize(w1_bf[b][:], "w1_%d" % b, at)
+            for c in range(N_TILES):
+                w1_mx[b, c] = (codes[:, c * P : (c + 1) * P], plane[:, c * P : (c + 1) * P])
 
         def readout(g, y, tiles, lo, width, pitch, at, start, stop):
             b = g % I_PASSES
@@ -359,88 +362,92 @@ def tile_list_creative_user_readout_kernel(
         multiply(7)
         multiply(8)
         linear(3)
-        saturate(4)
         linear(2)
         saturate(3)
         multiply(9)
         multiply(10)
-        linear(5)
-        saturate(6)
-        linear(4)
+        linear(7)
         saturate(7)
-        saturate(5)
+        multiply(11)
+        round_w1(0)
+        linear(8)
+        saturate(8)
+        multiply(12)
         weigh_gpsimd(0, 0, USERS, h2_a)
         weigh_gpsimd(0, USERS, 3 * USERS, h2_a)
         weigh_gpsimd(0, 3 * USERS, share, h2_a)
+        for n in (4, 5):
+            linear(n)
+            saturate(n)
+        if share < WIDE:
+            weigh_vector(0, share, WIDE, h2_a)
         linear(6)
-        weigh_vector(0, share, WIDE, h2_a)
-        linear(7)
-        linear(8)
-        multiply(11)
-        round_w1(0, every)
-        quantize_h(h2_a, I_PASSES, phases[0])
-        quantize_h(h1_a, 0, phases[0], room(0, 0))
-        quantize_h(h1_b, 0, phases[1], room(0, 1))
-        quantize_w1(0, every, room(0, 2))
+        saturate(6)
+        quantize_w1(0, None)
+        codes, plane = quantize(both_a[:], "first", None)
+        name_h(codes, plane, 0, I_PASSES, phases[0])
+        name_h(codes, plane, WIDE, 0, phases[0])
+        quantize_h(h1_b, 0, phases[1], room(0, 0))
         for c in every[:3]:
             wide_y[c] = bank(4 + c)
         wide(2, every[:3], True, False)
+        wide(0, every[:3], False, False)
 
         share = GPSIMD_USERS[1]
         saturate(9)
-        saturate(8)
-        multiply(12)
-        wide(0, every[:3], False, False)
-        saturate(10)
-        saturate(11)
-        linear(9)
+        linear(12)
+        saturate(12)
         weigh_gpsimd(1, 0, share, h2_b)
         linear(10)
+        saturate(10)
+        linear(9)
         weigh_vector(1, share, WIDE, h2_b)
         linear(11)
-        multiply(13)
+        multiply(15)
         multiply(14)
-        wide_y[3] = bank(0)
-        wide(2, [3], True, False)
-        wide(0, [3], False, False)
-        round_w1(1, every)
+        multiply(13)
+        round_w1(1)
+        saturate(11)
         quantize_h(h2_b, I_PASSES, phases[1])
-        quantize_h(h1_c, 0, phases[2], room(1, 0))
-        quantize_w1(1, every, room(1, 1))
-        wide(3, every, False, False)
+        quantize_h(h1_8, 0, [8, 9], room(1, 0))
+        quantize_h(h1_10, 0, [10, 11], room(1, 2))
+        quantize_w1(1, room(1, 1))
+        wide(3, every[:3], False, False)
+        wide_y[3] = bank(0)
+        for g in (2, 0, 3):
+            wide(g, [3], g == 2, False)
         wide(1, every, False, True)
 
         share = GPSIMD_USERS[2]
-        for n in range(12, 15):
-            saturate(n)
-        linear(12)
-        multiply(15)
+        linear(14)
+        saturate(13)
+        saturate(15)
+        linear_scalar(15)
+        saturate(14)
         weigh_gpsimd(2, 0, share, h2_c)
         linear(13)
         if share < PAIR:
             weigh_vector(2, share, PAIR, h2_c)
         weigh_vector(2, PAIR, WIDE, h2_c)
-        linear(14)
-        for c in low:
+        for c in every:
             store_scalar(wide_y[c], [c], 0, WIDE, nc.sync)
-        saturate(15)
-        linear_scalar(15)
-        pair = [(bank(4), low), (bank(5), high)]
-        for c in high:
-            store_scalar(wide_y[c], [c], 0, WIDE, nc.sync)
+        pair = [(bank(2), low), (bank(1), high)]
         for y, tiles in pair:
             for g in range(I_PASSES):
                 readout_pair(g, y, tiles, third, g == 0, False)
-        quantize_h(h1_d, 0, [12, 13], room(2, 0))
-        quantize_h(h1_14, 0, [14], room(2, 2))
+        quantize_h(h1_12, 0, [12, 13])
+        quantize_h(h1_14, 0, [14, 15], room(2, 0))
         quantize_h(h2_c, I_PASSES, phases[2])
-        sixth = bank(2)
+        sixth = bank(3)
         for g in range(I_PASSES):
             readout(g, sixth, every, fourth, USERS, USERS, 0, g == 0, False)
         for y, tiles in pair:
             for g in range(I_PASSES, 2 * I_PASSES):
                 readout_pair(g, y, tiles, third, False, g == 3)
-        ends = [(bank(6), low), (bank(3), high)]
+        ends = [(bank(number), [c]) for c, number in enumerate((4, 5, 6, 0))]
+        for g in range(I_PASSES):
+            for y, tiles in ends:
+                readout(g, y, tiles, last, USERS, USERS, 0, g == 0, False)
         for y, tiles in pair:
             store_scalar(y, tiles, third, fourth, nc.sync)
 
@@ -451,12 +458,8 @@ def tile_list_creative_user_readout_kernel(
             weigh_vector(3, share, USERS, h2_d)
         weigh_vector(3, PAIR, PAIR + USERS, h2_14, PAIR)
         quantize_h(h2_d, I_PASSES, [12, 13])
-        quantize_h(h1_15, 0, [15])
         for g in range(I_PASSES, 2 * I_PASSES):
             readout(g, sixth, every, fourth, USERS, USERS, 0, False, g == 3)
-        for g in range(I_PASSES):
-            for y, tiles in ends:
-                readout(g, y, tiles, last, USERS, USERS, 0, g == 0, False)
         store_scalar(sixth, low, fourth, last, nc.sync)
         store_scalar(sixth[:, PAIR:PASS], high, fourth, last, nc.sync)
 
@@ -466,5 +469,7 @@ def tile_list_creative_user_readout_kernel(
         for g in range(I_PASSES, 2 * I_PASSES):
             for y, tiles in ends:
                 readout(g, y, tiles, last, USERS, USERS, 0, False, g == 3)
-        store_scalar(ends[0][0], low, last, S2, nc.scalar)
-        store_vector(ends[1][0], high, last, S2)
+        store_scalar(ends[0][0], [0], last, S2, nc.sync)
+        store_vector(ends[1][0], [1], last, S2)
+        store_scalar(ends[2][0], [2], last, S2, nc.scalar)
+        store_vector(ends[3][0], [3], last, S2)

@@ -32,7 +32,7 @@ USER_SLICE = 512
 PAIR = 2 * USERS
 WIDE = 4 * USERS
 FIRST_LOAD, SECOND_LOAD = 384, 1024
-GPSIMD_USERS = [456, 280, 200, 80]
+GPSIMD_USERS = [464, 288, 200, 96, 64]
 KB = 1024
 
 
@@ -184,9 +184,9 @@ def tile_list_creative_user_readout_kernel(
         h2_b = half("h2_b", WIDE, room_b)
         h1_14 = half("h1_14", PAIR, room_b)
         h2_c = half("h2_c", WIDE, room_c)
-        h2_d = half("h2_d", PAIR, room_b)
+        h2_d = half("h2_d", PAIR, room_c)
         h2_14 = half("h2_14", USERS, room_c)
-        h2_15 = half("h2_15", USERS, room_b)
+        h2_15 = half("h2_15", USERS, room_c + KB)
         h1_of = [h1_a] * 4 + [h1_b] * 4 + [h1_8] * 2 + [h1_10] * 2 + [h1_12] * 2 + [h1_14] * 2
         column_of = [0, 1, 2, 3] * 2 + [0, 1] * 4
 
@@ -219,19 +219,6 @@ def tile_list_creative_user_readout_kernel(
                 MULT,
             )
 
-        def linear_scalar(n):
-            b = places[n][0]
-            at = column_of[n] * USERS
-            apart = keep.tile([P, PACK, USERS], BF16, name="apart", align_bytes=64)
-            for t in range(PACK):
-                nc.scalar.activation(
-                    out=apart[:, t, :], in_=accs[n][:, t * USERS : (t + 1) * USERS], func=ACT.Copy, scale=ga_t[:, b, t : t + 1]
-                )
-            nc.scalar.copy(
-                out=h1_of[n][:, at : at + USERS, :].rearrange("p (g i) t -> p g t i", i=2),
-                in_=apart[:].rearrange("p t (g i) -> p g t i", i=2),
-            )
-
         def saturate(n):
             s = phase_of[n]
             at = (n - phases[s][0]) * USERS
@@ -248,10 +235,13 @@ def tile_list_creative_user_readout_kernel(
                 MULT,
             )
 
-        def weigh_gpsimd(s, lo, hi, h2):
+        def weigh_gpsimd(s, lo, hi, h2, shift=0):
             b = places[phases[s][lo // USERS]][0]
             nc.gpsimd.tensor_tensor(
-                h2[:, lo:hi, :], tanh[s][:, lo:hi, :], gb_t[:, b : b + 1, :].to_broadcast([P, hi - lo, PACK]), MULT
+                h2[:, lo - shift : hi - shift, :],
+                tanh[s][:, lo:hi, :],
+                gb_t[:, b : b + 1, :].to_broadcast([P, hi - lo, PACK]),
+                MULT,
             )
 
         def quantize(h, name, at):
@@ -422,32 +412,26 @@ def tile_list_creative_user_readout_kernel(
         linear(14)
         saturate(13)
         saturate(15)
-        linear_scalar(15)
         saturate(14)
         weigh_gpsimd(2, 0, share, h2_c)
-        linear(13)
         if share < PAIR:
             weigh_vector(2, share, PAIR, h2_c)
         weigh_vector(2, PAIR, WIDE, h2_c)
+        linear(13)
         for c in every:
             store_scalar(wide_y[c], [c], 0, WIDE, nc.sync)
-        pair = [(bank(2), low), (bank(1), high)]
+        pair = [(bank(3), low), (bank(4), high)]
         for y, tiles in pair:
             for g in range(I_PASSES):
                 readout_pair(g, y, tiles, third, g == 0, False)
-        quantize_h(h1_12, 0, [12, 13])
-        quantize_h(h1_14, 0, [14, 15], room(2, 0))
         quantize_h(h2_c, I_PASSES, phases[2])
-        sixth = bank(3)
-        for g in range(I_PASSES):
-            readout(g, sixth, every, fourth, USERS, USERS, 0, g == 0, False)
+        quantize_h(h1_12, 0, [12, 13], room(2, 1))
         for y, tiles in pair:
             for g in range(I_PASSES, 2 * I_PASSES):
                 readout_pair(g, y, tiles, third, False, g == 3)
-        ends = [(bank(number), [c]) for c, number in enumerate((4, 5, 6, 0))]
+        sixth = bank(2)
         for g in range(I_PASSES):
-            for y, tiles in ends:
-                readout(g, y, tiles, last, USERS, USERS, 0, g == 0, False)
+            readout(g, sixth, every, fourth, USERS, USERS, 0, g == 0, False)
         for y, tiles in pair:
             store_scalar(y, tiles, third, fourth, nc.sync)
 
@@ -456,19 +440,27 @@ def tile_list_creative_user_readout_kernel(
         weigh_vector(3, USERS, PAIR, h2_d)
         if share < USERS:
             weigh_vector(3, share, USERS, h2_d)
-        weigh_vector(3, PAIR, PAIR + USERS, h2_14, PAIR)
+        linear(15)
         quantize_h(h2_d, I_PASSES, [12, 13])
+        quantize_h(h1_14, 0, [14, 15])
         for g in range(I_PASSES, 2 * I_PASSES):
             readout(g, sixth, every, fourth, USERS, USERS, 0, False, g == 3)
+        ends = [(bank(number), [c]) for c, number in enumerate((5, 6, 0, 1))]
+        for g in range(I_PASSES):
+            for y, tiles in ends:
+                readout(g, y, tiles, last, USERS, USERS, 0, g == 0, False)
         store_scalar(sixth, low, fourth, last, nc.sync)
         store_scalar(sixth[:, PAIR:PASS], high, fourth, last, nc.sync)
 
+        share = GPSIMD_USERS[4]
+        weigh_gpsimd(3, PAIR, PAIR + share, h2_14, PAIR)
         weigh_vector(4, 0, USERS, h2_15)
-        quantize_h(h2_14, I_PASSES, [14])
+        weigh_vector(3, PAIR + share, PAIR + USERS, h2_14, PAIR)
         quantize_h(h2_15, I_PASSES, [15])
-        for g in range(I_PASSES, 2 * I_PASSES):
+        quantize_h(h2_14, I_PASSES, [14])
+        for g in (3, 2):
             for y, tiles in ends:
-                readout(g, y, tiles, last, USERS, USERS, 0, False, g == 3)
+                readout(g, y, tiles, last, USERS, USERS, 0, False, g == 2)
         store_scalar(ends[0][0], [0], last, S2, nc.sync)
         store_vector(ends[1][0], [1], last, S2)
         store_scalar(ends[2][0], [2], last, S2, nc.scalar)

@@ -31,7 +31,7 @@ LIST_ROWS = 16
 USER_SLICE = 512
 PAIR = 2 * USERS
 WIDE = 4 * USERS
-FIRST_LOAD, SECOND_LOAD = 384, 1024
+FIRST_LOAD, SECOND_LOAD = 512, 1152
 GPSIMD_USERS = [464, 288, 200, 96, 64]
 KB = 1024
 
@@ -55,8 +55,9 @@ def tile_list_creative_user_readout_kernel(
         late_planes = keep.tile([P, (S + S2) // 4], I32, name="late_planes", align_bytes=64)
         w4_planes = keep.tile([P, I_PASSES, N // 4], I32, name="w4_planes", align_bytes=64)
 
-        nc.gpsimd.memset(v_rows[:], 0)
+        nc.vector.memset(v_rows[:], 0)
         nc.vector.memset(v2_rows[:], 0)
+        nc.vector.memset(g_rows[:], 0.0)
         nc.vector.memset(late_planes[:], 0)
         nc.vector.memset(w4_planes[:], 0)
 
@@ -68,11 +69,10 @@ def tile_list_creative_user_readout_kernel(
 
         ident = keep.tile([P, P], F32, name="ident")
         make_identity(nc, ident[:])
-        nc.scalar.activation(out=g_rows[:], in_=ident[:, 0:1].to_broadcast([P, PASS]), func=ACT.Copy, scale=0.0)
 
-        nc.sync.dma_start(idx[:], offs)
         load_words(v2_words[0], tab2_words[0], 0, FIRST_LOAD)
         load_rows(v_rows, tab_scales)
+        nc.sync.dma_start(idx[:], offs)
         nc.sync.dma_start(idx2[:], offs2)
         load_words(v2_words[0], tab2_words[0], FIRST_LOAD, SECOND_LOAD)
         load_rows(v2_rows, tab2_scales)

@@ -32,7 +32,7 @@ USER_SLICE = 512
 PAIR = 2 * USERS
 WIDE = 4 * USERS
 FIRST_LOAD, SECOND_LOAD = 512, 1152
-GPSIMD_USERS = [464, 288, 200, 96, 64]
+GPSIMD_USERS = [464, 312, 200, 96, 64]
 KB = 1024
 
 
@@ -159,7 +159,7 @@ def tile_list_creative_user_readout_kernel(
         places = [(b, lo) for b in range(I_PASSES) for lo in range(0, WIDE, USERS)]
         places.extend((b, lo) for b in range(I_PASSES) for lo in (third, third + USERS))
         places.extend((b, lo) for lo in (fourth, last) for b in range(I_PASSES))
-        score_banks = list(range(7)) + [n % 4 for n in range(8)] + [1]
+        score_banks = list(range(7)) + [0, 2, 3, 0, 1, 1, 2, 3, 1]
         phases = [range(0, 4), range(4, 8), range(8, 12), range(12, 15), range(15, 16)]
         phase_of = {n: s for s, members in enumerate(phases) for n in members}
 
@@ -177,18 +177,17 @@ def tile_list_creative_user_readout_kernel(
         both_a = half("both_a", 2 * WIDE, room_b)
         h2_a, h1_a = both_a[:, 0:WIDE, :], both_a[:, WIDE : 2 * WIDE, :]
         h1_b = keep.tile([P, WIDE, PACK], BF16, name="h1_b", align_bytes=64)
-        h1_8 = keep.tile([P, PAIR, PACK], BF16, name="h1_8", align_bytes=64)
         w1_bf = [half("w1_bf0", N, room_a), half("w1_bf1", N, room_c)]
-        h1_10 = half("h1_10", PAIR, room_a)
-        h1_12 = half("h1_12", PAIR, room_a + 2 * KB)
+        h1_c = half("h1_c", WIDE, room_a)
+        h1_12 = keep.tile([P, PAIR, PACK], BF16, name="h1_12", align_bytes=64)
         h2_b = half("h2_b", WIDE, room_b)
         h1_14 = half("h1_14", PAIR, room_b)
         h2_c = half("h2_c", WIDE, room_c)
         h2_d = half("h2_d", PAIR, room_c)
         h2_14 = half("h2_14", USERS, room_c)
         h2_15 = half("h2_15", USERS, room_c + KB)
-        h1_of = [h1_a] * 4 + [h1_b] * 4 + [h1_8] * 2 + [h1_10] * 2 + [h1_12] * 2 + [h1_14] * 2
-        column_of = [0, 1, 2, 3] * 2 + [0, 1] * 4
+        h1_of = [h1_a] * 4 + [h1_b] * 4 + [h1_c] * 4 + [h1_12] * 2 + [h1_14] * 2
+        column_of = [0, 1, 2, 3] * 3 + [0, 1] * 2
 
         accs, quantised = {}, {}
 
@@ -350,19 +349,19 @@ def tile_list_creative_user_readout_kernel(
         linear(0)
         saturate(1)
         multiply(7)
-        multiply(8)
+        multiply(12)
         linear(3)
         linear(2)
         saturate(3)
+        multiply(8)
         multiply(9)
-        multiply(10)
         linear(7)
         saturate(7)
-        multiply(11)
+        multiply(10)
         round_w1(0)
-        linear(8)
-        saturate(8)
-        multiply(12)
+        linear(12)
+        saturate(12)
+        multiply(11)
         weigh_gpsimd(0, 0, USERS, h2_a)
         weigh_gpsimd(0, USERS, 3 * USERS, h2_a)
         weigh_gpsimd(0, 3 * USERS, share, h2_a)
@@ -384,23 +383,22 @@ def tile_list_creative_user_readout_kernel(
         wide(0, every[:3], False, False)
 
         share = GPSIMD_USERS[1]
-        saturate(9)
-        linear(12)
-        saturate(12)
-        weigh_gpsimd(1, 0, share, h2_b)
-        linear(10)
-        saturate(10)
-        linear(9)
-        weigh_vector(1, share, WIDE, h2_b)
+        saturate(8)
         linear(11)
+        saturate(11)
+        weigh_gpsimd(1, 0, share, h2_b)
+        linear(9)
+        saturate(9)
+        linear(8)
+        weigh_vector(1, share, WIDE, h2_b)
+        linear(10)
         multiply(15)
         multiply(14)
         multiply(13)
         round_w1(1)
-        saturate(11)
+        saturate(10)
         quantize_h(h2_b, I_PASSES, phases[1])
-        quantize_h(h1_8, 0, [8, 9], room(1, 0))
-        quantize_h(h1_10, 0, [10, 11], room(1, 2))
+        quantize_h(h1_c, 0, phases[2], room(1, 0))
         quantize_w1(1, room(1, 1))
         wide(3, every[:3], False, False)
         wide_y[3] = bank(0)

@@ -25,15 +25,16 @@ K_PASSES = K // PASS
 I_PASSES = S // PASS
 QUADRANT = 32
 USERS = 128
-USER_TILES = S2 // USERS
 N_TILES = N // P
 LIST_ROWS = 16
-USER_SLICE = 512
 PAIR = 2 * USERS
 WIDE = 4 * USERS
 FIRST_LOAD, SECOND_LOAD = 512, 1152
-GPSIMD_USERS = [464, 312, 200, 96, 64]
 KB = 1024
+PHASES = 5
+TABLE_AT, CODES_AT = 16 * KB, 32 * KB
+USER_CUTS = [0, 256, 512, 1024]
+GPSIMD_USERS = {0: 200, 1: 160, 2: 116, 3: 72, 4: 64}
 
 
 def tile_list_creative_user_readout_kernel(
@@ -47,19 +48,22 @@ def tile_list_creative_user_readout_kernel(
 
         idx = keep.tile([P, S // LIST_ROWS], U16, name="idx")
         idx2 = keep.tile([P, S2 // LIST_ROWS], U16, name="idx2")
-        v_words = [keep.tile([P, T], I32, name="v_words%d" % a, align_bytes=64) for a in range(K_PASSES)]
+        v_words = [
+            shared.tile([P, T], I32, name="v_words%d" % a, align_bytes=64, offset=TABLE_AT + 8 * KB * a) for a in range(K_PASSES)
+        ]
         v2_words = [keep.tile([P, T2], I32, name="v2_words%d" % a, align_bytes=64) for a in range(K_PASSES)]
         v_rows = keep.tile([P, T // 4], I32, name="v_rows", align_bytes=64)
         v2_rows = keep.tile([P, T2 // 4], I32, name="v2_rows", align_bytes=64)
         g_rows = keep.tile([P, PASS], F32, name="g_rows")
-        late_planes = keep.tile([P, (S + S2) // 4], I32, name="late_planes", align_bytes=64)
+        plane_tiles = [keep.tile([P, (S + S2) // 4], I32, name="planes%d" % a, align_bytes=64) for a in range(K_PASSES)]
         w4_planes = keep.tile([P, I_PASSES, N // 4], I32, name="w4_planes", align_bytes=64)
 
         nc.vector.memset(v_rows[:], 0)
         nc.vector.memset(v2_rows[:], 0)
         nc.vector.memset(g_rows[:], 0.0)
-        nc.vector.memset(late_planes[:], 0)
         nc.vector.memset(w4_planes[:], 0)
+        for a in range(K_PASSES):
+            nc.vector.memset(plane_tiles[a][:], 0)
 
         def load_words(tile, words, lo, hi):
             nc.sync.dma_start(out=tile[:, lo:hi], in_=words[:, lo:hi, :].rearrange("p n t -> p (n t)").bitcast(I32))
@@ -86,44 +90,43 @@ def tile_list_creative_user_readout_kernel(
         for t in range(PACK):
             nc.tensor.transpose(gb_bank[:, t, :], g_rows[:, t::PACK], ident[:])
         gb_psum = gb_bank[:, :, 8:16:4].rearrange("p t b -> p b t")
-        g_t = keep.tile([P, 2 * I_PASSES, PACK], F32, name="g_t")
-        nc.scalar.copy(out=g_t[:], in_=gb_bank[:, :, 0:16:4].rearrange("p t b -> p b t"))
-        ga_t = g_t[:, 0:I_PASSES, :]
-        gb_t = g_t[:, I_PASSES : 2 * I_PASSES, :]
+        ga_t = keep.tile([P, I_PASSES, PACK], F32, name="ga_t")
+        nc.scalar.copy(out=ga_t[:], in_=gb_bank[:, :, 0:8:4].rearrange("p t b -> p b t"))
+
+        def room(j, k):
+            return CODES_AT + 2 * KB * (2 * j + k)
+
+        gb_of = []
+        for j in range(PHASES):
+            gains = shared.tile([P, I_PASSES, 16], F32, name="gb%d" % j, align_bytes=64, offset=room(j, 1) - 64)
+            nc.scalar.copy(out=gains[:, :, 0:PACK], in_=gb_psum)
+            gb_of.append(gains[:, :, 0:PACK])
 
         creative_words = [keep.tile([P, S], U32, name="creative_words%d" % a, align_bytes=64) for a in range(K_PASSES)]
         user_words = [keep.tile([P, S2], U32, name="user_words%d" % a, align_bytes=64) for a in range(K_PASSES)]
-        creative_rows = keep.tile([P, S], U8, name="creative_rows", align_bytes=64)
-        user_rows = keep.tile([P, S2], U8, name="user_rows", align_bytes=64)
-        early_planes = keep.tile([P, S + S2], U8, name="early_planes", align_bytes=64)
+        picked_rows = keep.tile([P, S + S2], U8, name="picked_rows", align_bytes=64)
 
-        for lo in range(0, S, PASS):
-            nc.vector.tensor_copy(
-                creative_rows[:, lo : lo + PASS],
-                v_rows[:].bitcast(U8).indirect(idx[:, lo // LIST_ROWS : (lo + PASS) // LIST_ROWS]),
-            )
-        nc.vector.tensor_copy(user_rows[:], v2_rows[:].bitcast(U8).indirect(idx2[:]))
-        for lo in range(0, S, PASS):
-            nc.vector.tensor_copy(
-                early_planes[:, lo : lo + PASS].rearrange("p (t m) -> p t m", t=PACK),
-                creative_rows[:, lo : lo + PASS].rearrange("p (m t) -> p t m", t=PACK),
-            )
-        nc.vector.tensor_copy(early_planes[:, S : S + S2].bitcast(I32), user_rows[:].bitcast(I32))
-        for r in range(1, 4):
-            nc.sync.dma_start(
-                out=early_planes[r:P:QUADRANT, :].bitcast(I32), in_=early_planes[8 * r : P : QUADRANT, :].bitcast(I32)
-            )
+        nc.vector.tensor_copy(
+            picked_rows[:, 0:S].rearrange("p (b t m) -> p b m t", m=P, t=PACK), v_rows[:].bitcast(U8).indirect(idx[:])
+        )
+        nc.vector.tensor_copy(picked_rows[:, S : S + S2], v2_rows[:].bitcast(U8).indirect(idx2[:]))
+
+        def move_rows(a, queue):
+            for r in range(4):
+                queue.dma_start(
+                    out=plane_tiles[a][4 * a + r : P : QUADRANT, :],
+                    in_=picked_rows[8 * r + 4 * a : P : QUADRANT, :].bitcast(I32),
+                )
+
+        move_rows(0, nc.sync)
         load_words(v2_words[1], tab2_words[1], 0, T2)
-        for r in range(4):
-            nc.sync.dma_start(
-                out=late_planes[4 + r : P : QUADRANT, :], in_=early_planes[8 * r + 4 : P : QUADRANT, :].bitcast(I32)
-            )
-        planes = [early_planes[:], late_planes[4:, :].bitcast(U8)]
+        move_rows(1, nc.sync)
+        planes = [plane_tiles[a][4 * a :, :].bitcast(U8) for a in range(K_PASSES)]
 
-        def gather_creatives(a, lo, hi):
+        def gather_creatives(a):
             nc.vector.tensor_copy(
-                creative_words[a][:, lo:hi].rearrange("p (b t m) -> p b m t", m=P, t=PACK),
-                v_words[a][:].bitcast(U32).indirect(idx[:, lo // LIST_ROWS : hi // LIST_ROWS]),
+                creative_words[a][:].rearrange("p (b t m) -> p b m t", m=P, t=PACK),
+                v_words[a][:].bitcast(U32).indirect(idx[:]),
             )
 
         def gather_users(a, lo, hi):
@@ -132,12 +135,15 @@ def tile_list_creative_user_readout_kernel(
             )
 
         gather_users(0, 0, S2)
-        gather_creatives(0, 0, S)
-        gather_creatives(1, 0, S)
-        gather_users(1, 0, USER_SLICE)
-        gather_users(1, USER_SLICE, S2)
+        gather_creatives(0)
+        gather_creatives(1)
+        for lo, hi in zip(USER_CUTS, USER_CUTS[1:]):
+            gather_users(1, lo, hi)
 
-        w1_raw = [keep.tile([P, PACK, N], F32, name="w1_raw%d" % b, align_bytes=64) for b in range(I_PASSES)]
+        w1_raw = [
+            shared.tile([P, PACK, N], F32, name="w1_raw%d" % b, align_bytes=64, offset=TABLE_AT + 8 * KB * b)
+            for b in range(I_PASSES)
+        ]
         w4_codes = keep.tile([P, I_PASSES, N // 2], I32, name="w4_codes", align_bytes=64)
         bias_t = keep.tile([P, N_TILES], F32, name="bias_t", align_bytes=64)
 
@@ -145,23 +151,24 @@ def tile_list_creative_user_readout_kernel(
             nc.sync.dma_start(out=w1_raw[b][:], in_=w1[b * PASS : (b + 1) * PASS, :].rearrange("(p t) n -> p t n", t=PACK))
 
         load_w1(0)
+        load_w1(1)
         nc.sync.dma_start(out=w4_codes[:], in_=w4_words.rearrange("b p c -> p b c").bitcast(I32))
         for q in range(P // QUADRANT):
             nc.sync.dma_start(
                 out=w4_planes[QUADRANT * q : QUADRANT * q + 4, :, :],
                 in_=w4_scales[:, 4 * q : 4 * q + 4, :].rearrange("b r c -> r b c").bitcast(I32),
             )
-        load_w1(1)
         with nc.allow_non_contiguous_dma(reason="one bias value for each partition and output tile"):
             nc.sync.dma_start(out=bias_t[:], in_=bias.rearrange("(c p) -> p c", p=P))
 
-        third, fourth, last = WIDE, WIDE + PAIR, S2 - USERS
-        places = [(b, lo) for b in range(I_PASSES) for lo in range(0, WIDE, USERS)]
-        places.extend((b, lo) for b in range(I_PASSES) for lo in (third, third + USERS))
-        places.extend((b, lo) for lo in (fourth, last) for b in range(I_PASSES))
-        score_banks = list(range(7)) + [0, 2, 3, 0, 1, 1, 2, 3, 1]
-        phases = [range(0, 4), range(4, 8), range(8, 12), range(12, 15), range(15, 16)]
-        phase_of = {n: s for s, members in enumerate(phases) for n in members}
+        groups = [(lo, PAIR) for lo in range(0, S2 - PAIR, PAIR)] + [(lo, USERS) for lo in (S2 - PAIR, S2 - USERS)]
+        places, members = [], []
+        for lo, width in groups:
+            first = len(places)
+            places.extend((b, at) for b in range(I_PASSES) for at in range(lo, lo + width, USERS))
+            members.append(range(first, len(places)))
+        group_of = {n: j for j, group in enumerate(members) for n in group}
+        score_banks = list(range(7)) + [0, 1, 2, 3, 4, 0, 1, 2, 3]
 
         def bank(number):
             return psum.tile([P, PASS], F32, name="bank%d" % number)
@@ -169,27 +176,21 @@ def tile_list_creative_user_readout_kernel(
         def half(name, users, at):
             return shared.tile([P, users, PACK], BF16, name=name, align_bytes=64, offset=at)
 
-        room_b, room_c, room_a, tanh_at = 0, 8 * KB, 12 * KB, 16 * KB
-        tanh = [
-            shared.tile([P, USERS * len(members), PACK], F32, name="tanh%d" % s, align_bytes=64, offset=tanh_at + 8 * KB * s)
-            for s, members in enumerate(phases)
+        tanh = [keep.tile([P, I_PASSES * width, PACK], F32, name="tanh%d" % lo, align_bytes=64) for lo, width in groups]
+        both_0 = half("both_0", 2 * WIDE, 0)
+        w1_bf = [half("w1_bf0", N, 12 * KB), half("w1_bf1", N, 8 * KB)]
+        h1 = [
+            both_0[:, 0:WIDE, :],
+            keep.tile([P, WIDE, PACK], BF16, name="h1_1", align_bytes=64)[:],
+            half("h1_2", WIDE, 12 * KB)[:],
+            half("h1_3", PAIR, 8 * KB)[:],
+            half("h1_4", PAIR, 0)[:],
         ]
-        both_a = half("both_a", 2 * WIDE, room_b)
-        h2_a, h1_a = both_a[:, 0:WIDE, :], both_a[:, WIDE : 2 * WIDE, :]
-        h1_b = keep.tile([P, WIDE, PACK], BF16, name="h1_b", align_bytes=64)
-        w1_bf = [half("w1_bf0", N, room_a), half("w1_bf1", N, room_c)]
-        h1_c = half("h1_c", WIDE, room_a)
-        h1_12 = keep.tile([P, PAIR, PACK], BF16, name="h1_12", align_bytes=64)
-        h2_b = half("h2_b", WIDE, room_b)
-        h1_14 = half("h1_14", PAIR, room_b)
-        h2_c = half("h2_c", WIDE, room_c)
-        h2_d = half("h2_d", PAIR, room_c)
-        h2_14 = half("h2_14", USERS, room_c)
-        h2_15 = half("h2_15", USERS, room_c + KB)
-        h1_of = [h1_a] * 4 + [h1_b] * 4 + [h1_c] * 4 + [h1_12] * 2 + [h1_14] * 2
-        column_of = [0, 1, 2, 3] * 3 + [0, 1] * 2
+        h2 = [both_0[:, WIDE : 2 * WIDE, :]] + [
+            half("h2_%d" % j, I_PASSES * groups[j][1], at)[:] for j, at in ((1, 0), (2, 0), (3, 8 * KB), (4, 8 * KB))
+        ]
 
-        accs, quantised = {}, {}
+        accs, quantised, w1_mx = {}, {}, {}
 
         def multiply(n):
             b, lo = places[n]
@@ -208,38 +209,32 @@ def tile_list_creative_user_readout_kernel(
                         stop=(a == K_PASSES - 1 and t == PACK - 1),
                     )
 
+        def slot(n):
+            at = (n - members[group_of[n]][0]) * USERS
+            return slice(at, at + USERS)
+
         def linear(n):
             b = places[n][0]
-            at = column_of[n] * USERS
             nc.vector.tensor_tensor(
-                h1_of[n][:, at : at + USERS, :],
+                h1[group_of[n]][:, slot(n), :],
                 accs[n][:].rearrange("p (t n) -> p n t", t=PACK),
                 ga_t[:, b : b + 1, :].to_broadcast([P, USERS, PACK]),
                 MULT,
             )
 
         def saturate(n):
-            s = phase_of[n]
-            at = (n - phases[s][0]) * USERS
             nc.scalar.activation(
-                out=tanh[s][:, at : at + USERS, :], in_=accs[n][:].rearrange("p (t n) -> p n t", t=PACK), func=ACT.Tanh
+                out=tanh[group_of[n]][:, slot(n), :], in_=accs[n][:].rearrange("p (t n) -> p n t", t=PACK), func=ACT.Tanh
             )
 
-        def weigh_vector(s, lo, hi, h2, shift=0):
-            b = places[phases[s][lo // USERS]][0]
-            nc.vector.tensor_tensor(
-                h2[:, lo - shift : hi - shift, :],
-                tanh[s][:, lo:hi, :],
-                gb_psum[:, b : b + 1, :].to_broadcast([P, hi - lo, PACK]),
-                MULT,
-            )
+        def weigh(engine, gains, j, lo, hi, first=0, last=I_PASSES):
+            def part(tile):
+                return tile.rearrange("p (b n) t -> p b n t", b=I_PASSES)[:, first:last, lo:hi, :]
 
-        def weigh_gpsimd(s, lo, hi, h2, shift=0):
-            b = places[phases[s][lo // USERS]][0]
-            nc.gpsimd.tensor_tensor(
-                h2[:, lo - shift : hi - shift, :],
-                tanh[s][:, lo:hi, :],
-                gb_t[:, b : b + 1, :].to_broadcast([P, hi - lo, PACK]),
+            engine.tensor_tensor(
+                part(h2[j]),
+                part(tanh[j][:]),
+                gains[:, first:last, :].unsqueeze(2).to_broadcast([P, last - first, hi - lo, PACK]),
                 MULT,
             )
 
@@ -253,19 +248,20 @@ def tile_list_creative_user_readout_kernel(
             nc.vector.quantize_mx(out=codes[:].bitcast(FP8X4), scales=plane[:], in_=h.rearrange("p n t -> p (n t)"))
             return codes, plane
 
-        def name_h(codes, plane, column, g0, members):
-            for e, n in enumerate(members):
-                b, lo = places[n]
-                quantised[g0 + b, lo] = (codes, plane, column + e * USERS)
+        def name_h(codes, plane, column, g0, j):
+            for b in range(I_PASSES):
+                quantised[g0 + b, j] = (codes, plane, column + b * groups[j][1])
 
-        def quantize_h(h, g0, members, at=None):
-            codes, plane = quantize(h[:], "h%d_%d" % (g0, members[0]), at)
-            name_h(codes, plane, 0, g0, members)
+        def quantize_h1(j, at=None):
+            name_h(*quantize(h1[j], "h1_%d" % j, at), 0, 0, j)
 
-        def room(s, k):
-            return tanh_at + 8 * KB * s + 2 * KB * k
+        def quantize_h2(j):
+            name_h(*quantize(h2[j], "h2_%d" % j, None), 0, I_PASSES, j)
 
-        w1_mx = {}
+        def quantize_h2_pass(j, b):
+            width = groups[j][1]
+            codes, plane = quantize(h2[j][:, b * width : (b + 1) * width, :], "h2_%d_%d" % (j, b), None)
+            quantised[I_PASSES + b, j] = (codes, plane, 0)
 
         def round_w1(b):
             for c in range(N_TILES):
@@ -275,23 +271,20 @@ def tile_list_creative_user_readout_kernel(
                 )
 
         def quantize_w1(b, at):
-            codes, plane = quantize(w1_bf[b][:], "w1_%d" % b, at)
-            for c in range(N_TILES):
-                w1_mx[b, c] = (codes[:, c * P : (c + 1) * P], plane[:, c * P : (c + 1) * P])
+            w1_mx[b] = quantize(w1_bf[b][:], "w1_%d" % b, at)
 
-        def readout(g, y, tiles, lo, width, pitch, at, start, stop):
-            b = g % I_PASSES
-            codes, plane, column = quantised[g, lo]
-            for c in tiles:
+        def readout(g, j, y, tiles, start, stop):
+            b, width = g % I_PASSES, groups[j][1]
+            codes, plane, column = quantised[g, j]
+            for place, c in enumerate(tiles):
                 if g < I_PASSES:
-                    w = w1_mx[b, c][0].bitcast(FP8X4)
-                    w_scale = w1_mx[b, c][1]
+                    w = w1_mx[b][0][:, c * P : (c + 1) * P].bitcast(FP8X4)
+                    w_scale = w1_mx[b][1][:, c * P : (c + 1) * P]
                 else:
                     w = w4_codes[:, b, :].bitcast(U8)[:, 2 * c * P : 2 * (c + 1) * P].bitcast(FP4X4)
                     w_scale = w4_planes[:, b, :].bitcast(U8)[:, c * P : (c + 1) * P]
-                place = (c - tiles[0]) * pitch + at
                 nc.tensor.matmul_mx(
-                    out=y[:, place : place + width],
+                    out=y[:, place * width : (place + 1) * width],
                     lhsT=w,
                     lhsT_scale=w_scale,
                     rhs=codes[:, column : column + width].bitcast(FP8X4),
@@ -300,17 +293,15 @@ def tile_list_creative_user_readout_kernel(
                     stop=(stop and c == tiles[-1]),
                 )
 
-        def readout_pair(g, y, tiles, lo, start, stop):
-            if g < I_PASSES:
-                readout(g, y, tiles, lo, PAIR, PAIR, 0, start, stop)
-            else:
-                readout(g, y, tiles, lo, USERS, PAIR, 0, start, False)
-                readout(g, y, tiles, lo + USERS, USERS, PAIR, USERS, False, stop)
+        def passes(j, outputs, order, opens, closes):
+            for y, tiles in outputs:
+                for g in order:
+                    readout(g, j, y, tiles, opens and g == order[0], closes and g == order[-1])
 
         out_tiles = out.rearrange("(c p) j -> p c j", p=P)
 
-        def store_scalar(y, tiles, lo, hi, queue):
-            width = hi - lo
+        def store_scalar(j, y, tiles, queue):
+            lo, width = groups[j]
             res = keep.tile([P, len(tiles), width], F32, name="res%d_%d" % (tiles[0], lo))
             for place, c in enumerate(tiles):
                 nc.scalar.activation(
@@ -319,10 +310,10 @@ def tile_list_creative_user_readout_kernel(
                     func=ACT.Identity,
                     bias=bias_t[:, c : c + 1],
                 )
-            queue.dma_start(out=out_tiles[:, tiles[0] : tiles[-1] + 1, lo:hi], in_=res[:])
+            queue.dma_start(out=out_tiles[:, tiles[0] : tiles[-1] + 1, lo : lo + width], in_=res[:])
 
-        def store_vector(y, tiles, lo, hi):
-            width = hi - lo
+        def store_vector(j, y, tiles):
+            lo, width = groups[j]
             res = keep.tile([P, len(tiles), width], F32, name="res%d_%d" % (tiles[0], lo))
             nc.vector.tensor_tensor(
                 res[:],
@@ -330,136 +321,103 @@ def tile_list_creative_user_readout_kernel(
                 bias_t[:, tiles[0] : tiles[-1] + 1].unsqueeze(2).to_broadcast([P, len(tiles), width]),
                 ADD,
             )
-            nc.sync.dma_start(out=out_tiles[:, tiles[0] : tiles[-1] + 1, lo:hi], in_=res[:])
+            nc.sync.dma_start(out=out_tiles[:, tiles[0] : tiles[-1] + 1, lo : lo + width], in_=res[:])
 
         every = list(range(N_TILES))
         low, high = every[:2], every[2:]
-        wide_y = {}
 
-        def wide(g, tiles, start, stop):
-            for c in tiles:
-                readout(g, wide_y[c], [c], 0, WIDE, WIDE, 0, start, stop)
+        def weigh_gpsimd(j, lo, hi, first=0, last=I_PASSES):
+            weigh(nc.gpsimd, gb_of[j], j, lo, hi, first, last)
 
-        share = GPSIMD_USERS[0]
+        def weigh_vector(j, lo, hi, first=0, last=I_PASSES):
+            weigh(nc.vector, gb_psum, j, lo, hi, first, last)
+
         for n in range(7):
             multiply(n)
-        saturate(0)
-        linear(1)
-        saturate(2)
-        linear(0)
-        saturate(1)
-        multiply(7)
-        multiply(12)
-        linear(3)
-        linear(2)
-        saturate(3)
-        multiply(8)
-        multiply(9)
-        linear(7)
-        saturate(7)
-        multiply(10)
+        for n in members[0]:
+            saturate(n)
+        for n in members[0]:
+            linear(n)
+        weigh_gpsimd(0, 0, USERS, 0, 1)
+        weigh_gpsimd(0, USERS, PAIR, 0, 1)
+        weigh_gpsimd(0, 0, GPSIMD_USERS[0], 1, 2)
+        for n in (7, 8, 9, 10):
+            multiply(n)
         round_w1(0)
-        linear(12)
-        saturate(12)
-        multiply(11)
-        weigh_gpsimd(0, 0, USERS, h2_a)
-        weigh_gpsimd(0, USERS, 3 * USERS, h2_a)
-        weigh_gpsimd(0, 3 * USERS, share, h2_a)
-        for n in (4, 5):
+        for n in (4, 5, 6):
             linear(n)
             saturate(n)
-        if share < WIDE:
-            weigh_vector(0, share, WIDE, h2_a)
-        linear(6)
-        saturate(6)
-        quantize_w1(0, None)
-        codes, plane = quantize(both_a[:], "first", None)
-        name_h(codes, plane, 0, I_PASSES, phases[0])
-        name_h(codes, plane, WIDE, 0, phases[0])
-        quantize_h(h1_b, 0, phases[1], room(0, 0))
-        for c in every[:3]:
-            wide_y[c] = bank(4 + c)
-        wide(2, every[:3], True, False)
-        wide(0, every[:3], False, False)
-
-        share = GPSIMD_USERS[1]
-        saturate(8)
-        linear(11)
-        saturate(11)
-        weigh_gpsimd(1, 0, share, h2_b)
-        linear(9)
-        saturate(9)
-        linear(8)
-        weigh_vector(1, share, WIDE, h2_b)
-        linear(10)
-        multiply(15)
-        multiply(14)
-        multiply(13)
+        weigh_vector(0, GPSIMD_USERS[0], PAIR, 1, 2)
+        linear(7)
+        saturate(7)
+        multiply(11)
+        multiply(12)
+        quantize_w1(0, room(0, 0))
+        codes, plane = quantize(both_0[:], "first", None)
+        name_h(codes, plane, 0, 0, 0)
+        name_h(codes, plane, WIDE, I_PASSES, 0)
+        quantize_h1(1, room(0, 1))
+        first = [(bank(5), low), (bank(6), high)]
         round_w1(1)
-        saturate(10)
-        quantize_h(h2_b, I_PASSES, phases[1])
-        quantize_h(h1_c, 0, phases[2], room(1, 0))
-        quantize_w1(1, room(1, 1))
-        wide(3, every[:3], False, False)
-        wide_y[3] = bank(0)
-        for g in (2, 0, 3):
-            wide(g, [3], g == 2, False)
-        wide(1, every, False, True)
 
-        share = GPSIMD_USERS[2]
-        linear(14)
-        saturate(13)
-        saturate(15)
+        weigh_gpsimd(1, 0, GPSIMD_USERS[1])
+        for n in (8, 9, 10):
+            linear(n)
+        weigh_vector(1, GPSIMD_USERS[1], PAIR)
+        linear(11)
+        passes(0, first, [0], True, False)
+        passes(0, first, [2, 3], False, False)
+        for n in members[2]:
+            saturate(n)
+        quantize_w1(1, room(1, 0))
+        quantize_h2(1)
+        quantize_h1(2, room(1, 1))
+        passes(0, first, [1], False, True)
+        for n in (13, 14, 15):
+            multiply(n)
+        second = [(bank(4), low), (bank(5), high)]
+
+        weigh_gpsimd(2, 0, GPSIMD_USERS[2])
+        for n in members[3]:
+            linear(n)
+            saturate(n)
+        weigh_vector(2, GPSIMD_USERS[2], PAIR)
+        for y, tiles in first:
+            store_scalar(0, y, tiles, nc.sync)
+        passes(1, second, [0, 1, 2, 3], True, True)
         saturate(14)
-        weigh_gpsimd(2, 0, share, h2_c)
-        if share < PAIR:
-            weigh_vector(2, share, PAIR, h2_c)
-        weigh_vector(2, PAIR, WIDE, h2_c)
-        linear(13)
-        for c in every:
-            store_scalar(wide_y[c], [c], 0, WIDE, nc.sync)
-        pair = [(bank(3), low), (bank(4), high)]
-        for y, tiles in pair:
-            for g in range(I_PASSES):
-                readout_pair(g, y, tiles, third, g == 0, False)
-        quantize_h(h2_c, I_PASSES, phases[2])
-        quantize_h(h1_12, 0, [12, 13], room(2, 1))
-        for y, tiles in pair:
-            for g in range(I_PASSES, 2 * I_PASSES):
-                readout_pair(g, y, tiles, third, False, g == 3)
-        sixth = bank(2)
-        for g in range(I_PASSES):
-            readout(g, sixth, every, fourth, USERS, USERS, 0, g == 0, False)
-        for y, tiles in pair:
-            store_scalar(y, tiles, third, fourth, nc.sync)
+        saturate(15)
+        quantize_h1(3, room(2, 0))
+        quantize_h2(2)
+        third = [(bank(6), low), (bank(0), high)]
+        passes(2, third, [0, 1], True, False)
 
-        share = GPSIMD_USERS[3]
-        weigh_gpsimd(3, 0, share, h2_d)
-        weigh_vector(3, USERS, PAIR, h2_d)
-        if share < USERS:
-            weigh_vector(3, share, USERS, h2_d)
+        weigh_gpsimd(3, 0, GPSIMD_USERS[3])
+        weigh_vector(3, GPSIMD_USERS[3], USERS)
+        linear(14)
         linear(15)
-        quantize_h(h2_d, I_PASSES, [12, 13])
-        quantize_h(h1_14, 0, [14, 15])
-        for g in range(I_PASSES, 2 * I_PASSES):
-            readout(g, sixth, every, fourth, USERS, USERS, 0, False, g == 3)
-        ends = [(bank(number), [c]) for c, number in enumerate((5, 6, 0, 1))]
-        for g in range(I_PASSES):
-            for y, tiles in ends:
-                readout(g, y, tiles, last, USERS, USERS, 0, g == 0, False)
-        store_scalar(sixth, low, fourth, last, nc.sync)
-        store_scalar(sixth[:, PAIR:PASS], high, fourth, last, nc.sync)
+        for y, tiles in second:
+            store_scalar(1, y, tiles, nc.sync)
+        passes(2, third, [2, 3], False, True)
+        quantize_h2(3)
+        quantize_h1(4, room(3, 0))
+        fourth = [(bank(1), low), (bank(4), high)]
+        passes(3, fourth, [0, 1], True, False)
+        passes(3, fourth, [2, 3], False, True)
+        for y, tiles in third:
+            store_scalar(2, y, tiles, nc.sync)
 
-        share = GPSIMD_USERS[4]
-        weigh_gpsimd(3, PAIR, PAIR + share, h2_14, PAIR)
-        weigh_vector(4, 0, USERS, h2_15)
-        weigh_vector(3, PAIR + share, PAIR + USERS, h2_14, PAIR)
-        quantize_h(h2_15, I_PASSES, [15])
-        quantize_h(h2_14, I_PASSES, [14])
-        for g in (3, 2):
-            for y, tiles in ends:
-                readout(g, y, tiles, last, USERS, USERS, 0, False, g == 2)
-        store_scalar(ends[0][0], [0], last, S2, nc.sync)
-        store_vector(ends[1][0], [1], last, S2)
-        store_scalar(ends[2][0], [2], last, S2, nc.scalar)
-        store_vector(ends[3][0], [3], last, S2)
+        weigh_gpsimd(4, 0, GPSIMD_USERS[4], 1, 2)
+        weigh_vector(4, 0, USERS, 0, 1)
+        weigh_vector(4, GPSIMD_USERS[4], USERS, 1, 2)
+        quantize_h2_pass(4, 0)
+        quantize_h2_pass(4, 1)
+        ends = [(bank(number), [c]) for c, number in enumerate((2, 3, 5, 6))]
+        for g in range(2 * I_PASSES):
+            passes(4, ends, [g], g == 0, g == 3)
+        for y, tiles in fourth:
+            store_scalar(3, y, tiles, nc.sync)
+        store_scalar(4, ends[0][0], [0], nc.sync)
+        store_vector(4, ends[1][0], [1])
+        store_scalar(4, ends[2][0], [2], nc.scalar)
+        store_vector(4, ends[3][0], [3])

@@ -55,15 +55,14 @@ def tile_list_creative_user_readout_kernel(
         v_rows = keep.tile([P, T // 4], I32, name="v_rows", align_bytes=64)
         v2_rows = keep.tile([P, T2 // 4], I32, name="v2_rows", align_bytes=64)
         g_rows = keep.tile([P, PASS], F32, name="g_rows")
-        plane_tiles = [keep.tile([P, (S + S2) // 4], I32, name="planes%d" % a, align_bytes=64) for a in range(K_PASSES)]
+        late_planes = keep.tile([P, (S + S2) // 4], I32, name="late_planes", align_bytes=64)
         w4_planes = keep.tile([P, I_PASSES, N // 4], I32, name="w4_planes", align_bytes=64)
 
         nc.vector.memset(v_rows[:], 0)
         nc.vector.memset(v2_rows[:], 0)
         nc.vector.memset(g_rows[:], 0.0)
+        nc.vector.memset(late_planes[:], 0)
         nc.vector.memset(w4_planes[:], 0)
-        for a in range(K_PASSES):
-            nc.vector.memset(plane_tiles[a][:], 0)
 
         def load_words(tile, words, lo, hi):
             nc.sync.dma_start(out=tile[:, lo:hi], in_=words[:, lo:hi, :].rearrange("p n t -> p (n t)").bitcast(I32))
@@ -104,24 +103,32 @@ def tile_list_creative_user_readout_kernel(
 
         creative_words = [keep.tile([P, S], U32, name="creative_words%d" % a, align_bytes=64) for a in range(K_PASSES)]
         user_words = [keep.tile([P, S2], U32, name="user_words%d" % a, align_bytes=64) for a in range(K_PASSES)]
-        picked_rows = keep.tile([P, S + S2], U8, name="picked_rows", align_bytes=64)
+        creative_rows = keep.tile([P, S], U8, name="creative_rows", align_bytes=64)
+        user_rows = keep.tile([P, S2], U8, name="user_rows", align_bytes=64)
+        early_planes = keep.tile([P, S + S2], U8, name="early_planes", align_bytes=64)
 
-        nc.vector.tensor_copy(
-            picked_rows[:, 0:S].rearrange("p (b t m) -> p b m t", m=P, t=PACK), v_rows[:].bitcast(U8).indirect(idx[:])
-        )
-        nc.vector.tensor_copy(picked_rows[:, S : S + S2], v2_rows[:].bitcast(U8).indirect(idx2[:]))
-
-        def move_rows(a, queue):
-            for r in range(4):
-                queue.dma_start(
-                    out=plane_tiles[a][4 * a + r : P : QUADRANT, :],
-                    in_=picked_rows[8 * r + 4 * a : P : QUADRANT, :].bitcast(I32),
-                )
-
-        move_rows(0, nc.sync)
+        for lo in range(0, S, PASS):
+            nc.vector.tensor_copy(
+                creative_rows[:, lo : lo + PASS],
+                v_rows[:].bitcast(U8).indirect(idx[:, lo // LIST_ROWS : (lo + PASS) // LIST_ROWS]),
+            )
+        nc.vector.tensor_copy(user_rows[:], v2_rows[:].bitcast(U8).indirect(idx2[:]))
+        for lo in range(0, S, PASS):
+            nc.vector.tensor_copy(
+                early_planes[:, lo : lo + PASS].rearrange("p (t m) -> p t m", t=PACK),
+                creative_rows[:, lo : lo + PASS].rearrange("p (m t) -> p t m", t=PACK),
+            )
+        nc.vector.tensor_copy(early_planes[:, S : S + S2].bitcast(I32), user_rows[:].bitcast(I32))
+        for r in range(1, 4):
+            nc.sync.dma_start(
+                out=early_planes[r:P:QUADRANT, :].bitcast(I32), in_=early_planes[8 * r : P : QUADRANT, :].bitcast(I32)
+            )
         load_words(v2_words[1], tab2_words[1], 0, T2)
-        move_rows(1, nc.sync)
-        planes = [plane_tiles[a][4 * a :, :].bitcast(U8) for a in range(K_PASSES)]
+        for r in range(4):
+            nc.sync.dma_start(
+                out=late_planes[4 + r : P : QUADRANT, :], in_=early_planes[8 * r + 4 : P : QUADRANT, :].bitcast(I32)
+            )
+        planes = [early_planes[:], late_planes[4:, :].bitcast(U8)]
 
         def gather_creatives(a):
             nc.vector.tensor_copy(

@@ -34,7 +34,7 @@ KB = 1024
 PHASES = 5
 TABLE_AT, CODES_AT = 16 * KB, 32 * KB
 USER_CUTS = [0, 256, 512, 1024]
-GPSIMD_USERS = {0: 200, 1: 160, 2: 116, 3: 72, 4: 64}
+GPSIMD_USERS = {0: 200, 1: 160, 2: 116, 3: 52, 4: 64}
 
 
 def tile_list_creative_user_readout_kernel(
@@ -229,6 +229,18 @@ def tile_list_creative_user_readout_kernel(
                 MULT,
             )
 
+        def linear_scalar(n):
+            b = places[n][0]
+            apart = keep.tile([P, PACK, USERS], BF16, name="apart%d" % n, align_bytes=64)
+            for t in range(PACK):
+                nc.scalar.activation(
+                    out=apart[:, t, :], in_=accs[n][:, t * USERS : (t + 1) * USERS], func=ACT.Copy, scale=ga_t[:, b, t : t + 1]
+                )
+            nc.scalar.copy(
+                out=h1[group_of[n]][:, slot(n), :].rearrange("p (g i) t -> p g t i", i=4),
+                in_=apart[:].rearrange("p t (g i) -> p g t i", i=4),
+            )
+
         def saturate(n):
             nc.scalar.activation(
                 out=tanh[group_of[n]][:, slot(n), :], in_=accs[n][:].rearrange("p (t n) -> p n t", t=PACK), func=ACT.Tanh
@@ -368,10 +380,9 @@ def tile_list_creative_user_readout_kernel(
         round_w1(1)
 
         weigh_gpsimd(1, 0, GPSIMD_USERS[1])
-        for n in (8, 9, 10):
+        for n in members[2]:
             linear(n)
         weigh_vector(1, GPSIMD_USERS[1], PAIR)
-        linear(11)
         passes(0, first, [0], True, False)
         passes(0, first, [2, 3], False, False)
         for n in members[2]:
@@ -402,7 +413,7 @@ def tile_list_creative_user_readout_kernel(
         weigh_gpsimd(3, 0, GPSIMD_USERS[3])
         weigh_vector(3, GPSIMD_USERS[3], USERS)
         linear(14)
-        linear(15)
+        linear_scalar(15)
         for y, tiles in second:
             store_scalar(1, y, tiles, nc.sync)
         passes(2, third, [2, 3], False, True)

@@ -92,6 +92,9 @@ def tile_list_creative_user_readout_kernel(
         ga_t = keep.tile([P, I_PASSES, PACK], F32, name="ga_t")
         nc.scalar.copy(out=ga_t[:], in_=gb_bank[:, :, 0:8:4].rearrange("p t b -> p b t"))
 
+        ga_users = keep.tile([P, I_PASSES, USERS, PACK], F32, name="ga_users", align_bytes=64)
+        nc.scalar.copy(out=ga_users[:], in_=ga_t[:].unsqueeze(2).to_broadcast([P, I_PASSES, USERS, PACK]))
+
         def room(j, k):
             return CODES_AT + 2 * KB * (2 * j + k)
 
@@ -225,7 +228,7 @@ def tile_list_creative_user_readout_kernel(
             nc.vector.tensor_tensor(
                 h1[group_of[n]][:, slot(n), :],
                 accs[n][:].rearrange("p (t n) -> p n t", t=PACK),
-                ga_t[:, b : b + 1, :].to_broadcast([P, USERS, PACK]),
+                ga_users[:, b, :, :],
                 MULT,
             )
 

@@ -29,7 +29,7 @@ N_TILES = N // P
 LIST_ROWS = 16
 PAIR = 2 * USERS
 WIDE = 4 * USERS
-FIRST_LOAD, SECOND_LOAD = 512, 1152
+FIRST_LOAD = 1536
 KB = 1024
 PHASES = 5
 TABLE_AT, CODES_AT = 16 * KB, 32 * KB
@@ -68,21 +68,20 @@ def tile_list_creative_user_readout_kernel(
             nc.sync.dma_start(out=tile[:, lo:hi], in_=words[:, lo:hi, :].rearrange("p n t -> p (n t)").bitcast(I32))
 
         def load_rows(tile, scales):
-            nc.sync.dma_start(out=tile[0:P:4, :], in_=scales.rearrange("a q n -> q a n").bitcast(I32))
+            nc.scalar.dma_start(out=tile[0:P:4, :], in_=scales.rearrange("a q n -> q a n").bitcast(I32))
 
         ident = keep.tile([P, P], F32, name="ident")
         make_identity(nc, ident[:])
 
-        load_words(v2_words[0], tab2_words[0], 0, FIRST_LOAD)
-        load_rows(v_rows, tab_scales)
         nc.sync.dma_start(idx[:], offs)
         nc.sync.dma_start(idx2[:], offs2)
-        load_words(v2_words[0], tab2_words[0], FIRST_LOAD, SECOND_LOAD)
+        load_words(v2_words[0], tab2_words[0], 0, FIRST_LOAD)
+        load_rows(v_rows, tab_scales)
         load_rows(v2_rows, tab2_scales)
-        load_words(v2_words[0], tab2_words[0], SECOND_LOAD, T2)
+        load_words(v2_words[0], tab2_words[0], FIRST_LOAD, T2)
         load_words(v_words[0], tab_words[0], 0, T)
         for first, g in ((0, ga), (8, gb)):
-            nc.sync.dma_start(out=g_rows[first : first + 8 : 4, :], in_=g.rearrange("(b i) -> b i", b=I_PASSES))
+            nc.scalar.dma_start(out=g_rows[first : first + 8 : 4, :], in_=g.rearrange("(b i) -> b i", b=I_PASSES))
         load_words(v_words[1], tab_words[1], 0, T)
 
         gb_bank = psum.tile([P, PACK, P], F32, name="gb_bank")
@@ -110,17 +109,12 @@ def tile_list_creative_user_readout_kernel(
         user_rows = keep.tile([P, S2], U8, name="user_rows", align_bytes=64)
         early_planes = keep.tile([P, S + S2], U8, name="early_planes", align_bytes=64)
 
-        for lo in range(0, S, PASS):
-            nc.vector.tensor_copy(
-                creative_rows[:, lo : lo + PASS],
-                v_rows[:].bitcast(U8).indirect(idx[:, lo // LIST_ROWS : (lo + PASS) // LIST_ROWS]),
-            )
+        nc.vector.tensor_copy(creative_rows[:], v_rows[:].bitcast(U8).indirect(idx[:]))
         nc.vector.tensor_copy(user_rows[:], v2_rows[:].bitcast(U8).indirect(idx2[:]))
-        for lo in range(0, S, PASS):
-            nc.vector.tensor_copy(
-                early_planes[:, lo : lo + PASS].rearrange("p (t m) -> p t m", t=PACK),
-                creative_rows[:, lo : lo + PASS].rearrange("p (m t) -> p t m", t=PACK),
-            )
+        nc.vector.tensor_copy(
+            early_planes[:, 0:S].rearrange("p (b t m) -> p b t m", b=I_PASSES, t=PACK),
+            creative_rows[:].rearrange("p (b m t) -> p b t m", b=I_PASSES, t=PACK),
+        )
         nc.vector.tensor_copy(early_planes[:, S : S + S2].bitcast(I32), user_rows[:].bitcast(I32))
         for r in range(1, 4):
             nc.sync.dma_start(

@@ -29,7 +29,7 @@ N_TILES = N // P
 LIST_ROWS = 16
 PAIR = 2 * USERS
 WIDE = 4 * USERS
-FIRST_LOAD = 1536
+FIRST_LOAD = 1024
 KB = 1024
 PHASES = 5
 TABLE_AT, CODES_AT = 16 * KB, 32 * KB
@@ -68,20 +68,20 @@ def tile_list_creative_user_readout_kernel(
             nc.sync.dma_start(out=tile[:, lo:hi], in_=words[:, lo:hi, :].rearrange("p n t -> p (n t)").bitcast(I32))
 
         def load_rows(tile, scales):
-            nc.scalar.dma_start(out=tile[0:P:4, :], in_=scales.rearrange("a q n -> q a n").bitcast(I32))
+            nc.sync.dma_start(out=tile[0:P:4, :], in_=scales.rearrange("a q n -> q a n").bitcast(I32))
 
         ident = keep.tile([P, P], F32, name="ident")
         make_identity(nc, ident[:])
 
-        nc.sync.dma_start(idx[:], offs)
-        nc.sync.dma_start(idx2[:], offs2)
         load_words(v2_words[0], tab2_words[0], 0, FIRST_LOAD)
         load_rows(v_rows, tab_scales)
+        nc.sync.dma_start(idx[:], offs)
+        nc.sync.dma_start(idx2[:], offs2)
         load_rows(v2_rows, tab2_scales)
         load_words(v2_words[0], tab2_words[0], FIRST_LOAD, T2)
         load_words(v_words[0], tab_words[0], 0, T)
         for first, g in ((0, ga), (8, gb)):
-            nc.scalar.dma_start(out=g_rows[first : first + 8 : 4, :], in_=g.rearrange("(b i) -> b i", b=I_PASSES))
+            nc.sync.dma_start(out=g_rows[first : first + 8 : 4, :], in_=g.rearrange("(b i) -> b i", b=I_PASSES))
         load_words(v_words[1], tab_words[1], 0, T)
 
         gb_bank = psum.tile([P, PACK, P], F32, name="gb_bank")

@@ -29,7 +29,7 @@ N_TILES = N // P
 LIST_ROWS = 16
 PAIR = 2 * USERS
 WIDE = 4 * USERS
-FIRST_LOAD = 1024
+FIRST_LOAD, SECOND_LOAD = 512, 1664
 KB = 1024
 PHASES = 5
 TABLE_AT, CODES_AT = 16 * KB, 32 * KB
@@ -54,7 +54,7 @@ def tile_list_creative_user_readout_kernel(
         v2_words = [keep.tile([P, T2], I32, name="v2_words%d" % a, align_bytes=64) for a in range(K_PASSES)]
         v_rows = keep.tile([P, T // 4], I32, name="v_rows", align_bytes=64)
         v2_rows = keep.tile([P, T2 // 4], I32, name="v2_rows", align_bytes=64)
-        g_rows = keep.tile([P, PASS], F32, name="g_rows")
+        g_rows = keep.tile([P, PASS], F32, name="g_rows", tag="rows_then_planes", align_bytes=64)
         late_planes = keep.tile([P, (S + S2) // 4], I32, name="late_planes", align_bytes=64)
         w4_planes = keep.tile([P, I_PASSES, N // 4], I32, name="w4_planes", align_bytes=64)
 
@@ -77,11 +77,12 @@ def tile_list_creative_user_readout_kernel(
         load_rows(v_rows, tab_scales)
         nc.sync.dma_start(idx[:], offs)
         nc.sync.dma_start(idx2[:], offs2)
+        load_words(v2_words[0], tab2_words[0], FIRST_LOAD, SECOND_LOAD)
         load_rows(v2_rows, tab2_scales)
-        load_words(v2_words[0], tab2_words[0], FIRST_LOAD, T2)
-        load_words(v_words[0], tab_words[0], 0, T)
         for first, g in ((0, ga), (8, gb)):
             nc.sync.dma_start(out=g_rows[first : first + 8 : 4, :], in_=g.rearrange("(b i) -> b i", b=I_PASSES))
+        load_words(v2_words[0], tab2_words[0], SECOND_LOAD, T2)
+        load_words(v_words[0], tab_words[0], 0, T)
         load_words(v_words[1], tab_words[1], 0, T)
 
         gb_bank = psum.tile([P, PACK, P], F32, name="gb_bank")
@@ -107,7 +108,7 @@ def tile_list_creative_user_readout_kernel(
         user_words = [keep.tile([P, S2], U32, name="user_words%d" % a, align_bytes=64) for a in range(K_PASSES)]
         creative_rows = keep.tile([P, S], U8, name="creative_rows", align_bytes=64)
         user_rows = keep.tile([P, S2], U8, name="user_rows", align_bytes=64)
-        early_planes = keep.tile([P, S + S2], U8, name="early_planes", align_bytes=64)
+        early_planes = keep.tile([P, S + S2], U8, name="early_planes", tag="rows_then_planes", align_bytes=64)
 
         nc.vector.tensor_copy(creative_rows[:], v_rows[:].bitcast(U8).indirect(idx[:]))
         nc.vector.tensor_copy(user_rows[:], v2_rows[:].bitcast(U8).indirect(idx2[:]))

@@ -369,7 +369,7 @@ def tile_list_creative_user_readout_kernel(
         saturate(7)
         multiply(11)
         multiply(12)
-        quantize_w1(0, room(0, 0))
+        quantize_w1(0, None)
         codes, plane = quantize(both_0[:], "first", None)
         name_h(codes, plane, 0, 0, 0)
         name_h(codes, plane, WIDE, I_PASSES, 0)
@@ -385,28 +385,33 @@ def tile_list_creative_user_readout_kernel(
         passes(0, first, [2, 3], False, False)
         for n in members[2]:
             saturate(n)
-        quantize_w1(1, room(1, 0))
+        quantize_w1(1, None)
         quantize_h2(1)
         quantize_h1(2, room(1, 1))
-        passes(0, first, [1], False, True)
         for n in (13, 14, 15):
             multiply(n)
-        second = [(bank(4), low), (bank(5), high)]
+        second = [(bank(4), low)]
+        passes(1, second, [0], True, False)
+        passes(0, first, [1], False, True)
+        passes(1, second, [1, 2, 3], False, True)
+        second.append((bank(5), high))
 
         weigh_gpsimd(2, 0, GPSIMD_USERS[2])
+        for y, tiles in first:
+            store_scalar(0, y, tiles, nc.sync)
         for n in members[3]:
             linear(n)
             saturate(n)
         weigh_vector(2, GPSIMD_USERS[2], PAIR)
-        for y, tiles in first:
-            store_scalar(0, y, tiles, nc.sync)
-        passes(1, second, [0, 1, 2, 3], True, True)
+        passes(1, second[1:], [0, 1, 2, 3], True, True)
         saturate(14)
         saturate(15)
         quantize_h1(3, room(2, 0))
         quantize_h2(2)
         third = [(bank(6), low), (bank(0), high)]
         passes(2, third, [0, 1], True, False)
+        fourth = [(bank(1), low)]
+        passes(3, fourth, [0, 1], True, False)
 
         weigh_gpsimd(3, 0, GPSIMD_USERS[3])
         weigh_vector(3, GPSIMD_USERS[3], USERS)
@@ -417,8 +422,8 @@ def tile_list_creative_user_readout_kernel(
         passes(2, third, [2, 3], False, True)
         quantize_h2(3)
         quantize_h1(4, room(3, 0))
-        fourth = [(bank(1), low), (bank(4), high)]
-        passes(3, fourth, [0, 1], True, False)
+        fourth.append((bank(4), high))
+        passes(3, fourth[1:], [0, 1], True, False)
         passes(3, fourth, [2, 3], False, True)
         for y, tiles in third:
             store_scalar(2, y, tiles, nc.sync)

@@ -34,7 +34,7 @@ KB = 1024
 PHASES = 5
 TABLE_AT, CODES_AT = 16 * KB, 32 * KB
 USER_CUTS = [0, 256, 512, 1024]
-GPSIMD_USERS = {0: 200, 1: 160, 2: 116, 3: 52, 4: 64}
+GPSIMD_USERS = {0: 220, 1: 168, 2: 116, 3: 52, 4: 64}
 
 
 def tile_list_creative_user_readout_kernel(

from contextlib import ExitStack

import concourse.mybir as mybir
from concourse.masks import make_identity

K, T, S, T2, S2, N = 1024, 2048, 1024, 4096, 1024, 512
FLOPS = 2 * K * S * S2 + 2 * 2 * S * N * S2

F32 = mybir.dt.float32
BF16 = mybir.dt.bfloat16
I32 = mybir.dt.int32
U32 = mybir.dt.uint32
U16 = mybir.dt.uint16
U8 = mybir.dt.uint8
FP8X4 = mybir.dt.float8_e4m3fn_x4
FP4X4 = mybir.dt.float4_e2m1fn_x4
ACT = mybir.ActivationFunctionType
MULT = mybir.AluOpType.mult
ADD = mybir.AluOpType.add

P = 128
PACK = 4
PASS = P * PACK
K_PASSES = K // PASS
I_PASSES = S // PASS
QUADRANT = 32
USERS = 128
N_TILES = N // P
LIST_ROWS = 16
PAIR = 2 * USERS
WIDE = 4 * USERS
FIRST_LOAD, SECOND_LOAD = 512, 1664
KB = 1024
PHASES = 5
TABLE_AT, CODES_AT = 16 * KB, 32 * KB
USER_CUTS = [0, 256, 512, 1024]
GPSIMD_USERS = {0: 220, 1: 168, 2: 116, 3: 52, 4: 64}


def tile_list_creative_user_readout_kernel(
    tc, tab_words, tab_scales, tab2_words, tab2_scales, offs, offs2, ga, gb, w1, w4_words, w4_scales, bias, out
):
    nc = tc.nc
    with ExitStack() as ctx:
        keep = ctx.enter_context(tc.tile_pool(name="keep", bufs=1))
        shared = ctx.enter_context(tc.tile_pool(name="shared", bufs=1))
        psum = ctx.enter_context(tc.psum_pool(name="psum", bufs=1))

        idx = keep.tile([P, S // LIST_ROWS], U16, name="idx")
        idx2 = keep.tile([P, S2 // LIST_ROWS], U16, name="idx2")
        v_words = [
            shared.tile([P, T], I32, name="v_words%d" % a, align_bytes=64, offset=TABLE_AT + 8 * KB * a) for a in range(K_PASSES)
        ]
        v2_words = [keep.tile([P, T2], I32, name="v2_words%d" % a, align_bytes=64) for a in range(K_PASSES)]
        v_rows = keep.tile([P, T // 4], I32, name="v_rows", align_bytes=64)
        v2_rows = keep.tile([P, T2 // 4], I32, name="v2_rows", align_bytes=64)
        g_rows = keep.tile([P, PASS], F32, name="g_rows", tag="rows_then_planes", align_bytes=64)
        late_planes = keep.tile([P, (S + S2) // 4], I32, name="late_planes", align_bytes=64)
        w4_planes = keep.tile([P, I_PASSES, N // 4], I32, name="w4_planes", align_bytes=64)

        nc.vector.memset(v_rows[:], 0)
        nc.vector.memset(v2_rows[:], 0)
        nc.vector.memset(g_rows[:], 0.0)
        nc.vector.memset(late_planes[:], 0)
        nc.vector.memset(w4_planes[:], 0)

        def load_words(tile, words, lo, hi):
            nc.sync.dma_start(out=tile[:, lo:hi], in_=words[:, lo:hi, :].rearrange("p n t -> p (n t)").bitcast(I32))

        def load_rows(tile, scales):
            nc.sync.dma_start(out=tile[0:P:4, :], in_=scales.rearrange("a q n -> q a n").bitcast(I32))

        ident = keep.tile([P, P], F32, name="ident")
        make_identity(nc, ident[:])

        load_words(v2_words[0], tab2_words[0], 0, FIRST_LOAD)
        load_rows(v_rows, tab_scales)
        nc.sync.dma_start(idx[:], offs)
        nc.sync.dma_start(idx2[:], offs2)
        load_words(v2_words[0], tab2_words[0], FIRST_LOAD, SECOND_LOAD)
        load_rows(v2_rows, tab2_scales)
        for first, g in ((0, ga), (8, gb)):
            nc.sync.dma_start(out=g_rows[first : first + 8 : 4, :], in_=g.rearrange("(b i) -> b i", b=I_PASSES))
        load_words(v2_words[0], tab2_words[0], SECOND_LOAD, T2)
        load_words(v_words[0], tab_words[0], 0, T)
        load_words(v_words[1], tab_words[1], 0, T)

        gb_bank = psum.tile([P, PACK, P], F32, name="gb_bank")
        for t in range(PACK):
            nc.tensor.transpose(gb_bank[:, t, :], g_rows[:, t::PACK], ident[:])
        gb_psum = gb_bank[:, :, 8:16:4].rearrange("p t b -> p b t")
        ga_t = keep.tile([P, I_PASSES, PACK], F32, name="ga_t")
        nc.scalar.copy(out=ga_t[:], in_=gb_bank[:, :, 0:8:4].rearrange("p t b -> p b t"))

        ga_users = keep.tile([P, I_PASSES, USERS, PACK], F32, name="ga_users", align_bytes=64)
        nc.scalar.copy(out=ga_users[:], in_=ga_t[:].unsqueeze(2).to_broadcast([P, I_PASSES, USERS, PACK]))

        def room(j, k):
            return CODES_AT + 2 * KB * (2 * j + k)

        gb_of = []
        for j in range(PHASES):
            gains = shared.tile([P, I_PASSES, 16], F32, name="gb%d" % j, align_bytes=64, offset=room(j, 1) - 64)
            nc.scalar.copy(out=gains[:, :, 0:PACK], in_=gb_psum)
            gb_of.append(gains[:, :, 0:PACK])

        creative_words = [keep.tile([P, S], U32, name="creative_words%d" % a, align_bytes=64) for a in range(K_PASSES)]
        user_words = [keep.tile([P, S2], U32, name="user_words%d" % a, align_bytes=64) for a in range(K_PASSES)]
        creative_rows = keep.tile([P, S], U8, name="creative_rows", align_bytes=64)
        user_rows = keep.tile([P, S2], U8, name="user_rows", align_bytes=64)
        early_planes = keep.tile([P, S + S2], U8, name="early_planes", tag="rows_then_planes", align_bytes=64)

        nc.vector.tensor_copy(creative_rows[:], v_rows[:].bitcast(U8).indirect(idx[:]))
        nc.vector.tensor_copy(user_rows[:], v2_rows[:].bitcast(U8).indirect(idx2[:]))
        nc.vector.tensor_copy(
            early_planes[:, 0:S].rearrange("p (b t m) -> p b t m", b=I_PASSES, t=PACK),
            creative_rows[:].rearrange("p (b m t) -> p b t m", b=I_PASSES, t=PACK),
        )
        nc.vector.tensor_copy(early_planes[:, S : S + S2].bitcast(I32), user_rows[:].bitcast(I32))
        for r in range(1, 4):
            nc.sync.dma_start(
                out=early_planes[r:P:QUADRANT, :].bitcast(I32), in_=early_planes[8 * r : P : QUADRANT, :].bitcast(I32)
            )
        load_words(v2_words[1], tab2_words[1], 0, T2)
        for r in range(4):
            nc.sync.dma_start(
                out=late_planes[4 + r : P : QUADRANT, :], in_=early_planes[8 * r + 4 : P : QUADRANT, :].bitcast(I32)
            )
        planes = [early_planes[:], late_planes[4:, :].bitcast(U8)]

        def gather_creatives(a):
            nc.vector.tensor_copy(
                creative_words[a][:].rearrange("p (b t m) -> p b m t", m=P, t=PACK),
                v_words[a][:].bitcast(U32).indirect(idx[:]),
            )

        def gather_users(a, lo, hi):
            nc.vector.tensor_copy(
                user_words[a][:, lo:hi], v2_words[a][:].bitcast(U32).indirect(idx2[:, lo // LIST_ROWS : hi // LIST_ROWS])
            )

        gather_users(0, 0, S2)
        gather_creatives(0)
        gather_creatives(1)
        for lo, hi in zip(USER_CUTS, USER_CUTS[1:]):
            gather_users(1, lo, hi)

        w1_raw = [
            shared.tile([P, PACK, N], F32, name="w1_raw%d" % b, align_bytes=64, offset=TABLE_AT + 8 * KB * b)
            for b in range(I_PASSES)
        ]
        w4_codes = keep.tile([P, I_PASSES, N // 2], I32, name="w4_codes", align_bytes=64)
        bias_t = keep.tile([P, N_TILES], F32, name="bias_t", align_bytes=64)

        def load_w1(b):
            nc.sync.dma_start(out=w1_raw[b][:], in_=w1[b * PASS : (b + 1) * PASS, :].rearrange("(p t) n -> p t n", t=PACK))

        load_w1(0)
        load_w1(1)
        nc.sync.dma_start(out=w4_codes[:], in_=w4_words.rearrange("b p c -> p b c").bitcast(I32))
        for q in range(P // QUADRANT):
            nc.sync.dma_start(
                out=w4_planes[QUADRANT * q : QUADRANT * q + 4, :, :],
                in_=w4_scales[:, 4 * q : 4 * q + 4, :].rearrange("b r c -> r b c").bitcast(I32),
            )
        with nc.allow_non_contiguous_dma(reason="one bias value for each partition and output tile"):
            nc.sync.dma_start(out=bias_t[:], in_=bias.rearrange("(c p) -> p c", p=P))

        groups = [(lo, PAIR) for lo in range(0, S2 - PAIR, PAIR)] + [(lo, USERS) for lo in (S2 - PAIR, S2 - USERS)]
        places, members = [], []
        for lo, width in groups:
            first = len(places)
            places.extend((b, at) for b in range(I_PASSES) for at in range(lo, lo + width, USERS))
            members.append(range(first, len(places)))
        group_of = {n: j for j, group in enumerate(members) for n in group}
        score_banks = list(range(7)) + [0, 1, 2, 3, 4, 0, 1, 2, 3]

        def bank(number):
            return psum.tile([P, PASS], F32, name="bank%d" % number)

        def half(name, users, at):
            return shared.tile([P, users, PACK], BF16, name=name, align_bytes=64, offset=at)

        tanh = [keep.tile([P, I_PASSES * width, PACK], F32, name="tanh%d" % lo, align_bytes=64) for lo, width in groups]
        both_0 = half("both_0", 2 * WIDE, 0)
        w1_bf = [half("w1_bf0", N, 12 * KB), half("w1_bf1", N, 8 * KB)]
        h1 = [
            both_0[:, 0:WIDE, :],
            keep.tile([P, WIDE, PACK], BF16, name="h1_1", align_bytes=64)[:],
            half("h1_2", WIDE, 12 * KB)[:],
            half("h1_3", PAIR, 8 * KB)[:],
            half("h1_4", PAIR, 0)[:],
        ]
        h2 = [both_0[:, WIDE : 2 * WIDE, :]] + [
            half("h2_%d" % j, I_PASSES * groups[j][1], at)[:] for j, at in ((1, 0), (2, 0), (3, 8 * KB), (4, 8 * KB))
        ]

        accs, quantised, w1_mx = {}, {}, {}

        def multiply(n):
            b, lo = places[n]
            acc = bank(score_banks[n])
            accs[n] = acc
            for a in range(K_PASSES):
                for t in range(PACK):
                    slots = slice(b * PASS + t * P, b * PASS + (t + 1) * P)
                    nc.tensor.matmul_mx(
                        out=acc[:, t * USERS : (t + 1) * USERS],
                        lhsT=creative_words[a][:, slots].bitcast(FP8X4),
                        lhsT_scale=planes[a][:, slots],
                        rhs=user_words[a][:, lo : lo + USERS].bitcast(FP8X4),
                        rhs_scale=planes[a][:, S + lo : S + lo + USERS],
                        start=(a == 0 and t == 0),
                        stop=(a == K_PASSES - 1 and t == PACK - 1),
                    )

        def slot(n):
            at = (n - members[group_of[n]][0]) * USERS
            return slice(at, at + USERS)

        def linear(n):
            b = places[n][0]
            nc.vector.tensor_tensor(
                h1[group_of[n]][:, slot(n), :],
                accs[n][:].rearrange("p (t n) -> p n t", t=PACK),
                ga_users[:, b, :, :],
                MULT,
            )

        def linear_scalar(n):
            b = places[n][0]
            apart = keep.tile([P, PACK, USERS], BF16, name="apart%d" % n, align_bytes=64)
            for t in range(PACK):
                nc.scalar.activation(
                    out=apart[:, t, :], in_=accs[n][:, t * USERS : (t + 1) * USERS], func=ACT.Copy, scale=ga_t[:, b, t : t + 1]
                )
            nc.scalar.copy(
                out=h1[group_of[n]][:, slot(n), :].rearrange("p (g i) t -> p g t i", i=4),
                in_=apart[:].rearrange("p t (g i) -> p g t i", i=4),
            )

        def saturate(n):
            nc.scalar.activation(
                out=tanh[group_of[n]][:, slot(n), :], in_=accs[n][:].rearrange("p (t n) -> p n t", t=PACK), func=ACT.Tanh
            )

        def weigh(engine, gains, j, lo, hi, first=0, last=I_PASSES):
            def part(tile):
                return tile.rearrange("p (b n) t -> p b n t", b=I_PASSES)[:, first:last, lo:hi, :]

            engine.tensor_tensor(
                part(h2[j]),
                part(tanh[j][:]),
                gains[:, first:last, :].unsqueeze(2).to_broadcast([P, last - first, hi - lo, PACK]),
                MULT,
            )

        def quantize(h, name, at):
            width = h.shape[1]
            if at is None:
                codes = keep.tile([P, width], U32, name="codes_" + name, align_bytes=64)
            else:
                codes = shared.tile([P, width], U32, name="codes_" + name, align_bytes=64, offset=at)
            plane = keep.tile([P, width], U8, name="plane_" + name, align_bytes=64)
            nc.vector.quantize_mx(out=codes[:].bitcast(FP8X4), scales=plane[:], in_=h.rearrange("p n t -> p (n t)"))
            return codes, plane

        def name_h(codes, plane, column, g0, j):
            for b in range(I_PASSES):
                quantised[g0 + b, j] = (codes, plane, column + b * groups[j][1])

        def quantize_h1(j, at=None):
            name_h(*quantize(h1[j], "h1_%d" % j, at), 0, 0, j)

        def quantize_h2(j):
            name_h(*quantize(h2[j], "h2_%d" % j, None), 0, I_PASSES, j)

        def quantize_h2_pass(j, b):
            width = groups[j][1]
            codes, plane = quantize(h2[j][:, b * width : (b + 1) * width, :], "h2_%d_%d" % (j, b), None)
            quantised[I_PASSES + b, j] = (codes, plane, 0)

        def round_w1(b):
            for c in range(N_TILES):
                nc.scalar.copy(
                    out=w1_bf[b][:, c * P : (c + 1) * P, :].rearrange("p (g i) t -> p g t i", i=2),
                    in_=w1_raw[b][:, :, c * P : (c + 1) * P].rearrange("p t (g i) -> p g t i", i=2),
                )

        def quantize_w1(b, at):
            w1_mx[b] = quantize(w1_bf[b][:], "w1_%d" % b, at)

        def readout(g, j, y, tiles, start, stop):
            b, width = g % I_PASSES, groups[j][1]
            codes, plane, column = quantised[g, j]
            for place, c in enumerate(tiles):
                if g < I_PASSES:
                    w = w1_mx[b][0][:, c * P : (c + 1) * P].bitcast(FP8X4)
                    w_scale = w1_mx[b][1][:, c * P : (c + 1) * P]
                else:
                    w = w4_codes[:, b, :].bitcast(U8)[:, 2 * c * P : 2 * (c + 1) * P].bitcast(FP4X4)
                    w_scale = w4_planes[:, b, :].bitcast(U8)[:, c * P : (c + 1) * P]
                nc.tensor.matmul_mx(
                    out=y[:, place * width : (place + 1) * width],
                    lhsT=w,
                    lhsT_scale=w_scale,
                    rhs=codes[:, column : column + width].bitcast(FP8X4),
                    rhs_scale=plane[:, column : column + width],
                    start=(start and c == tiles[0]),
                    stop=(stop and c == tiles[-1]),
                )

        def passes(j, outputs, order, opens, closes):
            for y, tiles in outputs:
                for g in order:
                    readout(g, j, y, tiles, opens and g == order[0], closes and g == order[-1])

        out_tiles = out.rearrange("(c p) j -> p c j", p=P)

        def store_scalar(j, y, tiles, queue):
            lo, width = groups[j]
            res = keep.tile([P, len(tiles), width], F32, name="res%d_%d" % (tiles[0], lo))
            for place, c in enumerate(tiles):
                nc.scalar.activation(
                    out=res[:, place, :],
                    in_=y[:, place * width : (place + 1) * width],
                    func=ACT.Identity,
                    bias=bias_t[:, c : c + 1],
                )
            queue.dma_start(out=out_tiles[:, tiles[0] : tiles[-1] + 1, lo : lo + width], in_=res[:])

        def store_vector(j, y, tiles):
            lo, width = groups[j]
            res = keep.tile([P, len(tiles), width], F32, name="res%d_%d" % (tiles[0], lo))
            nc.vector.tensor_tensor(
                res[:],
                y[:, 0 : len(tiles) * width].rearrange("p (c n) -> p c n", n=width),
                bias_t[:, tiles[0] : tiles[-1] + 1].unsqueeze(2).to_broadcast([P, len(tiles), width]),
                ADD,
            )
            nc.sync.dma_start(out=out_tiles[:, tiles[0] : tiles[-1] + 1, lo : lo + width], in_=res[:])

        every = list(range(N_TILES))
        low, high = every[:2], every[2:]

        def weigh_gpsimd(j, lo, hi, first=0, last=I_PASSES):
            weigh(nc.gpsimd, gb_of[j], j, lo, hi, first, last)

        def weigh_vector(j, lo, hi, first=0, last=I_PASSES):
            weigh(nc.vector, gb_psum, j, lo, hi, first, last)

        for n in range(7):
            multiply(n)
        for n in members[0]:
            saturate(n)
        for n in members[0]:
            linear(n)
        weigh_gpsimd(0, 0, USERS, 0, 1)
        weigh_gpsimd(0, USERS, PAIR, 0, 1)
        weigh_gpsimd(0, 0, GPSIMD_USERS[0], 1, 2)
        for n in (7, 8, 9, 10):
            multiply(n)
        round_w1(0)
        for n in (4, 5, 6):
            linear(n)
            saturate(n)
        weigh_vector(0, GPSIMD_USERS[0], PAIR, 1, 2)
        linear(7)
        saturate(7)
        multiply(11)
        multiply(12)
        quantize_w1(0, None)
        codes, plane = quantize(both_0[:], "first", None)
        name_h(codes, plane, 0, 0, 0)
        name_h(codes, plane, WIDE, I_PASSES, 0)
        quantize_h1(1, room(0, 1))
        first = [(bank(5), low), (bank(6), high)]
        round_w1(1)

        weigh_gpsimd(1, 0, GPSIMD_USERS[1])
        for n in members[2]:
            linear(n)
        weigh_vector(1, GPSIMD_USERS[1], PAIR)
        passes(0, first, [0], True, False)
        passes(0, first, [2, 3], False, False)
        for n in members[2]:
            saturate(n)
        quantize_w1(1, None)
        quantize_h2(1)
        quantize_h1(2, room(1, 1))
        for n in (13, 14, 15):
            multiply(n)
        second = [(bank(4), low)]
        passes(1, second, [0], True, False)
        passes(0, first, [1], False, True)
        passes(1, second, [1, 2, 3], False, True)
        second.append((bank(5), high))

        weigh_gpsimd(2, 0, GPSIMD_USERS[2])
        for y, tiles in first:
            store_scalar(0, y, tiles, nc.sync)
        for n in members[3]:
            linear(n)
            saturate(n)
        weigh_vector(2, GPSIMD_USERS[2], PAIR)
        passes(1, second[1:], [0, 1, 2, 3], True, True)
        saturate(14)
        saturate(15)
        quantize_h1(3, room(2, 0))
        quantize_h2(2)
        third = [(bank(6), low), (bank(0), high)]
        passes(2, third, [0, 1], True, False)
        fourth = [(bank(1), low)]
        passes(3, fourth, [0, 1], True, False)

        weigh_gpsimd(3, 0, GPSIMD_USERS[3])
        weigh_vector(3, GPSIMD_USERS[3], USERS)
        linear(14)
        linear_scalar(15)
        for y, tiles in second:
            store_scalar(1, y, tiles, nc.sync)
        passes(2, third, [2, 3], False, True)
        quantize_h2(3)
        quantize_h1(4, room(3, 0))
        fourth.append((bank(4), high))
        passes(3, fourth[1:], [0, 1], True, False)
        passes(3, fourth, [2, 3], False, True)
        for y, tiles in third:
            store_scalar(2, y, tiles, nc.sync)

        weigh_gpsimd(4, 0, GPSIMD_USERS[4], 1, 2)
        weigh_vector(4, 0, USERS, 0, 1)
        weigh_vector(4, GPSIMD_USERS[4], USERS, 1, 2)
        quantize_h2_pass(4, 0)
        quantize_h2_pass(4, 1)
        ends = [(bank(number), [c]) for c, number in enumerate((2, 3, 5, 6))]
        for g in range(2 * I_PASSES):
            passes(4, ends, [g], g == 0, g == 3)
        for y, tiles in fourth:
            store_scalar(3, y, tiles, nc.sync)
        store_scalar(4, ends[0][0], [0], nc.sync)
        store_vector(4, ends[1][0], [1])
        store_scalar(4, ends[2][0], [2], nc.scalar)
        store_vector(4, ends[3][0], [3])
